import numpy as np, ml_dtypes
CORES = [66,74,82,90,194,202,210,218]
N = 8
BF = ml_dtypes.bfloat16
def gentries(a):
    return np.ascontiguousarray(a.reshape(8, 16, -1).transpose(0, 2, 1)).reshape(8, -1)
def gtable(e):
    e = np.asarray(e); return np.ascontiguousarray(e.reshape(8, -1, 16).transpose(0, 2, 1)).reshape(128, -1).astype(np.int32)
F, A, GI, D, E, RO = 2048, 2048, 2, 512, 128, 3
L = GI + RO - 1
R = 16 // N
NE = [F] + [A] * GI + [D] * (RO - 1)
ST = [sum(NE[:e]) + e * E for e in range(L + 1)]
PO = [0] + [sum(NE[1:e]) for e in range(1, L + 1)]
W = ST[L] + NE[L]; M = GI * A + (RO - 1) * D
def cols(e):
    o = np.concatenate([np.arange(ST[k], ST[k] + NE[k]) for k in range(e)]); g = np.concatenate([np.arange(ST[k] + NE[k], ST[k] + NE[k] + E) for k in range(e)])
    return o, g
def parts(rng):
    h = rng.integers(0, 65536, (N, 8, 16, F)); t = rng.integers(0, 65536, (8, 16))
    s = np.zeros((N, 8, GI * A), np.int64); d = np.zeros((N, 8, M), np.int64); m = np.zeros((N, 8, L * E), np.int64)
    for e in range(1, L + 1):
        o, g = cols(e); p, n = PO[e], NE[e]
        if e <= GI: s[:, :, p:p + n] = rng.choice(o, (N, 8, n))
        d[:, :, p:p + n] = np.where(rng.random((N, 8, n)) < 0.25, rng.choice(g, (N, 8, n)), rng.choice(o, (N, 8, n)))
    for e in range(L): m[:, :, e * E:(e + 1) * E] = rng.integers(0, NE[e], (N, 8, E))
    return h, t, s, d, m
def pack(h, t, s, d, m):
    return {"trait": np.ascontiguousarray(h.reshape(N, 128, F)).astype(np.int32), "aim0": np.tile(t.reshape(1, 128, 1), (N, 1, 1)).astype(np.int32),
            "sire": np.stack([gtable(a) for a in s]), "dam": np.stack([gtable(a) for a in d]), "mg": np.stack([gtable(a) for a in m])}
def setup_inputs(rng):
    return pack(*parts(rng))
def plant(rng, h, t, s, d, m, g, j, up):
    t[g] = rng.integers(0, 1000, 16); low = rng.integers(1000, 5000, 14)
    for q in range(N):
        c = 1 + rng.permutation(F - 1); x, y, z, a0, a1, b = [int(v) for v in c[:6]]; rest = c[6:]
        w = rng.integers(20000, 55000, (16, F)); w[0] = rng.integers(60000, 65536, F); w[1] = rng.integers(2000, 40000, F)
        w[:2, [x, y, z, b]] = rng.integers(2000, 40000, (2, 4)); w[1, b] = rng.integers(60000, 65536); w[0, x] = 1000; w[1, y] = 1000
        w[2:, y] = rng.integers(1000, 5000, 14) + 5000 * (q % 2); w[2:, x] = w[2:, y] + 40000; w[2:, z] = rng.integers(60000, 65536, 14)
        w[2:, a0] = low; w[2:, a1] = low + up; w[2:, b] = low + 40000; h[q, g] = w
        col = a1
        for e in range(1, GI):
            k = int(rng.integers(0, A)); s[q, g, PO[e] + k] = a0; d[q, g, PO[e] + k] = col; col = ST[e] + k
        o = rng.choice(rest, A); k = rng.permutation(A)[:4]; o[k[:3]] = (x, y, z); p = PO[GI]
        s[q, g, p:p + A] = o; d[q, g, p:p + A] = o; s[q, g, p + k[3]] = a0; d[q, g, p + k[3]] = col
        v = rng.choice(rest, D); v[int(rng.integers(1, D - 1))] = ST[GI] + k[3]; v[j] = b
        d[q, g, PO[GI + 1]:PO[GI + 1] + D] = v; m[q, g, (GI + 1) * E] = j
def setup_inputs_ends(rng):
    h, t, s, d, m = parts(rng); t = rng.choice(np.array([0, 1, 32767, 65534, 65535]), (8, 16))
    for e in range(1, L + 1):
        o, g = cols(e); p, n = PO[e], NE[e]
        if e <= GI: s[:, 4:, p:p + n] = rng.choice(np.array([0, F - 1, o[-1]]), (N, 4, n))
        d[:, 4:, p:p + n] = rng.choice(np.array([0, F - 1, F, F + E - 1, o[-1], g[-1]]), (N, 4, n))
    for e in range(L): m[:, 4:, e * E:(e + 1) * E] = rng.choice(np.array([0, NE[e] - 1]), (N, 4, E))
    h[:, :4, :, 7] = t[:4]; h[:, :4, :, 9] = np.where(t[:4] < 32768, 65535, 0); a, z = (GI - 1) * A, GI * A - 1
    for g in range(4):
        x, y = (7, 9) if g < 2 else (9, 7)
        s[:, g, z] = x; d[:, g, z] = x; s[:, g, a] = y; d[:, g, a] = y
    plant(rng, h, t, s, d, m, 6, D - 1, 1); plant(rng, h, t, s, d, m, 7, 0, 0)
    return pack(h, t, s, d, m)
def setup_inputs_ghosts(rng):
    h, t, s, d, m = parts(rng)
    for e in range(1, L + 1):
        o, g = cols(e); p, n = PO[e], NE[e]
        d[:, 0::2, p:p + n] = rng.choice(g, (N, 4, n)); d[:, 1, p:p + n] = rng.choice(o, (N, n))
        d[:, 6, p:p + n] = rng.integers(ST[e] - E, ST[e], (N, n))
        if e > GI: d[:, 3, p:p + n] = rng.integers(ST[e - 1], ST[e - 1] + NE[e - 1], (N, n))
    d[:, 3, :GI * A] = s[:, 3]
    for e in range(L):
        m[:, 5, e * E:(e + 1) * E] = rng.integers(0, NE[e], (N, 1)); m[:, 7, e * E:(e + 1) * E] = NE[e] - 1
    return pack(h, t, s, d, m)
def setup_inputs_lines(rng):
    h, t, s, d, m = parts(rng); t[5] = rng.integers(0, 65536)
    for e in range(1, L + 1):
        p, n = PO[e], NE[e]; lo, hi = ST[e - 1], ST[e - 1] + NE[e - 1]
        if e <= GI:
            s[:, 0:2, p:p + n] = rng.integers(lo, hi, (N, 2, n)); s[:, 2:4, p:p + n] = rng.integers(0, F, (N, 2, n))
            s[:, 4, p:p + n] = np.where(rng.random((N, n)) < 0.9, rng.integers(lo, hi, (N, 1)), rng.integers(lo, hi, (N, n)))
            d[:, 7, p:p + n] = rng.integers(1, ST[e], (N, 1))
        d[:, 0::4, p:p + n] = rng.integers(lo, hi, (N, 2, n)); d[:, 1::4, p:p + n] = rng.integers(0, F, (N, 2, n))
        for g, k in ((2, 1), (3, 2), (6, 3)):
            y = min(k, e - 1); d[:, g, p:p + n] = rng.integers(ST[y], ST[y] + NE[y], (N, n))
    return pack(h, t, s, d, m)
def setup_inputs_spread(rng):
    h, t, s, d, m = parts(rng)
    h = np.minimum((np.exp2(17 * rng.random((N, 8, 1, F))) * rng.random((N, 8, 16, F))).astype(np.int64), 65535)
    t = np.minimum(np.exp2(16 * rng.random((8, 16))).astype(np.int64), 65535)
    for e in range(1, L + 1):
        o, g = cols(e); p, n = PO[e], NE[e]; o = rng.permutation(o); g = rng.permutation(g)
        if e <= GI: s[:, :, p:p + n] = o[(len(o) * rng.random((N, 8, n)) ** 4).astype(np.int64)]
        d[:, :, p:p + n] = np.where(rng.random((N, 8, n)) < 0.5, g[(len(g) * rng.random((N, 8, n)) ** 3).astype(np.int64)], o[(len(o) * rng.random((N, 8, n)) ** 3).astype(np.int64)])
    for e in range(L): m[:, :, e * E:(e + 1) * E] = (NE[e] * rng.random((N, 8, E)) ** 3).astype(np.int64)
    return pack(h, t, s, d, m)
def setup_inputs_ties(rng):
    h, t, s, d, m = parts(rng)
    h[:, 0] = 5; t[0] = rng.choice(np.array([3, 4, 1000, 60000]), 16)
    t[0, 14] = 5; h[:, 0, 14, 0] = 60000; t[0, 15] = 0; h[:, 0, 15] = 65535
    s[:, 0] = np.where(s[:, 0] == 0, 1, s[:, 0]); d[:, 0] = np.where(d[:, 0] == 0, 1, d[:, 0]); m[:, 0, :E] = np.where(m[:, 0, :E] == 0, 1, m[:, 0, :E])
    h[:, 1:3] = rng.choice(np.array([0, 1, 32768, 65535]), (N, 2, 16, F)); t[1:3] = rng.choice(np.array([0, 1, 32768, 65535]), (2, 16))
    h[:, 3:5, 8:] = h[:, 3:5, :8]; t[3:5, 8:] = t[3:5, :8]
    h[:, 5] = 65535 * rng.integers(0, 2, (N, 16, F)); t[5] = 65535 * rng.integers(0, 2, 16)
    h[:, 6] = h[:, 6][:, :, np.arange(F) % 16]
    t[7] = 32768; h[:, 7] = 32768 + 20000 * (2 * rng.integers(0, 2, (N, 16, F)) - 1)
    return pack(h, t, s, d, m)
def check_inputs(d):
    bad = []
    for k in ("trait", "aim0"):
        if np.min(d[k]) < 0 or np.max(d[k]) > 65535: bad.append("range of " + k)
    if np.any(d["aim0"] != d["aim0"][:1]): bad.append("aim0 alike on all ranks")
    s = np.stack([gentries(a) for a in d["sire"]]); w = np.stack([gentries(a) for a in d["dam"]]); m = np.stack([gentries(a) for a in d["mg"]])
    for e in range(1, GI + 1):
        if not np.all(np.isin(s[:, :, PO[e]:PO[e] + NE[e]], cols(e)[0])): bad.append("sires of generation " + str(e))
    for e in range(1, L + 1):
        x = w[:, :, PO[e]:PO[e] + NE[e]]
        if np.min(x) < 0 or np.max(x) >= ST[e]: bad.append("dams of generation " + str(e))
    for e in range(L):
        x = m[:, :, e * E:(e + 1) * E]
        if np.min(x) < 0 or np.max(x) >= NE[e]: bad.append("emigrants of generation " + str(e))
    return bad
def pick(w, ix):
    return np.take_along_axis(w, ix[:, :, None, :], 3)
def reference(trait, aim0, sire, dam, mg):
    h = trait.astype(np.int64).reshape(N, 8, 16, F); t = aim0.astype(np.int64).reshape(N, 8, 16, 1)
    sl = np.zeros((N, 8, M), np.int64); sl[:, :, :GI * A] = np.stack([gentries(a) for a in sire])
    dl = np.stack([gentries(a) for a in dam]).astype(np.int64); ml = np.stack([gentries(a) for a in mg]).astype(np.int64)
    top = np.zeros((N, 8, W), np.int64); top[:, :, :F] = np.arange(F)
    for e in range(1, GI + 1): top[:, :, ST[e]:ST[e] + NE[e]] = np.take_along_axis(top, sl[:, :, PO[e]:PO[e] + NE[e]], 2)
    f = np.zeros((N, 8, 16, W)); aims = []
    for rnd in range(1, RO + 1):
        new = GI + rnd - 1
        for e in range(new + 1):
            a, n, p = ST[e], NE[e], PO[e]
            if e == 0: f[:, :, :, :F] = 65535 - np.abs(h - t)
            else: f[:, :, :, a:a + n] = (pick(f, sl[:, :, p:p + n]) + pick(f, dl[:, :, p:p + n])) * 0.5
            if e < L: f[:, :, :, a + n:a + n + E] = np.roll(pick(f[:, :, :, a:a + n], ml[:, :, e * E:(e + 1) * E]), 1, axis=0)
        if rnd == RO: break
        a, n = ST[new], NE[new]; x = f[:, :, :, a:a + n]
        best = a + np.argmax(x, axis=3); least = a + np.argmin(x, axis=3)
        b, p = ST[new + 1], PO[new + 1]
        row = np.argmin(pick(f, dl[:, :, p:p + D]), axis=2)
        sl[:, :, p:p + D] = np.take_along_axis(best, row, 2)
        old = np.take_along_axis(h, np.take_along_axis(top, least, 2)[:, :, :, None], 3)[:, :, :, 0]
        top[:, :, b:b + D] = np.take_along_axis(top, sl[:, :, p:p + D], 2)
        t1 = np.stack([old[m // R, :, m] for m in range(16)], axis=1)
        t = np.tile(t1.reshape(1, 8, 16, 1), (N, 1, 1, 1)); aims.append(t.reshape(N, 128))
    made = np.concatenate([f[:, :, :, ST[e]:ST[e] + NE[e]] for e in range(GI + 1, L + 1)], axis=3)
    return {"yf": made.reshape(N, 128, (RO - 1) * D).astype(np.float32), "ys": np.stack([gtable(a) for a in sl[:, :, GI * A:]]).astype(np.float32), "yt": np.stack(aims, axis=2).astype(np.float32)}

@@ -1,0 +1,719 @@
+import numpy as np
+from concourse.bass import DstId, RemoteDMATransfer
+from concourse.mybir import AluOpType, AxisListType, ActivationFunctionType
+
+F32, BF, I32, U16 = "float32", "bfloat16", "int32", "uint16"
+NC = 140
+FWW = 16 * NC + 64
+BIG = 2 ** 24 - 1
+C16 = 1.5 * 2 ** 27
+C32 = 1.5 * 2 ** 28
+KI = -(16 * NC - 1) / 16.0
+KC = 7.5 * NC - 268.0
+
+ULAY = [("p1", 256), ("p2", 268), ("mg", 32), ("l1", 72), ("g2", 16), ("x", 128), ("i4", 32), ("m3", 40), ("m4", 32),
+        ("mG", 8), ("ca", 8), ("cc", 8), ("lf", 2), ("bl", 2), ("j2", 2), ("b2", 2)]
+UOFF = {}
+_o = 0
+for _n, _w in ULAY:
+    UOFF[_n] = (_o, _o + _w)
+    _o += _w
+UW = _o
+
+
+def _sb(n, d=F32):
+    return ("sbuf", [128, n], d)
+
+
+SCRATCH = {
+    "tri": _sb(2048, I32), "t0i": _sb(4, I32), "tt": _sb(2 * NC, I32), "t1": _sb(256, I32), "xi": _sb(64, I32),
+    "mgi": _sb(32, I32), "u": _sb(UW, U16), "hi": _sb(2 * NC, BF), "lo": _sb(2 * NC, BF), "fw": _sb(FWW, BF),
+    "wa": _sb(4608), "wb": _sb(4608), "w2": _sb(4352), "sb": _sb(2048), "gg": _sb(2048), "k1": _sb(2048), "k2": _sb(2048),
+    "k3": _sb(512), "k4": _sb(512), "res": _sb(1536, BF), "la": _sb(2048), "lc": _sb(2048), "lg": _sb(512),
+    "pb": _sb(72), "bl": _sb(72), "e0": _sb(128), "e1": _sb(256), "e2": _sb(512), "e3": _sb(512), "xa": _sb(640),
+    "xb": _sb(512), "xt": _sb(640), "xs": _sb(640), "wd2": _sb(1152), "wd3": _sb(1152), "d32": _sb(512), "d33": _sb(512),
+    "tg2": _sb(640), "tg3": _sb(640), "tb": _sb(512), "yfl": _sb(1024), "yfs": _sb(1024), "yss": _sb(64), "yts": _sb(2),
+    "f4t": _sb(512), "an1": _sb(12), "an2": _sb(12), "ci": _sb(256, I32), "cf": _sb(4096), "cb": _sb(2048, BF),
+    "pp": _sb(640, BF), "pn": _sb(512, BF),
+}
+for _n in ("ea", "eb", "ec", "pc", "pd", "pk", "pm", "py"):
+    SCRATCH[_n] = ("psum", [128, 512], F32)
+NDMA = 24
+SEMAPHORES = (["cV", "cS", "cP", "cG", "sent", "s0", "r0", "r1", "r2", "r3", "rb", "ra1", "ra2"]
+              + ["dm%d" % i for i in range(NDMA)])
+
+A = AluOpType
+ACT = ActivationFunctionType
+CY = 0.00104
+P = {"fix": 0.03, "sync": 0.12, "pe": 0.0008, "dma": 2.0, "hop": 3.0, "hopa": 5.0, "giss": 0.3, "first": 1.0, "look": 0.05,
+     "fv": 1600, "iters": 3000, "seed": 1, "wv": 0.2, "T": 0.5}
+PLAN = {}
+
+
+def build(T, topo, core, rank):
+    N = len(T.cores)
+    nodes = []
+    acc = {}
+    alloc = {"ci": 0, "cf": 0, "cb": 0, "dma": 0, "bank": 0, "rem": 0}
+
+    def ap(name, lo, hi, step=1, p=None):
+        t = T[name]
+        if p is None:
+            x = t[:, lo:hi] if step == 1 else t[:, lo:hi:step]
+        else:
+            x = t[p::16, lo:hi]
+        return {"ap": x, "r": [(name, lo, hi)], "n": len(range(lo, hi, step)), "dt": SCRATCH[name][2],
+                "ps": SCRATCH[name][0] == "psum", "ind": False}
+
+    def sub(a, lo, hi, step=1):
+        name, b, _e = a["r"][0]
+        return ap(name, b + lo, b + hi, step)
+
+    def new(name, n):
+        o = alloc[name]
+        alloc[name] = o + (n + 15) // 16 * 16
+        assert alloc[name] <= SCRATCH[name][1][1], name
+        return ap(name, o, o + n)
+
+    def ul(name, lo=0, hi=None):
+        b, e = UOFF[name]
+        return ap("u", b + lo, e if hi is None else b + hi)
+
+    def ind(win, off):
+        return {"ap": win["ap"].indirect(off["ap"]), "r": win["r"] + off["r"], "n": 16 * off["n"], "dt": win["dt"],
+                "ps": False, "ind": True}
+
+    def node(eng, fn, reads, writes, dur, lat=0.0, kind="c", sem=None, val=0, deps=()):
+        k = len(nodes)
+        d = {}
+        for x in deps:
+            d[x] = "raw"
+        rr = []
+        ww = []
+        for a in reads:
+            for (nm, lo, hi) in a["r"]:
+                if SCRATCH[nm][0] == "psum":
+                    ww.append((nm, 0, 512, True))
+                else:
+                    rr.append((nm, lo, hi))
+        for a in writes:
+            nm, lo, hi = a["r"][0]
+            if SCRATCH[nm][0] == "psum":
+                ww.append((nm, 0, 512, False))
+            else:
+                ww.append((nm, lo, hi, False))
+        for (nm, lo, hi) in rr:
+            for (j, l2, h2, w) in acc.get(nm, []):
+                if w and l2 < hi and lo < h2:
+                    d[j] = "raw"
+        for (nm, lo, hi, rd) in ww:
+            for (j, l2, h2, w) in acc.get(nm, []):
+                if l2 < hi and lo < h2 and j != k:
+                    if kind == "fw" and nodes[j]["kind"] == "fw":
+                        continue
+                    if rd and nodes[j]["eng"] != eng:
+                        d[j] = "raw"
+                    elif j not in d:
+                        d[j] = "ord" if (rd and eng != "VS") else "war"
+        for (nm, lo, hi) in rr:
+            acc.setdefault(nm, []).append((k, lo, hi, False))
+        for (nm, lo, hi, rd) in ww:
+            if kind != "fw" and not rd:
+                acc[nm] = [e for e in acc.get(nm, []) if not (lo <= e[1] and e[2] <= hi and e[0] != k)]
+            acc.setdefault(nm, []).append((k, lo, hi, True))
+        nodes.append({"eng": eng, "fn": fn, "deps": d, "dur": dur, "lat": lat, "kind": kind, "sem": sem, "val": val})
+        return k
+
+    def cost(n, c):
+        return P["fix"] + max(64, n * c) * CY
+
+    def cc(*xs):
+        if any(x["ind"] for x in xs):
+            return 1.56
+        return 0.5 if all(x["dt"] in (BF, U16) for x in xs) else 1.0
+
+    def isap(x):
+        return isinstance(x, dict)
+
+    def val(x):
+        return x["ap"] if isap(x) else x
+
+    def cp(out, in_, eng="V"):
+        def fn(g, e):
+            if e == "V":
+                return g.vector.tensor_copy(out["ap"], in_["ap"])
+            return g.scalar.activation(out["ap"], in_["ap"], ACT.Copy)
+        return node(eng, fn, [in_], [out], cost(out["n"], cc(out, in_) if (eng == "V" or in_["ind"]) else 1.0))
+
+    def aff(out, in_, scale, bias, eng="VS"):
+        def fn(g, e):
+            if e == "V":
+                return g.vector.tensor_scalar(out["ap"], in_["ap"], scale, bias, A.mult, A.add)
+            return g.scalar.activation(out["ap"], in_["ap"], ACT.Identity, bias=bias, scale=scale)
+        return node(eng, fn, [in_], [out], cost(out["n"], 1.56 if in_["ind"] else 1.0))
+
+    def ts(out, in0, s1, op0, s2=None, op1=None):
+        def fn(g, e):
+            if op1 is None:
+                return g.vector.tensor_scalar(out["ap"], in0["ap"], val(s1), None, op0)
+            return g.vector.tensor_scalar(out["ap"], in0["ap"], val(s1), val(s2), op0, op1)
+        return node("V", fn, [in0] + [x for x in (s1, s2) if isap(x)], [out], cost(out["n"], cc(out, in0)))
+
+    def tt(out, in0, in1, op):
+        c = 1.56 if in0["ind"] else (1.0 if (in0["ps"] or in1["ps"]) else 2.0)
+        return node("V", lambda g, e: g.vector.tensor_tensor(out["ap"], in0["ap"], in1["ap"], op), [in0, in1], [out],
+                    cost(out["n"], c))
+
+    def red(out, in_, op, neg=False):
+        return node("V", lambda g, e: g.vector.tensor_reduce(out["ap"], in_["ap"], AxisListType.X, op, negate=neg),
+                    [in_], [out], cost(in_["n"], 1.0))
+
+    def scan(out, d0, d1, op1, init=0.0):
+        return node("V", lambda g, e: g.vector.tensor_tensor_scan(out["ap"], d0["ap"], d1["ap"], init, A.add, op1),
+                    [d0, d1], [out], cost(out["n"], 1.0))
+
+    def mset(out, v):
+        return node("V", lambda g, e: g.vector.memset(out["ap"], v), [], [out], cost(out["n"], cc(out)))
+
+    def act(out, in_, func, bias, scale):
+        return node("S", lambda g, e: g.scalar.activation(out["ap"], in_["ap"], func, bias=val(bias), scale=scale),
+                    [in_] + ([bias] if isap(bias) else []), [out], cost(out["n"], 1.56 if in_["ind"] else 1.0))
+
+    def mms(out, pairs):
+        def fn(g, e):
+            r = None
+            for i, (l, x) in enumerate(pairs):
+                r = g.tensor.matmul(out["ap"], l["ap"], x["ap"], i == 0, i == len(pairs) - 1)
+            return r
+        rd = []
+        w = 0
+        for l, x in pairs:
+            rd += [l, x]
+            w += 4 if l["dt"] == F32 else 1
+        return node("P", fn, rd, [out], 0.05 + w * max(64, out["n"]) * P["pe"])
+
+    def iota(out, pat, base, cm):
+        def fn(g, e):
+            if out["dt"] == I32:
+                return g.iota(out["ap"], pat, base, cm)
+            return g.iota(out["ap"], pat, base, cm, allow_small_or_imprecise_dtypes=True)
+        return node("G", fn, [], [out], 0.13 + 2 * out["n"] * CY)
+
+    def keep(out, in_, pat, op, base, cm):
+        return node("G", lambda g, e: g.affine_select(out["ap"], in_["ap"], pat, op, 0.0, base, cm), [in_], [out],
+                    0.17 + 2 * out["n"] * CY)
+
+    def dma(q, out, in_, reads, writes, extra=0.0, kind="d", deps=()):
+        s = "dm%d" % alloc["dma"]
+        alloc["dma"] += 1
+
+        def fn(g, e):
+            qq = g.sync if q == "Y" else g.scalar
+            return qq.dma_start(out, in_)
+        return node(q, fn, reads, writes, 0.06, P["dma"] + extra, kind, s, 16, deps)
+
+    nxt = T.cores[(rank + 1) % N]
+
+    def issue():
+        alloc["rem"] += 1
+        return P["giss"] + (P["first"] if alloc["rem"] == 1 else 0.0)
+
+    def ring(parts, sem, ls="sent"):
+        en = topo.engines(core, nxt)
+        w = len(en) // len(parts)
+        rid, pid = topo.addr(nxt, core)
+
+        def fn(g, e):
+            return g.remote_dma_fused(
+                [RemoteDMATransfer(dst_ids=[DstId(rid=rid, pnc=pid)] * (len(b) - 1),
+                                   dma_engine_mask=sum(1 << x for x in en[i * w:i * w + w]), remote_sem=T.sem[sem],
+                                   srcs=[b[0]["ap"]], dsts=[x["ap"] for x in b[1:]]) for i, b in enumerate(parts)],
+                local_sem=T.sem[ls])
+        k = node("G", fn, [b[0] for b in parts], [], issue(), 1.0 if ls != "sent" else 0.0, "s", ls, len(en))
+        prv = T.cores[(rank - 1) % N]
+        node("X", None, [], [x for b in parts for x in b[1:]], 0.0,
+             P["hop"] - nodes[k]["lat"] + sum(x["n"] for b in parts for x in b[1:]) * 0.002, "x", sem,
+             len(topo.engines(prv, core)) * (len(parts[0]) - 1), [k])
+        return k
+
+    def common(src):
+        m = -1
+        for c in T.cores:
+            if c != src:
+                m &= topo.mask(src, c)
+        return m
+
+    def spread(land, sem):
+        m = common(core)
+        ids, dsts = [], []
+        for c in range(1, N):
+            d = T.cores[(rank - c) % N]
+            rid, pid = topo.addr(d, core)
+            ids.append(DstId(rid=rid, pnc=pid))
+            dsts.append(T[land][:, 3 + c:4 + c])
+        src = ap(land, 3, 4)
+
+        def fn(g, e):
+            tr = RemoteDMATransfer(dst_ids=ids, dma_engine_mask=m, remote_sem=T.sem[sem], srcs=[src["ap"]], dsts=dsts)
+            return g.remote_dma_fused([tr], local_sem=T.sem["sent"])
+        k = node("G", fn, [src], [], issue(), 0.0, "s", "sent", bin(m).count("1"))
+        tot = sum(bin(common(c)).count("1") for c in T.cores if c != core)
+        return node("X", None, [], [ap(land, 4, 11)], 0.0, P["hopa"], "x", sem, tot, [k])
+
+    for (dst, src) in ((ap("mgi", 0, 32), T.mg[:]), (ap("t1", 0, 128), T.sire[:, 0:128]), (ap("t1", 128, 256), T.dam[:, 0:128]),
+                       (ap("t0i", 0, 1), T.aim0[:]), (ap("tt", 4, 132), T.sire[:, 128:256]),
+                       (ap("tt", NC + 4, NC + 132), T.dam[:, 128:256]), (ap("xi", 0, 64), T.dam[:, 256:320])):
+        dma("Y", dst["ap"], src, [], [dst])
+    for c in range(4):
+        dst = ap("tri", 512 * c, 512 * c + 512)
+        dma("S", dst["ap"], T.trait[:, 512 * c:512 * c + 512], [], [dst], 0.7 * (c + 1))
+
+    fv = P["fv"]
+    mset(ap("fw", 0, fv), 0.0)
+    iota(ap("fw", fv, FWW), [[0, FWW - fv]], 0, 0)
+    pi_ = new("ci", 1)
+    iota(pi_, [[0, 1]], 0, 1)
+    gi = new("ci", 1)
+    ts(gi, pi_, 112, A.bitwise_and)
+    g16 = new("cf", 1)
+    cp(g16, gi)
+    for base, c0 in ((0, 4352), (NC, 4480)):
+        iota(ap("tt", base, base + 4), [[0, 4]], 4352, 0)
+        iota(ap("tt", base + 132, base + 140), [[16, 8]], c0, 1)
+        ts(ap("tt", base + 132, base + 140), ap("tt", base + 132, base + 140), g16, A.subtract)
+    k0 = new("cf", 32)
+    iota(k0, [[16, 32]], 6016, 1)
+    oneb, onef = new("cb", 160), new("cf", 144)
+    iota(oneb, [[0, 160]], 1, 0)
+    iota(onef, [[0, 144]], 1, 0)
+    bs, bd, b0 = new("cb", 144), new("cb", 144), new("cf", 144)
+    band = [[-16, 9], [200, 16]]
+    for b_, c0 in ((bs, 0), (bd, 2)):
+        keep(b_, sub(oneb, 0, 144), band, A.is_ge, -3000 - c0, 1)
+        keep(b_, b_, [[16, 9], [0, 16]], A.is_ge, 1 + c0, -1)
+    R = 16 // N
+    free_row = (R * (rank + 1)) % 16
+    keep(b0, onef, band, A.is_equal, -3000 - free_row, 1)
+    nid = new("cf", 128)
+    iota(nid, [[0, 128]], -1, 0)
+    keep(nid, nid, [[-1, 128]], A.is_equal, 0, 1)
+    bm, bmb = new("cf", 128), new("cb", 128)
+    for b_, one in ((bmb, oneb), (bm, onef)):
+        keep(b_, sub(one, 0, 128), [[-16, 8], [0, 16]], A.is_ge, 0, 1)
+        keep(b_, b_, [[16, 8], [0, 16]], A.is_ge, 15, -1)
+    keep(bm, bm, [[0, 8], [1, 16]], A.is_equal, -free_row, 0)
+    ib = [new("cb", 160), new("cb", 160)]
+    for h in range(2):
+        keep(ib[h], oneb, [[32, 5], [1016, 2], [1, 16]], A.is_equal, -16 - 1000 * (1 - h), -1)
+    for nm, n, sg in (("pp", 640, 1), ("pn", 512, -1)):
+        for o in range(0, n, 320):
+            iota(ap(nm, o, min(n, o + 320)), [[0, min(n, o + 320) - o]], sg, 0)
+        iota(ap(nm, 0, n, 16), [[0, n // 16]], -sg * BIG, 0)
+    age = {True: new("cf", 128), False: new("cf", 128)}
+    iota(age[True], [[0, 128]], 16, 0)
+    iota(age[False], [[0, 128]], -16, 0)
+    ey = new("ci", 32)
+    iota(ey, [[1, 32]], 128, -1)
+    ey2 = new("ci", 32)
+    ts(ey2, ey, 15, A.bitwise_and)
+    eye2 = new("cf", 32)
+    ts(eye2, ey2, 0.5, A.is_lt)
+    eye = sub(eye2, 0, 16)
+    selb = new("cb", 2)
+    tt(selb, sub(eye2, 0, 4, 2), sub(eye2, 1, 4, 2), A.add)
+    own = [new("cf", 8), new("cf", 8)]
+    tt(own[1], sub(eye2, R * rank, R * rank + 16, 2), sub(eye2, R * rank + 1, R * rank + 16, 2), A.add)
+    aff(own[0], own[1], 32.0, 0.0)
+    kt = new("cf", 8)
+    mset(kt, KI)
+
+    cp(ul("mg"), ap("mgi", 0, 32))
+    cp(ul("p1"), ap("t1", 0, 256))
+    cp(ul("p2"), ap("tt", 4, NC + 132))
+    mg0, mg1, mg3 = ul("mg", 0, 8), ul("mg", 8, 16), ul("mg", 24, 32)
+    b1, b1d = new("cf", 1), new("cf", 1)
+    ts(b1, ap("t0i", 0, 1), -32.0, A.mult)
+    aff(b1d, b1, 2.0, 0.0)
+    for h in range(2):
+        a_, b_ = h * NC, (h + 1) * NC
+        cp(ap("hi", a_, b_), ap("tt", a_, b_))
+        tt(ap("lo", a_, b_), ap("tt", a_, b_), ap("hi", a_, b_), A.subtract)
+        for j, nm in enumerate(("hi", "lo")):
+            dst = ap("fw", 0, 16 * NC, p=2 * h + j)
+            dma("Y", dst["ap"], T[nm][:, a_:b_], [ap(nm, a_, b_)], [dst], 0.3, "fw")
+    fw = ap("fw", 0, FWW)
+
+    def place(ym, u):
+        n = ym["n"]
+        fl, t2 = new("cf", n), new("cf", n)
+        ts(fl, ym, C16, A.add, C16, A.subtract)
+        aff(t2, ym, float(NC), KC)
+        aff(fl, fl, KI, 0.0)
+        tt(t2, t2, fl, A.add)
+        cp(u, t2)
+
+    def parents(us, ro, bank_, rs):
+        c = 0
+        for u in us:
+            cp(ap("res", ro + 16 * c, ro + 16 * (c + u["n"])), ind(fw, u), "VS")
+            c += u["n"]
+        for ch, b_ in enumerate((bs, bd)):
+            mms(ap(bank_, ch * c, ch * c + c),
+                [(sub(b_, 15 - m, 143 - m), ap("res", ro + m, ro + 16 * c, 16)) for m in range(16)]
+                + ([(nid, rs)] if rs is not None else []))
+
+    def bank():
+        alloc["bank"] += 1
+        return ("ea", "eb", "ec")[alloc["bank"] % 3]
+
+    ym = new("cf", 72)
+    ts(sub(ym, 0, 8), ap("mgi", 16, 24), 4352.0 - 7.5, A.add)
+    ts(sub(ym, 8, 72), ap("xi", 0, 64), 4351.0, A.max, -7.5, A.add)
+    r1 = new("cf", 64)
+    ts(r1, ap("xi", 0, 64), -1.0, A.mult, 4352.0, A.add)
+    act(r1, r1, ACT.Relu, 0.0, 1.0)
+    place(ym, ul("l1"))
+    parents([ul("l1", 0, 8)], 0, "pd", None)
+    cp(ul("g2"), ap("pd", 0, 16))
+
+    cp(ap("e0", 0, 128), ind(ap("tri", 0, 2048), mg0))
+    k0_ = ring([(ap("e0", 0, 128), ap("wa", 2048, 2176), ap("wb", 2048, 2176))], "r0", "s0")
+    for c in range(4):
+        a_, b_ = 512 * c, 512 * c + 512
+        cp(ap("wa", a_, b_), ap("tri", a_, b_))
+    for c in range(4):
+        a_, b_ = 2176 + 512 * c, 2176 + 512 * c + 512
+        cp(ap("wa", a_, b_), ind(ap("wa", 0, 2048), ul("p1", 32 * c, 32 * c + 32)), "VS")
+        cp(ap("wb", a_, b_), ind(ap("wa", 0, 2176), ul("p1", 128 + 32 * c, 160 + 32 * c)), "VS")
+    cp(ap("e1", 0, 128), ind(ap("wa", 2176, 4224), mg1), "VS")
+    cp(ap("e1", 128, 256), ind(ap("wb", 2176, 4224), mg1), "VS")
+    ring([(ap("e1", 0, 128), ap("wa", 4224, 4352)), (ap("e1", 128, 256), ap("wb", 4224, 4352))], "r1")
+    dma("Y", T.wb[:, 0:2048], T.wa[:, 0:2048], [ap("wa", 0, 2048)], [ap("wb", 0, 2048)], 3.0, "d", [k0_])
+    for a_, b_ in ((0, 512), (512, 1024), (1024, 1536), (1536, 2048), (2048, 2176)):
+        act(ap("w2", a_, b_), ap("wa", a_, b_), ACT.Abs, b1d, 64.0)
+        bk = ap(bank(), 0, b_ - a_)
+        o_ = ap("w2", 2176 + a_, 2176 + b_)
+        act(o_, ap("wa", 2176 + a_, 2176 + b_), ACT.Abs, b1, 32.0)
+        act(bk, ap("wb", 2176 + a_, 2176 + b_), ACT.Abs, b1, 32.0)
+        tt(o_, o_, bk, A.add)
+    cp(ap("e2", 0, 256), ind(ap("wa", 0, 4352), ul("g2")), "VS")
+    cp(ap("e2", 256, 512), ind(ap("wb", 0, 4352), ul("g2")), "VS")
+    ring([(ap("e2", 0, 256), ap("wa", 4352, 4608)), (ap("e2", 256, 512), ap("wb", 4352, 4608))], "r2")
+    for c in range(4):
+        a_, b_ = 512 * c, 512 * c + 512
+        e_ = 32 * c
+        cp(ap("sb", a_, b_), ind(ap("w2", 0, 4224), ul("p2", e_, e_ + 32)), "VS")
+        tt(ap("gg", a_, b_), ind(ap("w2", 0, 4352), ul("p2", NC + e_, NC + e_ + 32)), ap("sb", a_, b_), A.add)
+        scan(ap("k1", a_, b_), ap("pp", 0, 512), ap("gg", a_, b_), A.max)
+        scan(ap("k2", a_, b_), ap("pn", 0, 512), ap("gg", a_, b_), A.min)
+
+    def where(out, kb, n, big, base):
+        k = ap(kb, 15, n, 16)
+        ns = n // 16
+        sg = 1.0 if big else -1.0
+        op = A.max if big else A.min
+        m_, th = new("cf", 1), new("cf", 1)
+        kp, z = new("cf", ns), new("cf", ns)
+        red(m_, k, op)
+        aff(kp, k, 1.0, 15.0 * sg)
+        low = 0.0
+        if big and n == 512:
+            low = 1024.0
+            kq = new("cf", ns)
+            aff(kq, k, 1.0, -low)
+            k = kq
+        ts(kp, kp, m_, A.is_lt if big else A.is_gt, -8192.0 * sg, A.mult)
+        ts(th, m_, C32, A.add, C32, A.subtract)
+        tt(kp, kp, k, A.add)
+        scan(z, sub(age[big], 0, ns), kp, op, -1e9 * sg)
+        if big:
+            ts(out, th, sub(z, ns - 1, ns), A.subtract, 15.0 + 16.0 * (ns - 1) - low + base, A.add)
+        else:
+            ts(out, sub(z, ns - 1, ns), th, A.subtract, 15.0 + 16.0 * (ns - 1) + base, A.add)
+
+    def step(jm, u, w):
+        fl, c2 = new("cf", 1), new("cf", 1)
+        ts(fl, jm, C16, A.add, C16, A.subtract)
+        aff(c2, jm, float(NC), KC)
+        ts(u, kt, fl, A.mult, c2, A.add)
+        st = new("cb", 128)
+        tt(st, ind(fw, u), bmb, A.mult)
+        mms(ap("pk", 0, w), [(st, sub(selb, 0, w))])
+
+    def diag(out, win, u):
+        t_ = new("cf", 16)
+        tt(t_, ind(win, u), eye, A.mult)
+        red(out, t_, A.add)
+
+    def aims(land, sem, k, b_, b2, sc):
+        spread(land, sem)
+        t_ = new("cf", 8)
+        tt(t_, ap(land, 3, 11), own[k], A.mult)
+        red(b_, t_, A.add, True)
+        aff(b2, b_, 2.0, 0.0)
+        aff(ap("yts", k, k + 1), b_, -1.0 / sc, 0.0)
+
+    wa, wb = ap("wa", 0, 4608), ap("wb", 0, 4608)
+    jl = new("cf", 1)
+    where(jl, "k1", 2048, True, 4352.0 - 7.5)
+    step(jl, ul("ca"), 1)
+    cp(ul("lf", 0, 1), ap("pk", 0, 1))
+    diag(ap("an1", 3, 4), ap("wa", 0, 4224), ul("lf", 0, 1))
+    b2, b2d, b3, b3d = new("cf", 1), new("cf", 1), new("cf", 1), new("cf", 1)
+    aims("an1", "ra1", 0, b2, b2d, 32.0)
+
+    jb = new("cf", 1)
+    where(jb, "k2", 2048, False, 4352.0 - 7.5)
+    step(jb, ul("cc"), 2)
+    cp(ul("bl"), ap("pk", 0, 2))
+    cp(ap("bl", 0, 32), ind(ap("wa", 0, 4352), ul("bl")), "VS")
+    cp(ap("bl", 32, 64), ind(ap("wb", 0, 4352), ul("bl")), "VS")
+
+    parents([ul("l1", 8, 40), ul("l1", 40, 72)], 512, "pc", r1)
+    cp(ul("x"), ap("pc", 0, 128))
+    for i, lv in enumerate(("la", "lc")):
+        for k in range(4):
+            o = 32 * i + 64 * (k // 2)
+            cp(ap(lv, 512 * k, 512 * k + 512), ind((wa, wb)[k % 2], ul("x", o, o + 32)), "VS")
+    for k in range(4):
+        cp(ap("e3", 128 * k, 128 * k + 128), ind(ap("la", 512 * k, 512 * k + 512), mg3), "VS")
+    ring([(ap("e3", 0, 512), ap("lg", 0, 512))], "r3")
+    d4 = ap("xi", 32, 64)
+    q1, kf = new("cf", 32), new("cf", 32)
+    ts(kf, k0, g16, A.subtract)
+    ts(q1, d4, 6527.5, A.is_lt, -8192.0, A.mult)
+    tt(q1, q1, d4, A.add)
+    tt(q1, q1, kf, A.max)
+    ts(ul("i4"), q1, -6016.0, A.add)
+
+    def big_sum(out, lv, b_, sc):
+        act(out, ap(lv, 0, 512), ACT.Abs, b_, sc)
+        for k in range(1, 4):
+            bk = ap(bank(), 0, 512)
+            act(bk, ap(lv, 512 * k, 512 * k + 512), ACT.Abs, b_, sc)
+            tt(out, out, bk, A.add)
+
+    def small_sum(out, src, tmp, b_, sc):
+        n = src["n"] // 4
+        act(tmp, src, ACT.Abs, b_, sc)
+        tt(sub(tmp, 0, 2 * n), sub(tmp, 0, 2 * n), sub(tmp, 2 * n, 4 * n), A.add)
+        tt(out, sub(tmp, 0, n), sub(tmp, n, 2 * n), A.add)
+
+    def ghost_sum(out, tmp, b_, sc):
+        bk = ap(bank(), 0, 256)
+        act(sub(tmp, 0, 256), ap("lg", 0, 256), ACT.Abs, b_, sc)
+        act(bk, ap("lg", 256, 512), ACT.Abs, b_, sc)
+        tt(sub(tmp, 0, 256), sub(tmp, 0, 256), bk, A.add)
+        tt(out, sub(tmp, 0, 128), sub(tmp, 128, 256), A.add)
+
+    def worst_row(x, u, extra):
+        n = x["n"]
+        node("V", lambda g, e: g.vector.transpose(T.xt[:, 0:n], x["ap"]), [x], [ap("xt", 0, n)], cost(n, 1))
+        scan(ap("xs", 0, n), ap("pp", 0, n), ap("xt", 0, n), A.max)
+        w = n // 16
+        a_, r_ = new("cf", w), new("cb", w)
+        ts(a_, ap("xs", 15, n, 16), C32, A.add, C32, A.subtract)
+        tt(r_, a_, ap("xs", 15, n, 16), A.subtract)
+        for h in range(2):
+            mms(ap("pm", h, w, 2),
+                [(sub(ib[h], 16 - 16 * (par - h), 144 - 16 * (par - h)), sub(r_, par, w, 2)) for par in range(2)])
+        ts(u, ap("pm", 0, w), 15.0, A.add)
+        if extra is not None:
+            aff(extra, ap("pm", w - 8, w), 1.0, 15.0)
+
+    def sires(col, u, k, base):
+        r_, tb = new("cf", 16), new("cf", 16)
+        ts(r_, eye, col, A.mult)
+        mms(ap("py", 0, 16), [(bm, r_)])
+        if k == 0:
+            ts(tb, ap("bl", 0, 16), sub(own[1], 0, 1), A.mult)
+            tt(tb, tb, ap("py", 0, 16), A.add)
+        else:
+            cp(tb, ap("py", 0, 16), "VS")
+        cp(ap("yfl", 512 * k, 512 * k + 512), ind(tb, u), "VS")
+        mms(ap("py", 32, 64), [(sub(b0, 15 - m, 143 - m), ap("yfl", 512 * k + m, 512 * k + 512, 16)) for m in range(16)])
+        aff(ap("yss", 32 * k, 32 * k + 32), ap("py", 32, 64), 1.0, base)
+
+    big_sum(ap("xa", 0, 512), "la", b1, 32.0)
+    cp(ap("xa", 512, 640), ind(ap("xa", 0, 512), mg3), "VS")
+    worst_row(ap("xa", 0, 640), ul("m3"), ap("bl", 64, 72))
+    ring([(ap("bl", 0, 72), ap("pb", 0, 72))], "rb")
+    cp(ul("mG"), ap("pb", 64, 72))
+    m3 = ul("m3", 0, 32)
+    sires(jb, m3, 0, 7.5)
+
+    def third(wd, d3, tg, o_, b_, bd_, sc):
+        bv, pv = ap("tb", o_ + 128, o_ + 144), ap("tb", o_ + 144, o_ + 160)
+        small_sum(bv, ap("bl", 0, 64), ap("tb", o_, o_ + 64), b_, sc)
+        big_sum(ap(d3, 0, 512), "la", b_, sc)
+        tt(ap(wd, 512, 1024), ind(bv, m3), ap(d3, 0, 512), A.add)
+        small_sum(pv, ap("pb", 0, 64), ap("tb", o_ + 64, o_ + 128), b_, sc)
+        ghost_sum(ap(tg, 512, 640), ap(tg, 0, 256), b_, sc)
+        tt(ap(wd, 1024, 1152), ind(pv, ul("mG")), ap(tg, 512, 640), A.add)
+        big_sum(ap(wd, 0, 512), "lc", bd_, 2 * sc)
+
+    bo, bv, tv = new("cf", 1), new("cf", 16), new("cf", 64)
+    aff(bo, ap("an1", 3, 4), -32.0, 0.0)
+    small_sum(bv, ap("bl", 0, 64), tv, bo, 32.0)
+    big_sum(ap("sb", 0, 512), "la", bo, 32.0)
+    tt(ap("sb", 512, 1024), ind(bv, m3), ap("sb", 0, 512), A.add)
+    scan(ap("k3", 0, 512), ap("pp", 0, 512), ap("sb", 512, 1024), A.max)
+    where(ul("j2", 0, 1), "k3", 512, True, 0.0)
+    diag(ap("an2", 3, 4), ap("yfl", 0, 512), ul("j2", 0, 1))
+    aims("an2", "ra2", 1, b3, b3d, 1.0)
+    third("wd2", "d32", "tg2", 0, b2, b2d, 32.0)
+    scan(ap("k4", 0, 512), ap("pn", 0, 512), ap("wd2", 512, 1024), A.min)
+    jc = new("cf", 1)
+    where(jc, "k4", 512, False, 0.0)
+    cp(ul("b2", 0, 1), jc)
+    cp(ap("xb", 0, 512), ind(ap("wd2", 0, 1152), ul("i4")), "VS")
+    worst_row(ap("xb", 0, 512), ul("m4"), None)
+    sires(jc, ul("m4"), 1, 6528.0)
+
+    third("wd3", "d33", "tg3", 256, b3, b3d, 1.0)
+    aff(ap("yfs", 0, 512), ap("wd3", 512, 1024), -0.125, 65535.0)
+    bt = new("cf", 16)
+    aff(bt, ind(ap("wd3", 512, 1024), ul("b2", 0, 1)), -0.0625, 0.0)
+    for c in range(2):
+        a_, b_ = 256 * c, 256 * c + 256
+        aff(ap("f4t", a_, b_), ind(ap("wd3", 0, 1152), ul("i4", 16 * c, 16 * c + 16)), -0.0625, 65535.0)
+        tt(ap("yfs", 512 + a_, 512 + b_), ind(bt, ul("m4", 16 * c, 16 * c + 16)), ap("f4t", a_, b_), A.add)
+    dma("Y", T.yt[:], T.yts[:], [ap("yts", 0, 2)], [])
+    dma("Y", T.ys[:], T.yss[:], [ap("yss", 0, 64)], [])
+    dma("Y", T.yf[:, 0:512], T.yfs[:, 0:512], [ap("yfs", 0, 512)], [], 0.5)
+    for c in (512, 768):
+        dma("Y", T.yf[:, c:c + 256], T.yfs[:, c:c + 256], [ap("yfs", c, c + 256)], [], 0.25)
+    assert alloc["dma"] <= NDMA
+    return nodes
+
+
+def run_list(dur, eng, pre, post, pr):
+    n = len(dur)
+    left = [len(x) for x in pre]
+    ready = {}
+    for k in range(n):
+        if left[k] == 0:
+            ready.setdefault(eng[k], {})[k] = 0.0
+    free = {}
+    st = [0.0] * n
+    order = []
+    look = P["look"]
+    for _ in range(n):
+        t0, e0 = 1e18, None
+        for e, r in ready.items():
+            if r:
+                t = max(min(r.values()), free.get(e, 0.0))
+                if t < t0:
+                    t0, e0 = t, e
+        r = ready[e0]
+        lim = t0 + look
+        k = max((pr[j], j) for j, rt in r.items() if rt <= lim)[1]
+        s = max(r.pop(k), free.get(e0, 0.0))
+        st[k] = s
+        if e0 != "X":
+            free[e0] = s + dur[k]
+        order.append(k)
+        for j, _d in post[k]:
+            left[j] -= 1
+            if left[j] == 0:
+                ready.setdefault(eng[j], {})[j] = max(st[i] + dur[i] + d for i, d in pre[j])
+    return order, st
+
+
+def schedule(nodes):
+    n = len(nodes)
+    if n in PLAN:
+        return PLAN[n]
+    dur = [x["dur"] for x in nodes] + [0.0]
+    pre = [[(j, nodes[j]["lat"] + P["sync"]) for j in x["deps"]] for x in nodes]
+    has = set(j for x in nodes for j in x["deps"])
+    pre.append([(k, nodes[k]["lat"]) for k in range(n) if k not in has])
+    post = [[] for _ in range(n + 1)]
+    for k in range(n + 1):
+        for j, d in pre[k]:
+            post[j].append((k, d))
+    flex = [k for k in range(n) if nodes[k]["eng"] == "VS"]
+    eng = ["S" if x["eng"] == "VS" else x["eng"] for x in nodes] + ["X"]
+    pr = [0.0] * (n + 1)
+    for k in range(n, -1, -1):
+        pr[k] = dur[k] + max([pr[j] + d for j, d in post[k]] + [0.0])
+    rng = np.random.default_rng(P["seed"])
+
+    def both(eng, pr):
+        o, st = run_list(dur, eng, pre, post, pr)
+        _o, sb = run_list(dur, eng, post, pre, [st[k] + dur[k] for k in range(n + 1)])
+        p2 = [sb[k] + dur[k] for k in range(n + 1)]
+        o2, s2 = run_list(dur, eng, pre, post, p2)
+        return (o, st, pr) if st[n] <= s2[n] else (o2, s2, p2)
+
+    def score(c, eng):
+        return c[1][n] + P["wv"] * sum(dur[k] for k in flex if eng[k] == "V")
+    best = both(eng, pr)
+    for it in range(P["iters"]):
+        e2 = list(eng)
+        for _i in range(int(rng.integers(0, 4))):
+            k = flex[int(rng.integers(len(flex)))]
+            e2[k] = "V" if e2[k] == "S" else "S"
+        p2 = list(best[2])
+        for _i in range(int(rng.integers(0, 6))):
+            p2[int(rng.integers(n))] += float(rng.normal(0, 1.0))
+        c = both(e2, p2)
+        if score(c, e2) <= score(best, eng) + P["T"] * (1 - it / P["iters"]) * rng.random() ** 4:
+            best, eng = c, e2
+    PLAN[n] = ([k for k in best[0] if k < n], best[1], eng)
+    return PLAN[n]
+
+
+def rank_program(g, core, T, topo):
+    rank = T.rank_of(core)
+    if rank is None:
+        return
+    nodes = build(T, topo, core, rank)
+    order, _st, eng = schedule(nodes)
+    for k, x in enumerate(nodes):
+        x["on"] = eng[k]
+    q = {"V": g.vector, "S": g.scalar, "P": g.tensor, "G": g, "Y": g.sync}
+    need = set()
+    for k, x in enumerate(nodes):
+        if x["on"] == "X":
+            continue
+        for j, how in x["deps"].items():
+            y = nodes[j]
+            if y["kind"] == "c" and (y["on"] != x["on"] or x["kind"] != "c" or (how != "ord" and y["on"] != "P")):
+                need.add(j)
+    cnt = {"V": 0, "S": 0, "P": 0, "G": 0}
+    seen = {}
+    sent = 0
+    for k in order:
+        x = nodes[k]
+        e = x["on"]
+        if e == "X":
+            continue
+        want = {}
+        for j, how in x["deps"].items():
+            y = nodes[j]
+            if y["kind"] == "c":
+                if y["on"] == e and x["kind"] == "c" and (how == "ord" or e == "P"):
+                    continue
+                s, v = "c" + y["on"], y["sig"]
+            else:
+                s, v = y["sem"], y["val"]
+            want[s] = max(want.get(s, 0), v)
+        for s, v in want.items():
+            if seen.get((e, s), 0) < v:
+                q[e].wait_ge(T.sem[s], v)
+                seen[(e, s)] = v
+        ins = x["fn"](g, e)
+        if x["kind"] == "c":
+            if k in need:
+                cnt[e] += 1
+                x["sig"] = cnt[e]
+                ins.then_inc(T.sem["c" + e], 1)
+        elif x["kind"] == "s":
+            sent += x["val"] if x["sem"] == "sent" else 0
+        else:
+            ins.then_inc(T.sem[x["sem"]], 16)
+    g.wait_ge(T.sem["sent"], sent)
+    for x in nodes:
+        if x["kind"] in ("d", "fw") and not any(seen.get((e, x["sem"]), 0) for e in q):
+            g.sync.wait_ge(T.sem[x["sem"]], 16)

@@ -3,16 +3,20 @@ from concourse.bass import DstId, RemoteDMATransfer
 from concourse.mybir import AluOpType, AxisListType, ActivationFunctionType
 
 F32, BF, I32, U16 = "float32", "bfloat16", "int32", "uint16"
-NC = 140
-FWW = 16 * NC + 64
-BIG = 2 ** 24 - 1
+NC = 156
+MAP = 16 * NC
+F0 = 12
+HALF = F0 + MAP + 4
+FWW = F0 + 2 * MAP + 4
 C16 = 1.5 * 2 ** 27
-C32 = 1.5 * 2 ** 28
+C1 = 1.5 * 2 ** 23
 KI = -(16 * NC - 1) / 16.0
-KC = 7.5 * NC - 268.0
+KC = 7.5 * NC - 268.0 + F0
+TO2 = 2176.0 + 16 * MAP - 7.5
 
-ULAY = [("p1", 256), ("p2", 268), ("mg", 32), ("l1", 72), ("g2", 16), ("x", 128), ("i4", 32), ("m3", 40), ("m4", 32),
-        ("mG", 8), ("ca", 8), ("cc", 8), ("lf", 2), ("bl", 2), ("j2", 2), ("b2", 2)]
+ULAY = [("p", 512), ("mg", 32), ("l1", 80), ("xs", 128), ("l2", 128), ("x", 256), ("g1", 32), ("lg", 24), ("g2", 48),
+        ("i4", 32), ("m3", 40), ("m4", 32), ("a1", 16), ("a2", 16), ("a3", 4), ("a4", 4), ("ca", 8), ("cc", 8), ("c2", 24),
+        ("tw", 2), ("tb", 4), ("b2", 2)]
 UOFF = {}
 _o = 0
 for _n, _w in ULAY:
@@ -26,27 +30,26 @@ def _sb(n, d=F32):
 
 
 SCRATCH = {
-    "tri": _sb(2048, I32), "t0i": _sb(4, I32), "tt": _sb(2 * NC, I32), "t1": _sb(256, I32), "xi": _sb(64, I32),
-    "mgi": _sb(32, I32), "u": _sb(UW, U16), "hi": _sb(2 * NC, BF), "lo": _sb(2 * NC, BF), "fw": _sb(FWW, BF),
-    "wa": _sb(4608), "wb": _sb(4608), "w2": _sb(4352), "sb": _sb(2048), "gg": _sb(2048), "k1": _sb(2048), "k2": _sb(2048),
-    "k3": _sb(512), "k4": _sb(512), "res": _sb(1536, BF), "la": _sb(2048), "lc": _sb(2048), "lg": _sb(512),
-    "pb": _sb(72), "bl": _sb(72), "e0": _sb(128), "e1": _sb(256), "e2": _sb(512), "e3": _sb(512), "xa": _sb(640),
-    "xb": _sb(512), "xt": _sb(640), "xs": _sb(640), "wd2": _sb(1152), "wd3": _sb(1152), "d32": _sb(512), "d33": _sb(512),
-    "tg2": _sb(640), "tg3": _sb(640), "tb": _sb(512), "yfl": _sb(1024), "yfs": _sb(1024), "yss": _sb(64), "yts": _sb(2),
-    "f4t": _sb(512), "an1": _sb(12), "an2": _sb(12), "ci": _sb(256, I32), "cf": _sb(4096), "cb": _sb(2048, BF),
-    "pp": _sb(640, BF), "pn": _sb(512, BF),
+    "tw": _sb(2944, I32), "t0i": _sb(4, I32), "li": _sb(608, I32), "u": _sb(UW, U16), "hi": _sb(4 * NC, BF),
+    "lo": _sb(4 * NC, BF), "fw": _sb(FWW, BF), "h0": _sb(2176), "w2": _sb(4608), "sa": _sb(2048),
+    "sb": _sb(2048), "gg": _sb(2048), "k1": _sb(1024), "k2": _sb(1024), "k3": _sb(256), "k4": _sb(256),
+    "res": _sb(3712, BF), "la": _sb(2048), "lc": _sb(2048), "bl": _sb(64), "e0": _sb(128, I32), "e1": _sb(256, I32),
+    "e2": _sb(512, I32), "e3": _sb(256), "xa": _sb(1152), "xb": _sb(512), "xt": _sb(640), "xs": _sb(640), "wd2": _sb(1152),
+    "wd3": _sb(1152), "d3": _sb(2048), "bk": _sb(256), "yb": _sb(512, BF), "cs": _sb(256), "yfl": _sb(512),
+    "yfs": _sb(1024), "yss": _sb(64), "yts": _sb(2), "f4t": _sb(512), "an1": _sb(12), "an2": _sb(12), "cf": _sb(6144),
+    "cb": _sb(3072, BF), "pp": _sb(640, BF), "le": _sb(1024),
 }
-for _n in ("ea", "eb", "ec", "pc", "pd", "pk", "pm", "py"):
+for _n in ("ea", "eb", "ec", "ed", "pc", "pk", "pm", "py"):
     SCRATCH[_n] = ("psum", [128, 512], F32)
-NDMA = 24
-SEMAPHORES = (["cV", "cS", "cP", "cG", "sent", "s0", "r0", "r1", "r2", "r3", "rb", "ra1", "ra2"]
+NDMA = 36
+SEMAPHORES = (["cV", "cS", "cP", "cG", "sent", "r0", "r1", "r2", "r3", "r4", "ra1", "ra2"]
               + ["dm%d" % i for i in range(NDMA)])
 
 A = AluOpType
 ACT = ActivationFunctionType
 CY = 0.00104
-P = {"fix": 0.03, "sync": 0.12, "pe": 0.0008, "dma": 2.0, "hop": 3.0, "hopa": 5.0, "giss": 0.3, "first": 1.0, "look": 0.05,
-     "fv": 1600, "iters": 3000, "seed": 1, "wv": 0.2, "T": 0.5}
+P = {"fix": 0.03, "sync": 0.12, "pe": 0.0006, "dma": 2.0, "hop": 3.0, "hopa": 5.0, "giss": 0.3, "first": 1.0,
+     "iters": 12000, "seed": 1, "T": 0.05, "bias": 0.5, "sd": 2.0, "own": 2, "si": "VS", "su": "VS", "early": 0}
 PLAN = {}
 
 
@@ -54,26 +57,28 @@ def build(T, topo, core, rank):
     N = len(T.cores)
     nodes = []
     acc = {}
-    alloc = {"ci": 0, "cf": 0, "cb": 0, "dma": 0, "bank": 0, "rem": 0}
+    alloc = {"cf": 0, "cb": 0, "dma": 0, "rem": 0}
 
-    def ap(name, lo, hi, step=1, p=None):
+    def ap(name, lo, hi, step=1, p=None, top=None):
         t = T[name]
-        if p is None:
-            x = t[:, lo:hi] if step == 1 else t[:, lo:hi:step]
-        else:
+        if p is not None:
             x = t[p::16, lo:hi]
+        elif top is not None:
+            x = t[0:top, lo:hi] if step == 1 else t[0:top, lo:hi:step]
+        else:
+            x = t[:, lo:hi] if step == 1 else t[:, lo:hi:step]
         return {"ap": x, "r": [(name, lo, hi)], "n": len(range(lo, hi, step)), "dt": SCRATCH[name][2],
-                "ps": SCRATCH[name][0] == "psum", "ind": False}
+                "ps": SCRATCH[name][0] == "psum", "ind": False, "top": top}
 
     def sub(a, lo, hi, step=1):
         name, b, _e = a["r"][0]
-        return ap(name, b + lo, b + hi, step)
+        return ap(name, b + lo, b + hi, step, None, a["top"])
 
-    def new(name, n):
+    def new(name, n, top=None):
         o = alloc[name]
         alloc[name] = o + (n + 15) // 16 * 16
         assert alloc[name] <= SCRATCH[name][1][1], name
-        return ap(name, o, o + n)
+        return ap(name, o, o + n, 1, None, top)
 
     def ul(name, lo=0, hi=None):
         b, e = UOFF[name]
@@ -114,14 +119,17 @@ def build(T, topo, core, rank):
                     if rd and nodes[j]["eng"] != eng:
                         d[j] = "raw"
                     elif j not in d:
-                        d[j] = "ord" if (rd and eng != "VS") else "war"
+                        d[j] = "ord" if (rd and eng != "VS" and nodes[j]["rd"].get(nm)) else "war"
         for (nm, lo, hi) in rr:
             acc.setdefault(nm, []).append((k, lo, hi, False))
+        only = {}
         for (nm, lo, hi, rd) in ww:
+            only[nm] = only.get(nm, True) and rd
             if kind != "fw" and not rd:
                 acc[nm] = [e for e in acc.get(nm, []) if not (lo <= e[1] and e[2] <= hi and e[0] != k)]
             acc.setdefault(nm, []).append((k, lo, hi, True))
-        nodes.append({"eng": eng, "fn": fn, "deps": d, "dur": dur, "lat": lat, "kind": kind, "sem": sem, "val": val})
+        nodes.append({"eng": eng, "fn": fn, "deps": d, "dur": dur, "lat": lat, "kind": kind, "sem": sem, "val": val,
+                      "rd": only, "nm": "%s%d" % (writes or reads or [{"r": [("out", 0)]}])[0]["r"][0][:2]})
         return k
 
     def cost(n, c):
@@ -138,6 +146,9 @@ def build(T, topo, core, rank):
     def val(x):
         return x["ap"] if isap(x) else x
 
+    def aps(*xs):
+        return [x for x in xs if isap(x)]
+
     def cp(out, in_, eng="V"):
         def fn(g, e):
             if e == "V":
@@ -148,36 +159,41 @@ def build(T, topo, core, rank):
     def aff(out, in_, scale, bias, eng="VS"):
         def fn(g, e):
             if e == "V":
-                return g.vector.tensor_scalar(out["ap"], in_["ap"], scale, bias, A.mult, A.add)
-            return g.scalar.activation(out["ap"], in_["ap"], ACT.Identity, bias=bias, scale=scale)
-        return node(eng, fn, [in_], [out], cost(out["n"], 1.56 if in_["ind"] else 1.0))
+                return g.vector.tensor_scalar(out["ap"], in_["ap"], val(scale), val(bias), A.mult, A.add)
+            return g.scalar.activation(out["ap"], in_["ap"], ACT.Identity, bias=val(bias), scale=val(scale))
+        return node(eng, fn, aps(in_, scale, bias), [out], cost(out["n"], 1.56 if in_["ind"] else 1.0))
 
     def ts(out, in0, s1, op0, s2=None, op1=None):
         def fn(g, e):
             if op1 is None:
                 return g.vector.tensor_scalar(out["ap"], in0["ap"], val(s1), None, op0)
             return g.vector.tensor_scalar(out["ap"], in0["ap"], val(s1), val(s2), op0, op1)
-        return node("V", fn, [in0] + [x for x in (s1, s2) if isap(x)], [out], cost(out["n"], cc(out, in0)))
+        return node("V", fn, aps(in0, s1, s2), [out], cost(out["n"], cc(out, in0)))
 
     def tt(out, in0, in1, op):
         c = 1.56 if in0["ind"] else (1.0 if (in0["ps"] or in1["ps"]) else 2.0)
         return node("V", lambda g, e: g.vector.tensor_tensor(out["ap"], in0["ap"], in1["ap"], op), [in0, in1], [out],
                     cost(out["n"], c))
 
-    def red(out, in_, op, neg=False):
-        return node("V", lambda g, e: g.vector.tensor_reduce(out["ap"], in_["ap"], AxisListType.X, op, negate=neg),
-                    [in_], [out], cost(in_["n"], 1.0))
+    def red(out, in_, op):
+        def fn(g, e):
+            if e == "V":
+                return g.vector.tensor_reduce(out["ap"], in_["ap"], AxisListType.X, op)
+            return g.scalar.activation(in_["ap"], in_["ap"], ACT.Identity, accum_out=out["ap"])
+        both = op is A.add
+        return node("VS" if both else "V", fn, [in_], [out] + [in_] * both, cost(in_["n"], 1.0))
 
-    def scan(out, d0, d1, op1, init=0.0):
-        return node("V", lambda g, e: g.vector.tensor_tensor_scan(out["ap"], d0["ap"], d1["ap"], init, A.add, op1),
-                    [d0, d1], [out], cost(out["n"], 1.0))
+    def scan(out, d0, d1, op0, op1, init):
+        return node("V", lambda g, e: g.vector.tensor_tensor_scan(out["ap"], d0["ap"], d1["ap"], val(init), op0, op1),
+                    aps(d0, d1, init), [out], cost(out["n"], 1.0))
 
     def mset(out, v):
         return node("V", lambda g, e: g.vector.memset(out["ap"], v), [], [out], cost(out["n"], cc(out)))
 
-    def act(out, in_, func, bias, scale):
-        return node("S", lambda g, e: g.scalar.activation(out["ap"], in_["ap"], func, bias=val(bias), scale=scale),
-                    [in_] + ([bias] if isap(bias) else []), [out], cost(out["n"], 1.56 if in_["ind"] else 1.0))
+    def act(out, in_, func, bias, scale, total=None):
+        def fn(g, e):
+            return g.scalar.activation(out["ap"], in_["ap"], func, bias=val(bias), scale=val(scale), accum_out=val(total))
+        return node("S", fn, aps(in_, bias, scale), aps(out, total), cost(out["n"], 1.56 if in_["ind"] else 1.0))
 
     def mms(out, pairs):
         def fn(g, e):
@@ -199,18 +215,18 @@ def build(T, topo, core, rank):
             return g.iota(out["ap"], pat, base, cm, allow_small_or_imprecise_dtypes=True)
         return node("G", fn, [], [out], 0.13 + 2 * out["n"] * CY)
 
-    def keep(out, in_, pat, op, base, cm):
-        return node("G", lambda g, e: g.affine_select(out["ap"], in_["ap"], pat, op, 0.0, base, cm), [in_], [out],
+    def keep(out, in_, pat, op, base, cm, fill=0.0):
+        return node("G", lambda g, e: g.affine_select(out["ap"], in_["ap"], pat, op, fill, base, cm), [in_], [out],
                     0.17 + 2 * out["n"] * CY)
 
-    def dma(q, out, in_, reads, writes, extra=0.0, kind="d", deps=()):
+    def dma(q, out, in_, reads, writes, extra=0.0, kind="d"):
         s = "dm%d" % alloc["dma"]
         alloc["dma"] += 1
 
         def fn(g, e):
             qq = g.sync if q == "Y" else g.scalar
             return qq.dma_start(out, in_)
-        return node(q, fn, reads, writes, 0.06, P["dma"] + extra, kind, s, 16, deps)
+        return node(q, fn, reads, writes, 0.06, P["dma"] + extra, kind, s, 16)
 
     nxt = T.cores[(rank + 1) % N]
 
@@ -218,23 +234,20 @@ def build(T, topo, core, rank):
         alloc["rem"] += 1
         return P["giss"] + (P["first"] if alloc["rem"] == 1 else 0.0)
 
-    def ring(parts, sem, ls="sent"):
+    def ring(parts, sem):
         en = topo.engines(core, nxt)
         w = len(en) // len(parts)
         rid, pid = topo.addr(nxt, core)
 
         def fn(g, e):
             return g.remote_dma_fused(
-                [RemoteDMATransfer(dst_ids=[DstId(rid=rid, pnc=pid)] * (len(b) - 1),
-                                   dma_engine_mask=sum(1 << x for x in en[i * w:i * w + w]), remote_sem=T.sem[sem],
-                                   srcs=[b[0]["ap"]], dsts=[x["ap"] for x in b[1:]]) for i, b in enumerate(parts)],
-                local_sem=T.sem[ls])
-        k = node("G", fn, [b[0] for b in parts], [], issue(), 1.0 if ls != "sent" else 0.0, "s", ls, len(en))
+                [RemoteDMATransfer(dst_ids=[DstId(rid=rid, pnc=pid)], dma_engine_mask=sum(1 << x for x in en[i * w:i * w + w]),
+                                   remote_sem=T.sem[sem], srcs=[b[0]["ap"]], dsts=[b[1]["ap"]]) for i, b in enumerate(parts)],
+                local_sem=T.sem["sent"])
+        k = node("G", fn, [b[0] for b in parts], [], issue(), 0.0, "s", "sent", len(en))
         prv = T.cores[(rank - 1) % N]
-        node("X", None, [], [x for b in parts for x in b[1:]], 0.0,
-             P["hop"] - nodes[k]["lat"] + sum(x["n"] for b in parts for x in b[1:]) * 0.002, "x", sem,
-             len(topo.engines(prv, core)) * (len(parts[0]) - 1), [k])
-        return k
+        node("X", None, [], [b[1] for b in parts], 0.0, P["hop"] + sum(b[1]["n"] for b in parts) * 0.002, "x", sem,
+             len(topo.engines(prv, core)), [k])
 
     def common(src):
         m = -1
@@ -260,88 +273,91 @@ def build(T, topo, core, rank):
         tot = sum(bin(common(c)).count("1") for c in T.cores if c != core)
         return node("X", None, [], [ap(land, 4, 11)], 0.0, P["hopa"], "x", sem, tot, [k])
 
-    for (dst, src) in ((ap("mgi", 0, 32), T.mg[:]), (ap("t1", 0, 128), T.sire[:, 0:128]), (ap("t1", 128, 256), T.dam[:, 0:128]),
-                       (ap("t0i", 0, 1), T.aim0[:]), (ap("tt", 4, 132), T.sire[:, 128:256]),
-                       (ap("tt", NC + 4, NC + 132), T.dam[:, 128:256]), (ap("xi", 0, 64), T.dam[:, 256:320])):
+    si, su = P["si"], P["su"]
+    for (dst, src) in ((ap("li", 576, 608), T.mg[:]), (ap("li", 0, 256), T.sire[:]), (ap("li", 256, 576), T.dam[:]),
+                       (ap("t0i", 0, 1), T.aim0[:])):
         dma("Y", dst["ap"], src, [], [dst])
     for c in range(4):
-        dst = ap("tri", 512 * c, 512 * c + 512)
+        dst = ap("tw", 512 * c, 512 * c + 512)
         dma("S", dst["ap"], T.trait[:, 512 * c:512 * c + 512], [], [dst], 0.7 * (c + 1))
 
-    fv = P["fv"]
-    mset(ap("fw", 0, fv), 0.0)
-    iota(ap("fw", fv, FWW), [[0, FWW - fv]], 0, 0)
-    pi_ = new("ci", 1)
-    iota(pi_, [[0, 1]], 0, 1)
-    gi = new("ci", 1)
-    ts(gi, pi_, 112, A.bitwise_and)
-    g16 = new("cf", 1)
-    cp(g16, gi)
-    for base, c0 in ((0, 4352), (NC, 4480)):
-        iota(ap("tt", base, base + 4), [[0, 4]], 4352, 0)
-        iota(ap("tt", base + 132, base + 140), [[16, 8]], c0, 1)
-        ts(ap("tt", base + 132, base + 140), ap("tt", base + 132, base + 140), g16, A.subtract)
-    k0 = new("cf", 32)
-    iota(k0, [[16, 32]], 6016, 1)
+    mset(ap("fw", 0, HALF), 0.0)
+    cp(ap("fw", HALF, FWW), ap("fw", 0, FWW - HALF), "S")
+    mset(ap("hi", 0, 2 * NC), 4352.0)
+    mset(ap("hi", 2 * NC, 4 * NC), 2176.0)
+    mset(ap("lo", 0, 4 * NC), 0.0)
+    for b, lo_, hi_, base in ((1, 132, 140, 4480), (2, 140, 156, 2432), (3, 132, 140, 2304), (3, 140, 156, 2688)):
+        iota(ap("hi", b * NC + lo_, b * NC + hi_), [[128, (hi_ - lo_) // 8], [0, 8]], base, 0)
+    npp = 640 if P["early"] else 512
+    aff(ap("pp", 0, npp), ap("fw", 0, npp), 0.0, 1.0 / 32, "S")
+    aff(ap("pp", 0, npp, 16), ap("pp", 1, npp, 16), 0.0, -2.0 ** 22, "S")
+    R = 16 // N
+    free_row = (R * (rank + 1)) % 16
     oneb, onef = new("cb", 160), new("cf", 144)
     iota(oneb, [[0, 160]], 1, 0)
-    iota(onef, [[0, 144]], 1, 0)
-    bs, bd, b0 = new("cb", 144), new("cb", 144), new("cf", 144)
+    e16, r16 = new("cb", 128, 16), new("cb", 352, 16)
+    keep(e16, ap("cb", 0, 128, 1, None, 16), [[0, 8], [1, 16]], A.is_equal, 0, -1)
+    iota(sub(r16, 0, 256), [[-1, 16], [0, 16]], 0, 0)
+    keep(sub(r16, 0, 256), sub(r16, 0, 256), [[0, 16], [1, 16]], A.is_equal, 0, -1, -2.0 ** 25)
+    iota(sub(r16, 256, 272), [[2, 16]], 0, 0)
+    iota(sub(r16, 272, 276), [[8, 4]], 0, 0)
+    iota(sub(r16, 276, 300), [[0, 3], [16, 8]], 0, 1)
+    keep(sub(r16, 300, 332), ap("cb", 0, 32, 1, None, 16), [[0, 2], [1, 16]], A.is_equal, 0, -1)
+    iota(sub(r16, 332, 337), [[0, 5]], 1, 0)
+    keep(sub(r16, 316, 333), sub(r16, 316, 333), [[0, 17]], A.is_ge, -R * rank, 1)
+    keep(sub(r16, 316, 333), sub(r16, 316, 333), [[0, 17]], A.is_ge, R * rank + R - 1, -1)
+    keep(sub(r16, 333, 337), sub(r16, 333, 337), [[-2, 2], [0, 2]], A.is_ge, 0, 1)
+    keep(sub(r16, 333, 337), sub(r16, 333, 337), [[2, 2], [0, 2]], A.is_ge, 1, -1)
+    mms(ap("py", 0, 337), [(e16, sub(r16, 0, 337))])
+    wt, cx, selb = new("cf", 276), new("cf", 57), new("cb", 4)
+    cp(cx, ap("py", 276, 333), "S")
+    aff(wt, ap("py", 0, 276), 1.0 / 32, 0.0, "S")
+    cp(selb, ap("py", 333, 337), "S")
+    row, eye, eyeo, own = sub(cx, 0, 1), sub(cx, 24, 40), sub(cx, 40, 56), sub(cx, 56, 57)
+    kk = {16: sub(wt, 256, 272), 4: sub(wt, 272, 276)}
+    for b in range(4):
+        w = (8, 24)[b // 2]
+        cp(ap("lo", b * NC + 132, b * NC + 132 + w), sub(cx, 0, w), "S")
+    bs, bd, b0, b0b = new("cb", 144), new("cb", 144), new("cf", 144), new("cb", 144)
     band = [[-16, 9], [200, 16]]
     for b_, c0 in ((bs, 0), (bd, 2)):
         keep(b_, sub(oneb, 0, 144), band, A.is_ge, -3000 - c0, 1)
         keep(b_, b_, [[16, 9], [0, 16]], A.is_ge, 1 + c0, -1)
-    R = 16 // N
-    free_row = (R * (rank + 1)) % 16
+    iota(onef, [[0, 144]], 1, 0)
     keep(b0, onef, band, A.is_equal, -3000 - free_row, 1)
+    keep(b0b, sub(oneb, 0, 144), band, A.is_equal, -3000 - free_row, 1)
     nid = new("cf", 128)
     iota(nid, [[0, 128]], -1, 0)
     keep(nid, nid, [[-1, 128]], A.is_equal, 0, 1)
     bm, bmb = new("cf", 128), new("cb", 128)
-    for b_, one in ((bmb, oneb), (bm, onef)):
-        keep(b_, sub(one, 0, 128), [[-16, 8], [0, 16]], A.is_ge, 0, 1)
-        keep(b_, b_, [[16, 8], [0, 16]], A.is_ge, 15, -1)
-    keep(bm, bm, [[0, 8], [1, 16]], A.is_equal, -free_row, 0)
+    keep(bmb, sub(oneb, 0, 128), [[-16, 8], [0, 16]], A.is_ge, 0, 1)
+    keep(bmb, bmb, [[16, 8], [0, 16]], A.is_ge, 15, -1)
+    keep(bm, bmb, [[0, 8], [1, 16]], A.is_equal, -free_row, 0)
     ib = [new("cb", 160), new("cb", 160)]
     for h in range(2):
         keep(ib[h], oneb, [[32, 5], [1016, 2], [1, 16]], A.is_equal, -16 - 1000 * (1 - h), -1)
-    for nm, n, sg in (("pp", 640, 1), ("pn", 512, -1)):
-        for o in range(0, n, 320):
-            iota(ap(nm, o, min(n, o + 320)), [[0, min(n, o + 320) - o]], sg, 0)
-        iota(ap(nm, 0, n, 16), [[0, n // 16]], -sg * BIG, 0)
-    age = {True: new("cf", 128), False: new("cf", 128)}
-    iota(age[True], [[0, 128]], 16, 0)
-    iota(age[False], [[0, 128]], -16, 0)
-    ey = new("ci", 32)
-    iota(ey, [[1, 32]], 128, -1)
-    ey2 = new("ci", 32)
-    ts(ey2, ey, 15, A.bitwise_and)
-    eye2 = new("cf", 32)
-    ts(eye2, ey2, 0.5, A.is_lt)
-    eye = sub(eye2, 0, 16)
-    selb = new("cb", 2)
-    tt(selb, sub(eye2, 0, 4, 2), sub(eye2, 1, 4, 2), A.add)
-    own = [new("cf", 8), new("cf", 8)]
-    tt(own[1], sub(eye2, R * rank, R * rank + 16, 2), sub(eye2, R * rank + 1, R * rank + 16, 2), A.add)
-    aff(own[0], own[1], 32.0, 0.0)
-    kt = new("cf", 8)
-    mset(kt, KI)
+    cnc, kt, kf = new("cf", 8), new("cf", 8), new("cf", 32)
+    iota(cnc, [[0, 8]], NC, 0)
+    aff(kt, cnc, 0.0, KI, "S")
+    iota(kf, [[16, 32]], 6016, 0)
+    aff(kf, kf, 1.0, row, "S")
 
-    cp(ul("mg"), ap("mgi", 0, 32))
-    cp(ul("p1"), ap("t1", 0, 256))
-    cp(ul("p2"), ap("tt", 4, NC + 132))
-    mg0, mg1, mg3 = ul("mg", 0, 8), ul("mg", 8, 16), ul("mg", 24, 32)
+    cp(ul("mg"), ap("li", 576, 608), su)
+    cp(ul("p", 0, 256), ap("li", 0, 256), su)
+    cp(ul("p", 256, 512), ap("li", 256, 512), su)
+    mg0, mg3 = ul("mg", 0, 8), ul("mg", 24, 32)
     b1, b1d = new("cf", 1), new("cf", 1)
-    ts(b1, ap("t0i", 0, 1), -32.0, A.mult)
-    aff(b1d, b1, 2.0, 0.0)
-    for h in range(2):
-        a_, b_ = h * NC, (h + 1) * NC
-        cp(ap("hi", a_, b_), ap("tt", a_, b_))
-        tt(ap("lo", a_, b_), ap("tt", a_, b_), ap("hi", a_, b_), A.subtract)
+    aff(b1, ap("t0i", 0, 1), -1.0, 0.0)
+    aff(b1d, ap("t0i", 0, 1), -2.0, 0.0)
+    for b, src in enumerate((128, 384, 0, 256)):
+        a_ = b * NC
+        cp(ap("hi", a_ + 4, a_ + 132), ap("li", src, src + 128), "VS")
+        tt(ap("lo", a_ + 4, a_ + 132), ap("li", src, src + 128), ap("hi", a_ + 4, a_ + 132), A.subtract)
         for j, nm in enumerate(("hi", "lo")):
-            dst = ap("fw", 0, 16 * NC, p=2 * h + j)
-            dma("Y", dst["ap"], T[nm][:, a_:b_], [ap(nm, a_, b_)], [dst], 0.3, "fw")
-    fw = ap("fw", 0, FWW)
+            o = F0 + MAP * (b // 2)
+            dst = ap("fw", o, o + MAP, p=2 * (b % 2) + j)
+            dma("Y", dst["ap"], T[nm][:, a_:a_ + NC], [ap(nm, a_, a_ + NC)], [dst], 0.3, "fw")
+    fw, fwa, fw1 = ap("fw", 0, FWW), ap("fw", 0, HALF + 32), ap("fw", 16, HALF)
 
     def place(ym, u):
         n = ym["n"]
@@ -350,230 +366,267 @@ def build(T, topo, core, rank):
         aff(t2, ym, float(NC), KC)
         aff(fl, fl, KI, 0.0)
         tt(t2, t2, fl, A.add)
-        cp(u, t2)
+        cp(u, t2, su)
 
-    def parents(us, ro, bank_, rs):
+    def parents(win, us, ro, bank_, rs):
         c = 0
         for u in us:
-            cp(ap("res", ro + 16 * c, ro + 16 * (c + u["n"])), ind(fw, u), "VS")
+            cp(ap("res", ro + 16 * c, ro + 16 * (c + u["n"])), ind(win, u), "VS")
             c += u["n"]
         for ch, b_ in enumerate((bs, bd)):
             mms(ap(bank_, ch * c, ch * c + c),
                 [(sub(b_, 15 - m, 143 - m), ap("res", ro + m, ro + 16 * c, 16)) for m in range(16)]
                 + ([(nid, rs)] if rs is not None else []))
 
-    def bank():
-        alloc["bank"] += 1
-        return ("ea", "eb", "ec")[alloc["bank"] % 3]
+    def second(y):
+        ym, r_ = new("cf", y["n"]), new("cf", y["n"])
+        ts(ym, y, 2175.0, A.max, TO2, A.add)
+        act(r_, y, ACT.Relu, 2176.0, -1.0)
+        return ym, r_
 
-    ym = new("cf", 72)
-    ts(sub(ym, 0, 8), ap("mgi", 16, 24), 4352.0 - 7.5, A.add)
-    ts(sub(ym, 8, 72), ap("xi", 0, 64), 4351.0, A.max, -7.5, A.add)
-    r1 = new("cf", 64)
-    ts(r1, ap("xi", 0, 64), -1.0, A.mult, 4352.0, A.add)
-    act(r1, r1, ACT.Relu, 0.0, 1.0)
+    ym, r1 = new("cf", 80), new("cf", 64)
+    aff(sub(ym, 0, 8), ap("li", 584, 592), 1.0, 2176.0 + TO2)
+    aff(sub(ym, 8, 16), ap("li", 592, 600), 1.0, 4352.0 - 7.5)
+    ts(sub(ym, 16, 80), ap("li", 512, 576), 4351.0, A.max, -7.5, A.add)
+    act(r1, ap("li", 512, 576), ACT.Relu, 4352.0, -1.0)
     place(ym, ul("l1"))
-    parents([ul("l1", 0, 8)], 0, "pd", None)
-    cp(ul("g2"), ap("pd", 0, 16))
-
-    cp(ap("e0", 0, 128), ind(ap("tri", 0, 2048), mg0))
-    k0_ = ring([(ap("e0", 0, 128), ap("wa", 2048, 2176), ap("wb", 2048, 2176))], "r0", "s0")
-    for c in range(4):
-        a_, b_ = 512 * c, 512 * c + 512
-        cp(ap("wa", a_, b_), ap("tri", a_, b_))
-    for c in range(4):
-        a_, b_ = 2176 + 512 * c, 2176 + 512 * c + 512
-        cp(ap("wa", a_, b_), ind(ap("wa", 0, 2048), ul("p1", 32 * c, 32 * c + 32)), "VS")
-        cp(ap("wb", a_, b_), ind(ap("wa", 0, 2176), ul("p1", 128 + 32 * c, 160 + 32 * c)), "VS")
-    cp(ap("e1", 0, 128), ind(ap("wa", 2176, 4224), mg1), "VS")
-    cp(ap("e1", 128, 256), ind(ap("wb", 2176, 4224), mg1), "VS")
-    ring([(ap("e1", 0, 128), ap("wa", 4224, 4352)), (ap("e1", 128, 256), ap("wb", 4224, 4352))], "r1")
-    dma("Y", T.wb[:, 0:2048], T.wa[:, 0:2048], [ap("wa", 0, 2048)], [ap("wb", 0, 2048)], 3.0, "d", [k0_])
-    for a_, b_ in ((0, 512), (512, 1024), (1024, 1536), (1536, 2048), (2048, 2176)):
-        act(ap("w2", a_, b_), ap("wa", a_, b_), ACT.Abs, b1d, 64.0)
-        bk = ap(bank(), 0, b_ - a_)
-        o_ = ap("w2", 2176 + a_, 2176 + b_)
-        act(o_, ap("wa", 2176 + a_, 2176 + b_), ACT.Abs, b1, 32.0)
-        act(bk, ap("wb", 2176 + a_, 2176 + b_), ACT.Abs, b1, 32.0)
-        tt(o_, o_, bk, A.add)
-    cp(ap("e2", 0, 256), ind(ap("wa", 0, 4352), ul("g2")), "VS")
-    cp(ap("e2", 256, 512), ind(ap("wb", 0, 4352), ul("g2")), "VS")
-    ring([(ap("e2", 0, 256), ap("wa", 4352, 4608)), (ap("e2", 256, 512), ap("wb", 4352, 4608))], "r2")
-    for c in range(4):
-        a_, b_ = 512 * c, 512 * c + 512
-        e_ = 32 * c
-        cp(ap("sb", a_, b_), ind(ap("w2", 0, 4224), ul("p2", e_, e_ + 32)), "VS")
-        tt(ap("gg", a_, b_), ind(ap("w2", 0, 4352), ul("p2", NC + e_, NC + e_ + 32)), ap("sb", a_, b_), A.add)
-        scan(ap("k1", a_, b_), ap("pp", 0, 512), ap("gg", a_, b_), A.max)
-        scan(ap("k2", a_, b_), ap("pn", 0, 512), ap("gg", a_, b_), A.min)
-
-    def where(out, kb, n, big, base):
-        k = ap(kb, 15, n, 16)
-        ns = n // 16
-        sg = 1.0 if big else -1.0
-        op = A.max if big else A.min
-        m_, th = new("cf", 1), new("cf", 1)
-        kp, z = new("cf", ns), new("cf", ns)
-        red(m_, k, op)
-        aff(kp, k, 1.0, 15.0 * sg)
-        low = 0.0
-        if big and n == 512:
-            low = 1024.0
-            kq = new("cf", ns)
-            aff(kq, k, 1.0, -low)
-            k = kq
-        ts(kp, kp, m_, A.is_lt if big else A.is_gt, -8192.0 * sg, A.mult)
-        ts(th, m_, C32, A.add, C32, A.subtract)
-        tt(kp, kp, k, A.add)
-        scan(z, sub(age[big], 0, ns), kp, op, -1e9 * sg)
-        if big:
-            ts(out, th, sub(z, ns - 1, ns), A.subtract, 15.0 + 16.0 * (ns - 1) - low + base, A.add)
-        else:
-            ts(out, sub(z, ns - 1, ns), th, A.subtract, 15.0 + 16.0 * (ns - 1) + base, A.add)
-
-    def step(jm, u, w):
-        fl, c2 = new("cf", 1), new("cf", 1)
-        ts(fl, jm, C16, A.add, C16, A.subtract)
-        aff(c2, jm, float(NC), KC)
-        ts(u, kt, fl, A.mult, c2, A.add)
-        st = new("cb", 128)
-        tt(st, ind(fw, u), bmb, A.mult)
-        mms(ap("pk", 0, w), [(st, sub(selb, 0, w))])
-
-    def diag(out, win, u):
-        t_ = new("cf", 16)
-        tt(t_, ind(win, u), eye, A.mult)
-        red(out, t_, A.add)
-
-    def aims(land, sem, k, b_, b2, sc):
-        spread(land, sem)
-        t_ = new("cf", 8)
-        tt(t_, ap(land, 3, 11), own[k], A.mult)
-        red(b_, t_, A.add, True)
-        aff(b2, b_, 2.0, 0.0)
-        aff(ap("yts", k, k + 1), b_, -1.0 / sc, 0.0)
-
-    wa, wb = ap("wa", 0, 4608), ap("wb", 0, 4608)
-    jl = new("cf", 1)
-    where(jl, "k1", 2048, True, 4352.0 - 7.5)
-    step(jl, ul("ca"), 1)
-    cp(ul("lf", 0, 1), ap("pk", 0, 1))
-    diag(ap("an1", 3, 4), ap("wa", 0, 4224), ul("lf", 0, 1))
-    b2, b2d, b3, b3d = new("cf", 1), new("cf", 1), new("cf", 1), new("cf", 1)
-    aims("an1", "ra1", 0, b2, b2d, 32.0)
-
-    jb = new("cf", 1)
-    where(jb, "k2", 2048, False, 4352.0 - 7.5)
-    step(jb, ul("cc"), 2)
-    cp(ul("bl"), ap("pk", 0, 2))
-    cp(ap("bl", 0, 32), ind(ap("wa", 0, 4352), ul("bl")), "VS")
-    cp(ap("bl", 32, 64), ind(ap("wb", 0, 4352), ul("bl")), "VS")
-
-    parents([ul("l1", 8, 40), ul("l1", 40, 72)], 512, "pc", r1)
-    cp(ul("x"), ap("pc", 0, 128))
-    for i, lv in enumerate(("la", "lc")):
-        for k in range(4):
-            o = 32 * i + 64 * (k // 2)
-            cp(ap(lv, 512 * k, 512 * k + 512), ind((wa, wb)[k % 2], ul("x", o, o + 32)), "VS")
-    for k in range(4):
-        cp(ap("e3", 128 * k, 128 * k + 128), ind(ap("la", 512 * k, 512 * k + 512), mg3), "VS")
-    ring([(ap("e3", 0, 512), ap("lg", 0, 512))], "r3")
-    d4 = ap("xi", 32, 64)
-    q1, kf = new("cf", 32), new("cf", 32)
-    ts(kf, k0, g16, A.subtract)
+    d4 = ap("li", 544, 576)
+    q1 = new("cf", 32)
     ts(q1, d4, 6527.5, A.is_lt, -8192.0, A.mult)
     tt(q1, q1, d4, A.add)
     tt(q1, q1, kf, A.max)
     ts(ul("i4"), q1, -6016.0, A.add)
 
-    def big_sum(out, lv, b_, sc):
-        act(out, ap(lv, 0, 512), ACT.Abs, b_, sc)
+    cp(ap("e0", 0, 128), ind(ap("tw", 0, 2048), mg0), si)
+    ring([(ap("e0", 0, 128), ap("tw", 2048, 2176))], "r0")
+    for a_, b_ in ((0, 512), (512, 1024), (1024, 1536), (1536, 2048), (2048, 2176)):
+        act(ap("h0", a_, b_), ap("tw", a_, b_), ACT.Abs, b1, 1.0)
+        aff(ap("w2", a_, b_), ap("h0", a_, b_), 2.0, 0.0)
+    parents(fw, [ul("l1", 0, 16)], 0, "pk", None)
+    cp(ul("g1"), ap("pk", 0, 32), su)
+    yg, rg = second(ap("pk", 8, 32))
+    for h in range(2):
+        cp(ap("e1", 128 * h, 128 * h + 128), ind(ap("tw", 0, 2176), ul("g1", 16 * h, 16 * h + 8)), si)
+    ring([(ap("e1", 0, 256), ap("tw", 2176, 2432))], "r1")
+    place(yg, ul("lg"))
+    parents(fw, [ul("lg")], 256, "pk", rg)
+    cp(ul("g2"), ap("pk", 0, 48), su)
+    for k, o in enumerate((0, 16, 24, 40)):
+        cp(ap("e2", 128 * k, 128 * k + 128), ind(ap("tw", 0, 2432), ul("g2", o, o + 8)), si)
+    ring([(ap("e2", 0, 512), ap("tw", 2432, 2944))], "r2")
+    for c in range(4):
+        a_, b_ = 512 * c, 512 * c + 512
+        cp(ap("sa", a_, b_), ind(ap("h0", 0, 2048), ul("p", 32 * c, 32 * c + 32)), "VS")
+        tt(ap("w2", 2176 + a_, 2176 + b_), ind(ap("h0", 0, 2176), ul("p", 256 + 32 * c, 288 + 32 * c)), ap("sa", a_, b_), A.add)
+
+    def pair(out, o, n, bk):
+        act(out, ap("tw", o, o + n), ACT.Abs, b1, 1.0)
+        act(ap(bk, 0, n), ap("tw", o + n, o + 2 * n), ACT.Abs, b1, 1.0)
+        tt(out, out, ap(bk, 0, n), A.add)
+
+    pair(ap("w2", 4224, 4352), 2176, 128, "ea")
+    pair(ap("w2", 4352, 4608), 2432, 256, "eb")
+    parents(fwa, [ul("l1", 16, 48), ul("l1", 48, 80)], 640, "pc", r1)
+    cp(ul("xs", 0, 96), ap("pc", 0, 96), su)
+    y2, r2 = second(ap("pc", 0, 128))
+    place(y2, ul("l2"))
+    parents(fw, [ul("l2", 32 * c, 32 * c + 32) for c in range(4)], 1664, "py", r2)
+    cp(ul("x"), ap("py", 0, 256), su)
+
+    def runs(out, src, big, lo, hi):
+        op = A.max if big else A.min
+        scan(ap(out, lo // 2, hi // 2), sub(src, lo, hi, 2), sub(src, lo + 1, hi, 2), op, op,
+             ap(out, lo // 2 - 1, lo // 2) if lo else (-1.0 if big else 2.0 ** 21))
+
+    gg = ap("gg", 0, 2048)
+    for c in range(4):
+        a_, b_ = 512 * c, 512 * c + 512
+        cp(ap("sb", a_, b_), ind(ap("w2", 0, 4224), ul("p", 128 + 32 * c, 160 + 32 * c)), "VS")
+        tt(ap("gg", a_, b_), ind(ap("w2", 0, 4352), ul("p", 384 + 32 * c, 416 + 32 * c)), ap("sb", a_, b_), A.add)
+        runs("k1", gg, True, a_, b_)
+        runs("k2", gg, False, a_, b_)
+
+    def where(run, src, big, u):
+        n, w = src["n"], u["n"]
+        best = ap(run, n // 2 - 1, n // 2)
+        cnt, k, r_ = new("cf", 1), new("cf", 1), new("cf", 1)
+        junk, t_ = new("cf", n // w), new("cf", 16 * w)
+        op = A.add if big else A.subtract
+        act(junk, ap(run, w // 2 - 1, n // 2, w // 2), ACT.Sign, best, -1.0, cnt)
+        ts(u, kk[w], cnt, op, float(w), A.mult)
+        tt(t_, ind(src, u), sub(wt, 0, 16 * w), op)
+        red(r_, t_, A.max if big else A.min)
+        return cnt, k, r_, t_, best
+
+    def look_up(win, u, o, lo, hi):
+        st = new("cb", 128)
+        tt(st, ind(win, u), bmb, A.mult)
+        mms(ap("pk", o, o + hi - lo), [(st, sub(selb, lo, hi))])
+
+    def step(run, big, ua, u, o, lo, hi):
+        cnt, k, r_, _t, best = where(run, gg, big, ua)
+        ts(k, r_, best, A.subtract, -32.0 if big else 32.0, A.mult)
+        ts(u, cnc, k, A.mult, cnt, A.add if big else A.subtract)
+        look_up(fw1, u, o, lo, hi)
+        return cnt, k
+
+    def aims(land, sem, k):
+        spread(land, sem)
+        b_, b2_ = new("cf", 1), new("cf", 1)
+        act(new("cf", 8), ap(land, 3, 11), ACT.Identity, 0.0, -1.0, b_)
+        aff(b2_, b_, 2.0, 0.0)
+        aff(ap("yts", k, k + 1), b_, -1.0, 0.0)
+        return b_, b2_
+
+    step("k1", True, ul("a1"), ul("ca"), 0, 0, 1)
+    cnt, kb = step("k2", False, ul("a2"), ul("cc"), 1, 1, 3)
+    jb = new("cf", 1)
+    aff(jb, cnt, -16.0, kb)
+    y3, r3 = second(ap("pk", 0, 3))
+    fl3, c3 = new("cf", 3), new("cf", 3)
+    ts(fl3, y3, C16, A.add, C16, A.subtract)
+    aff(c3, y3, float(NC), KC)
+    for i, (o, lo_, hi_) in enumerate(((8, 0, 1), (9, 1, 3), (11, 1, 3))):
+        u = ul("c2", 8 * i, 8 * i + 8)
+        aff(u, kt, sub(fl3, i, i + 1), sub(c3, i, i + 1), su)
+        look_up(fw, u, o, lo_, hi_)
+    ts(ul("tw", 0, 1), ap("pk", 8, 9), sub(r3, 0, 1), A.subtract)
+    for i in range(2):
+        ts(ul("tb", 2 * i, 2 * i + 2), ap("pk", 9 + 2 * i, 11 + 2 * i), sub(r3, 1 + i, 2 + i), A.subtract)
+    tp = new("cf", 16)
+    tt(tp, ind(ap("tw", 0, 2432), ul("tw", 0, 1)), eyeo, A.mult)
+    red(ap("an1", 3, 4), tp, A.add)
+    b2, b2d = aims("an1", "ra1", 0)
+    cp(ap("bl", 0, 64), ind(ap("tw", 0, 2432), ul("tb")), "VS")
+
+    tw = ap("tw", 0, 2944)
+    for i, lv in enumerate(("la", "lc")):
+        for k in range(4):
+            o = 32 * i + 64 * k
+            cp(ap(lv, 512 * k, 512 * k + 512), ind(tw, ul("x", o, o + 32)), "VS")
+
+    def big_sum(out, lv, b_, sc, n=512, banks=None):
+        bk = [ap(x, 0, n) for x in (banks or (("ea", "eb") if lv == "la" else ("ec", "ed")))]
+        act(out, ap(lv, 0, n), ACT.Abs, b_, sc)
         for k in range(1, 4):
-            bk = ap(bank(), 0, 512)
-            act(bk, ap(lv, 512 * k, 512 * k + 512), ACT.Abs, b_, sc)
-            tt(out, out, bk, A.add)
+            act(bk[k % 2], ap(lv, n * k, n * k + n), ACT.Abs, b_, sc)
+            tt(out, out, bk[k % 2], A.add)
 
-    def small_sum(out, src, tmp, b_, sc):
-        n = src["n"] // 4
-        act(tmp, src, ACT.Abs, b_, sc)
-        tt(sub(tmp, 0, 2 * n), sub(tmp, 0, 2 * n), sub(tmp, 2 * n, 4 * n), A.add)
-        tt(out, sub(tmp, 0, n), sub(tmp, n, 2 * n), A.add)
+    def best_sum(b_):
+        t_, bv = new("cf", 64), new("cf", 16)
+        act(t_, ap("bl", 0, 64), ACT.Abs, b_, 1.0)
+        tt(sub(t_, 0, 32), sub(t_, 0, 32), sub(t_, 32, 64), A.add)
+        tt(bv, sub(t_, 0, 16), sub(t_, 16, 32), A.add)
+        return bv
 
-    def ghost_sum(out, tmp, b_, sc):
-        bk = ap(bank(), 0, 256)
-        act(sub(tmp, 0, 256), ap("lg", 0, 256), ACT.Abs, b_, sc)
-        act(bk, ap("lg", 256, 512), ACT.Abs, b_, sc)
-        tt(sub(tmp, 0, 256), sub(tmp, 0, 256), bk, A.add)
-        tt(out, sub(tmp, 0, 128), sub(tmp, 128, 256), A.add)
-
-    def worst_row(x, u, extra):
+    def worst_row(x, u):
         n = x["n"]
         node("V", lambda g, e: g.vector.transpose(T.xt[:, 0:n], x["ap"]), [x], [ap("xt", 0, n)], cost(n, 1))
-        scan(ap("xs", 0, n), ap("pp", 0, n), ap("xt", 0, n), A.max)
+        scan(ap("xs", 0, n), ap("pp", 0, n), ap("xt", 0, n), A.add, A.max, 0.0)
         w = n // 16
         a_, r_ = new("cf", w), new("cb", w)
-        ts(a_, ap("xs", 15, n, 16), C32, A.add, C32, A.subtract)
+        ts(a_, ap("xs", 15, n, 16), C1, A.add, C1, A.subtract)
         tt(r_, a_, ap("xs", 15, n, 16), A.subtract)
         for h in range(2):
             mms(ap("pm", h, w, 2),
                 [(sub(ib[h], 16 - 16 * (par - h), 144 - 16 * (par - h)), sub(r_, par, w, 2)) for par in range(2)])
-        ts(u, ap("pm", 0, w), 15.0, A.add)
-        if extra is not None:
-            aff(extra, ap("pm", w - 8, w), 1.0, 15.0)
+        aff(u, ap("pm", 0, w), 32.0, 15.0, su)
 
     def sires(col, u, k, base):
         r_, tb = new("cf", 16), new("cf", 16)
-        ts(r_, eye, col, A.mult)
+        aff(r_, eye, col, 0.0)
         mms(ap("py", 0, 16), [(bm, r_)])
         if k == 0:
-            ts(tb, ap("bl", 0, 16), sub(own[1], 0, 1), A.mult)
+            aff(tb, ap("bl", 0, 16), own, 0.0)
             tt(tb, tb, ap("py", 0, 16), A.add)
         else:
-            cp(tb, ap("py", 0, 16), "VS")
-        cp(ap("yfl", 512 * k, 512 * k + 512), ind(tb, u), "VS")
-        mms(ap("py", 32, 64), [(sub(b0, 15 - m, 143 - m), ap("yfl", 512 * k + m, 512 * k + 512, 16)) for m in range(16)])
+            aff(tb, ap("py", 0, 16), 1.0, -256.0)
+        flat, pick = (("yfl", b0), ("yb", b0b))[k]
+        cp(ap(flat, 0, 512), ind(tb, u), "VS")
+        mms(ap("py", 32, 64), [(sub(pick, 15 - m, 143 - m), ap(flat, m, 512, 16)) for m in range(16)])
         aff(ap("yss", 32 * k, 32 * k + 32), ap("py", 32, 64), 1.0, base)
 
-    big_sum(ap("xa", 0, 512), "la", b1, 32.0)
-    cp(ap("xa", 512, 640), ind(ap("xa", 0, 512), mg3), "VS")
-    worst_row(ap("xa", 0, 640), ul("m3"), ap("bl", 64, 72))
-    ring([(ap("bl", 0, 72), ap("pb", 0, 72))], "rb")
-    cp(ul("mG"), ap("pb", 64, 72))
+    w2 = ap("w2", 0, 4608)
+    cp(ap("xa", 640, 1152), ind(w2, ul("xs", 0, 32)), "VS")
+    tt(ap("xa", 0, 512), ind(w2, ul("xs", 64, 96)), ap("xa", 640, 1152), A.add)
+    if P["early"]:
+        cp(ap("xa", 512, 640), ind(ap("xa", 0, 512), mg3), "VS")
+        for k in range(4):
+            cp(ap("le", 128 * k, 128 * k + 128), ind(ap("la", 512 * k, 512 * k + 512), mg3), "VS")
+    worst_row(ap("xa", 0, npp), ul("m3", 0, npp // 16))
     m3 = ul("m3", 0, 32)
-    sires(jb, m3, 0, 7.5)
+    sires(jb, m3, 0, 4352.0)
 
-    def third(wd, d3, tg, o_, b_, bd_, sc):
-        bv, pv = ap("tb", o_ + 128, o_ + 144), ap("tb", o_ + 144, o_ + 160)
-        small_sum(bv, ap("bl", 0, 64), ap("tb", o_, o_ + 64), b_, sc)
-        big_sum(ap(d3, 0, 512), "la", b_, sc)
-        tt(ap(wd, 512, 1024), ind(bv, m3), ap(d3, 0, 512), A.add)
-        small_sum(pv, ap("pb", 0, 64), ap("tb", o_ + 64, o_ + 128), b_, sc)
-        ghost_sum(ap(tg, 512, 640), ap(tg, 0, 256), b_, sc)
-        tt(ap(wd, 1024, 1152), ind(pv, ul("mG")), ap(tg, 512, 640), A.add)
-        big_sum(ap(wd, 0, 512), "lc", bd_, 2 * sc)
+    def made(out, b_, o):
+        bv = best_sum(b_)
+        big_sum(ap("d3", o, o + 512), "la", b_, 1.0)
+        tt(out, ind(bv, m3), ap("d3", o, o + 512), A.add)
+        return bv
 
-    bo, bv, tv = new("cf", 1), new("cf", 16), new("cf", 64)
-    aff(bo, ap("an1", 3, 4), -32.0, 0.0)
-    small_sum(bv, ap("bl", 0, 64), tv, bo, 32.0)
-    big_sum(ap("sb", 0, 512), "la", bo, 32.0)
-    tt(ap("sb", 512, 1024), ind(bv, m3), ap("sb", 0, 512), A.add)
-    scan(ap("k3", 0, 512), ap("pp", 0, 512), ap("sb", 512, 1024), A.max)
-    where(ul("j2", 0, 1), "k3", 512, True, 0.0)
-    diag(ap("an2", 3, 4), ap("yfl", 0, 512), ul("j2", 0, 1))
-    aims("an2", "ra2", 1, b3, b3d, 1.0)
-    third("wd2", "d32", "tg2", 0, b2, b2d, 32.0)
-    scan(ap("k4", 0, 512), ap("pn", 0, 512), ap("wd2", 512, 1024), A.min)
+    def next_aim(x):
+        runs("k3", x, True, 0, 512)
+        _c, _k, r_, t_, _b = where("k3", x, True, ul("a3"))
+        ts(t_, t_, r_, A.is_equal, own, A.mult)
+        y_ = new("cf", 64)
+        tt(y_, ind(ap("yfl", 0, 512), ul("a3")), t_, A.mult)
+        red(ap("an2", 3, 4), y_, A.add)
+        return aims("an2", "ra2", 1)
+
+    def third(w_, b_, bd_, k, bv):
+        e3 = ap("e3", 128 * k, 128 * k + 128)
+        if k and P["early"]:
+            big_sum(ap("le", 512, 640), "le", b_, 1.0, 128, ("pk", "pc"))
+            tt(e3, ind(bv, ul("m3", 32, 40)), ap("le", 512, 640), A.add)
+        else:
+            cp(e3, ind(ap(w_, 512, 1024), mg3), "VS")
+        ring([(e3, ap(w_, 1024, 1152))], ("r3", "r4")[k])
+        big_sum(ap(w_, 0, 512), "lc", bd_, 2.0)
+
+    xo = ap("d3", 1536, 2048)
+    bo = new("cf", 1)
+    aff(bo, ap("an1", 3, 4), -1.0, 0.0)
+    if P["own"] == 1:
+        made(xo, bo, 0)
+    else:
+        for k in range(4):
+            for r in range(R):
+                p0 = 32 * k + 16 * r
+                dma("Y", T.cs[p0:p0 + 16, :], T.la[R * rank + r::16, 512 * k:512 * k + 512],
+                    [ap("la", 512 * k, 512 * k + 512)], [ap("cs", 0, 256)], 0.2, "fw")
+        back, out_, bc, pc_ = ap("bk", 0, 256), new("cf", 128), new("cf", 1), new("cf", 256)
+        b32 = ap("bk", 0, 256, 1, None, 32)
+        iota(b32, [[0, 256]], 1, 0)
+        keep(b32, b32, [[-1, 2], [-2, 8], [-16, 16]], A.is_equal, 16 * R * rank, 1)
+        for k in range(1, 4):
+            dma("Y", T.bk[32 * k:32 * k + 32, :], T.bk[0:32, :], [back], [back])
+        iota(out_, [[0, 128]], -1, 0)
+        for k in range(4):
+            x = sub(out_, 32 * k, 32 * k + 32)
+            keep(x, x, [[-1, 2], [-16, 8], [0, 2]], A.is_equal, -R * rank, 1)
+        mms(ap("pk", 0, 1), [(out_, ap("an1", 3, 4))])
+        cp(bc, ap("pk", 0, 1), "VS")
+        act(pc_, ap("cs", 0, 256), ACT.Abs, bc, 1.0)
+        for c in range(2):
+            mms(ap("ea", 256 * c, 256 * c + 256), [(sub(back, 128 * c, 128 * c + 128), pc_)])
+        cp(ap("d3", 0, 512), ind(best_sum(bo), m3), "VS")
+        tt(xo, ap("d3", 0, 512), ap("ea", 0, 512), A.add)
+    b3, b3d = next_aim(xo)
+    x2, x3 = ap("wd2", 512, 1024), ap("wd3", 512, 1024)
+    third("wd2", b2, b2d, 0, made(x2, b2, 512))
+    runs("k4", x2, False, 0, 512)
+    cnt, kc, r_, _t, best = where("k4", x2, False, ul("a4"))
+    ts(kc, r_, best, A.subtract, 32.0, A.mult)
     jc = new("cf", 1)
-    where(jc, "k4", 512, False, 0.0)
-    cp(ul("b2", 0, 1), jc)
+    aff(ul("b2", 0, 1), cnt, -4.0, kc, su)
+    aff(jc, cnt, -4.0, kc)
     cp(ap("xb", 0, 512), ind(ap("wd2", 0, 1152), ul("i4")), "VS")
-    worst_row(ap("xb", 0, 512), ul("m4"), None)
-    sires(jc, ul("m4"), 1, 6528.0)
+    worst_row(ap("xb", 0, 512), ul("m4"))
+    sires(jc, ul("m4"), 1, 6528.0 + 256.0)
 
-    third("wd3", "d33", "tg3", 256, b3, b3d, 1.0)
-    aff(ap("yfs", 0, 512), ap("wd3", 512, 1024), -0.125, 65535.0)
+    third("wd3", b3, b3d, 1, made(x3, b3, 1024))
+    aff(ap("yfs", 0, 512), x3, -0.125, 65535.0)
     bt = new("cf", 16)
-    aff(bt, ind(ap("wd3", 512, 1024), ul("b2", 0, 1)), -0.0625, 0.0)
+    aff(bt, ind(x3, ul("b2", 0, 1)), -0.0625, 0.0)
     for c in range(2):
         a_, b_ = 256 * c, 256 * c + 256
         aff(ap("f4t", a_, b_), ind(ap("wd3", 0, 1152), ul("i4", 16 * c, 16 * c + 16)), -0.0625, 65535.0)
@@ -587,37 +640,34 @@ def build(T, topo, core, rank):
     return nodes
 
 
-def run_list(dur, eng, pre, post, pr):
+def lay_out(order, dur, eng, pre, bias):
     n = len(dur)
-    left = [len(x) for x in pre]
-    ready = {}
-    for k in range(n):
-        if left[k] == 0:
-            ready.setdefault(eng[k], {})[k] = 0.0
-    free = {}
-    st = [0.0] * n
-    order = []
-    look = P["look"]
-    for _ in range(n):
-        t0, e0 = 1e18, None
-        for e, r in ready.items():
-            if r:
-                t = max(min(r.values()), free.get(e, 0.0))
-                if t < t0:
-                    t0, e0 = t, e
-        r = ready[e0]
-        lim = t0 + look
-        k = max((pr[j], j) for j, rt in r.items() if rt <= lim)[1]
-        s = max(r.pop(k), free.get(e0, 0.0))
-        st[k] = s
-        if e0 != "X":
-            free[e0] = s + dur[k]
-        order.append(k)
-        for j, _d in post[k]:
-            left[j] -= 1
-            if left[j] == 0:
-                ready.setdefault(eng[j], {})[j] = max(st[i] + dur[i] + d for i, d in pre[j])
-    return order, st
+    st, on = [0.0] * n, [None] * n
+    line = {e: [] for e in "VSPGY"}
+    for k in order:
+        t0 = 0.0
+        for j, d in pre[k]:
+            t = st[j] + dur[j] + d
+            if t > t0:
+                t0 = t
+        if eng[k] == "X":
+            st[k], on[k] = t0, "X"
+            continue
+        best = None
+        for e in eng[k]:
+            t, ln = t0, line[e]
+            i = len(ln)
+            while i > 0 and ln[i - 1][1] > t0:
+                i -= 1
+            while i < len(ln) and ln[i][0] < t + dur[k]:
+                t = max(t, ln[i][1])
+                i += 1
+            c = t + (bias if e == "V" else 0.0)
+            if best is None or c < best[0]:
+                best = (c, t, e, i)
+        _c, st[k], on[k], i = best
+        line[on[k]].insert(i, (st[k], st[k] + dur[k]))
+    return st, on
 
 
 def schedule(nodes):
@@ -632,35 +682,48 @@ def schedule(nodes):
     for k in range(n + 1):
         for j, d in pre[k]:
             post[j].append((k, d))
-    flex = [k for k in range(n) if nodes[k]["eng"] == "VS"]
-    eng = ["S" if x["eng"] == "VS" else x["eng"] for x in nodes] + ["X"]
+    eng = [x["eng"] for x in nodes] + ["X"]
+    rng = np.random.default_rng(P["seed"])
+
+    def rank_by(key, pre, post):
+        left = [len(x) for x in pre]
+        key = list(key)
+        todo = [k for k in range(n + 1) if not left[k]]
+        for k in todo:
+            for j, _d in post[k]:
+                key[j] = max(key[j], key[k] + 1e-6)
+                left[j] -= 1
+                if not left[j]:
+                    todo.append(j)
+        return sorted(range(n + 1), key=lambda k: key[k])
+
+    def both(key, bias, eng):
+        st, on = lay_out(rank_by(key, pre, post), dur, eng, pre, bias)
+        sb, _o = lay_out(rank_by([-st[k] - dur[k] for k in range(n + 1)], post, pre), dur, on, post, 0.0)
+        s2, o2 = lay_out(rank_by([-sb[k] - dur[k] for k in range(n + 1)], pre, post), dur, eng, pre, bias)
+        return (st, on) if st[n] < s2[n] else (s2, o2)
+
     pr = [0.0] * (n + 1)
     for k in range(n, -1, -1):
         pr[k] = dur[k] + max([pr[j] + d for j, d in post[k]] + [0.0])
-    rng = np.random.default_rng(P["seed"])
-
-    def both(eng, pr):
-        o, st = run_list(dur, eng, pre, post, pr)
-        _o, sb = run_list(dur, eng, post, pre, [st[k] + dur[k] for k in range(n + 1)])
-        p2 = [sb[k] + dur[k] for k in range(n + 1)]
-        o2, s2 = run_list(dur, eng, pre, post, p2)
-        return (o, st, pr) if st[n] <= s2[n] else (o2, s2, p2)
-
-    def score(c, eng):
-        return c[1][n] + P["wv"] * sum(dur[k] for k in flex if eng[k] == "V")
-    best = both(eng, pr)
+    cur = best = both([-x for x in pr], P["bias"], eng)
+    big = [k for k in range(n) if eng[k] == "VS"]
     for it in range(P["iters"]):
-        e2 = list(eng)
-        for _i in range(int(rng.integers(0, 4))):
-            k = flex[int(rng.integers(len(flex)))]
-            e2[k] = "V" if e2[k] == "S" else "S"
-        p2 = list(best[2])
+        key = list(cur[0])
+        for _i in range(int(rng.integers(1, 5))):
+            key[int(rng.integers(n))] += float(rng.normal(0, P["sd"]))
+        e2 = list(cur[1])
         for _i in range(int(rng.integers(0, 6))):
-            p2[int(rng.integers(n))] += float(rng.normal(0, 1.0))
-        c = both(e2, p2)
-        if score(c, e2) <= score(best, eng) + P["T"] * (1 - it / P["iters"]) * rng.random() ** 4:
-            best, eng = c, e2
-    PLAN[n] = ([k for k in best[0] if k < n], best[1], eng)
+            e2[big[int(rng.integers(len(big)))]] = "VS"
+        if rng.random() < 0.3:
+            k = big[int(rng.integers(len(big)))]
+            e2[k] = "S" if cur[1][k] == "V" else "V"
+        c = both(key, P["bias"] * 2 * rng.random(), e2)
+        if c[0][n] <= cur[0][n] - P["T"] * (1 - it / P["iters"]) * np.log(rng.random()):
+            cur = c
+            if c[0][n] < best[0][n]:
+                best = c
+    PLAN[n] = (sorted(range(n), key=lambda k: (best[0][k], k)), best[0], best[1])
     return PLAN[n]
 
 
@@ -710,7 +773,7 @@ def rank_program(g, core, T, topo):
                 x["sig"] = cnt[e]
                 ins.then_inc(T.sem["c" + e], 1)
         elif x["kind"] == "s":
-            sent += x["val"] if x["sem"] == "sent" else 0
+            sent += x["val"]
         else:
             ins.then_inc(T.sem[x["sem"]], 16)
     g.wait_ge(T.sem["sent"], sent)

@@ -5,18 +5,17 @@ from concourse.mybir import AluOpType, AxisListType, ActivationFunctionType
 F32, BF, I32, U16 = "float32", "bfloat16", "int32", "uint16"
 NC = 156
 MAP = 16 * NC
-F0 = 12
-HALF = F0 + MAP + 4
-FWW = F0 + 2 * MAP + 4
+F0 = NC - 4
+FWW = F0 + MAP + 40
 C16 = 1.5 * 2 ** 27
 C1 = 1.5 * 2 ** 23
 KI = -(16 * NC - 1) / 16.0
 KC = 7.5 * NC - 268.0 + F0
-TO2 = 2176.0 + 16 * MAP - 7.5
+TO2 = 2176.0 - 7.5
 
-ULAY = [("p", 512), ("mg", 32), ("l1", 80), ("xs", 128), ("l2", 128), ("x", 256), ("g1", 32), ("lg", 24), ("g2", 48),
+ULAY = [("p", 512), ("mg", 32), ("l1", 80), ("xs", 128), ("l2", 128), ("x", 256), ("g1", 32), ("lg", 16), ("g2", 32),
         ("i4", 32), ("m3", 40), ("m4", 32), ("a1", 16), ("a2", 16), ("a3", 4), ("a4", 4), ("ca", 8), ("cc", 8), ("c2", 24),
-        ("tw", 2), ("tb", 4), ("b2", 2)]
+        ("tw", 2), ("tb", 4), ("b2", 2), ("zl", 8)]
 UOFF = {}
 _o = 0
 for _n, _w in ULAY:
@@ -30,26 +29,27 @@ def _sb(n, d=F32):
 
 
 SCRATCH = {
-    "tw": _sb(2944, I32), "t0i": _sb(4, I32), "li": _sb(608, I32), "u": _sb(UW, U16), "hi": _sb(4 * NC, BF),
+    "tw": _sb(2944, I32), "t0i": _sb(8, I32), "li": _sb(608, I32), "u": _sb(UW, U16), "hi": _sb(4 * NC, BF),
     "lo": _sb(4 * NC, BF), "fw": _sb(FWW, BF), "h0": _sb(2176), "w2": _sb(4608), "sa": _sb(2048),
     "sb": _sb(2048), "gg": _sb(2048), "k1": _sb(1024), "k2": _sb(1024), "k3": _sb(256), "k4": _sb(256),
-    "res": _sb(3712, BF), "la": _sb(2048), "lc": _sb(2048), "bl": _sb(64), "e0": _sb(128, I32), "e1": _sb(256, I32),
+    "res": _sb(3712, BF), "la": _sb(2048), "lc": _sb(2048), "bl": _sb(64), "e0": _sb(128, I32), "e1": _sb(272, I32), "z": _sb(264, I32),
     "e2": _sb(512, I32), "e3": _sb(256), "xa": _sb(1152), "xb": _sb(512), "xt": _sb(640), "xs": _sb(640), "wd2": _sb(1152),
     "wd3": _sb(1152), "d3": _sb(2048), "bk": _sb(256), "yb": _sb(512, BF), "cs": _sb(256), "yfl": _sb(512),
     "yfs": _sb(1024), "yss": _sb(64), "yts": _sb(2), "f4t": _sb(512), "an1": _sb(12), "an2": _sb(12), "cf": _sb(6144),
-    "cb": _sb(3072, BF), "pp": _sb(640, BF), "le": _sb(1024),
+    "cb": _sb(3584, BF), "pp": _sb(640, BF), "le": _sb(1024), "lt": _sb(1024), "pq": _sb(4096),
 }
 for _n in ("ea", "eb", "ec", "ed", "pc", "pk", "pm", "py"):
     SCRATCH[_n] = ("psum", [128, 512], F32)
 NDMA = 36
-SEMAPHORES = (["cV", "cS", "cP", "cG", "sent", "r0", "r1", "r2", "r3", "r4", "ra1", "ra2"]
+SEMAPHORES = (["cV", "cS", "cP", "cG", "sent", "r0", "r1", "r2", "r3", "r4", "r5", "r6", "ra1", "ra2"]
               + ["dm%d" % i for i in range(NDMA)])
 
 A = AluOpType
 ACT = ActivationFunctionType
 CY = 0.00104
 P = {"fix": 0.03, "sync": 0.12, "pe": 0.0006, "dma": 2.0, "hop": 3.0, "hopa": 5.0, "giss": 0.3, "first": 1.0,
-     "iters": 12000, "seed": 1, "T": 0.05, "bias": 0.5, "sd": 2.0, "own": 2, "si": "VS", "su": "VS", "early": 0}
+     "iters": 14000, "seed": 1, "T": 0.2, "bias": 0.5, "sd": 2.0, "si": "VS", "su": "VS", "early": 1, "e2v": 1,
+     "pairs": "", "xape": 1, "sum": "B", "far": (0, 0, 3, 0), "skip": 1, "wo": 0.5, "slow": 1.35, "late": 1.35}
 PLAN = {}
 
 
@@ -179,9 +179,9 @@ def build(T, topo, core, rank):
         def fn(g, e):
             if e == "V":
                 return g.vector.tensor_reduce(out["ap"], in_["ap"], AxisListType.X, op)
-            return g.scalar.activation(in_["ap"], in_["ap"], ACT.Identity, accum_out=out["ap"])
-        both = op is A.add
-        return node("VS" if both else "V", fn, [in_], [out] + [in_] * both, cost(in_["n"], 1.0))
+            return g.scalar.activation(junk[0]["ap"], in_["ap"], ACT.Identity, accum_out=out["ap"])
+        junk = [new("cf", in_["n"])] if op is A.add else []
+        return node("VS" if junk else "V", fn, [in_], [out] + junk, cost(in_["n"], 1.0))
 
     def scan(out, d0, d1, op0, op1, init):
         return node("V", lambda g, e: g.vector.tensor_tensor_scan(out["ap"], d0["ap"], d1["ap"], val(init), op0, op1),
@@ -195,11 +195,11 @@ def build(T, topo, core, rank):
             return g.scalar.activation(out["ap"], in_["ap"], func, bias=val(bias), scale=val(scale), accum_out=val(total))
         return node("S", fn, aps(in_, bias, scale), aps(out, total), cost(out["n"], 1.56 if in_["ind"] else 1.0))
 
-    def mms(out, pairs):
+    def mms(out, pairs, start=True, stop=True):
         def fn(g, e):
             r = None
             for i, (l, x) in enumerate(pairs):
-                r = g.tensor.matmul(out["ap"], l["ap"], x["ap"], i == 0, i == len(pairs) - 1)
+                r = g.tensor.matmul(out["ap"], l["ap"], x["ap"], start and i == 0, stop and i == len(pairs) - 1)
             return r
         rd = []
         w = 0
@@ -228,13 +228,12 @@ def build(T, topo, core, rank):
             return qq.dma_start(out, in_)
         return node(q, fn, reads, writes, 0.06, P["dma"] + extra, kind, s, 16)
 
-    nxt = T.cores[(rank + 1) % N]
-
     def issue():
         alloc["rem"] += 1
         return P["giss"] + (P["first"] if alloc["rem"] == 1 else 0.0)
 
-    def ring(parts, sem):
+    def ring(parts, sem, far=1):
+        nxt = T.cores[(rank + far) % N]
         en = topo.engines(core, nxt)
         w = len(en) // len(parts)
         rid, pid = topo.addr(nxt, core)
@@ -245,7 +244,7 @@ def build(T, topo, core, rank):
                                    remote_sem=T.sem[sem], srcs=[b[0]["ap"]], dsts=[b[1]["ap"]]) for i, b in enumerate(parts)],
                 local_sem=T.sem["sent"])
         k = node("G", fn, [b[0] for b in parts], [], issue(), 0.0, "s", "sent", len(en))
-        prv = T.cores[(rank - 1) % N]
+        prv = T.cores[(rank - far) % N]
         node("X", None, [], [b[1] for b in parts], 0.0, P["hop"] + sum(b[1]["n"] for b in parts) * 0.002, "x", sem,
              len(topo.engines(prv, core)), [k])
 
@@ -281,64 +280,78 @@ def build(T, topo, core, rank):
         dst = ap("tw", 512 * c, 512 * c + 512)
         dma("S", dst["ap"], T.trait[:, 512 * c:512 * c + 512], [], [dst], 0.7 * (c + 1))
 
-    mset(ap("fw", 0, HALF), 0.0)
-    cp(ap("fw", HALF, FWW), ap("fw", 0, FWW - HALF), "S")
+    mset(ap("fw", 0, FWW), 0.0)
     mset(ap("hi", 0, 2 * NC), 4352.0)
     mset(ap("hi", 2 * NC, 4 * NC), 2176.0)
     mset(ap("lo", 0, 4 * NC), 0.0)
     for b, lo_, hi_, base in ((1, 132, 140, 4480), (2, 140, 156, 2432), (3, 132, 140, 2304), (3, 140, 156, 2688)):
         iota(ap("hi", b * NC + lo_, b * NC + hi_), [[128, (hi_ - lo_) // 8], [0, 8]], base, 0)
-    npp = 640 if P["early"] else 512
-    aff(ap("pp", 0, npp), ap("fw", 0, npp), 0.0, 1.0 / 32, "S")
-    aff(ap("pp", 0, npp, 16), ap("pp", 1, npp, 16), 0.0, -2.0 ** 22, "S")
+    npp = 640 if P["early"] and "b" not in P["sum"].lower() else 512
+    for o in range(0, npp, 320):
+        x = ap("pp", o, min(npp, o + 320))
+        iota(x, [[0, x["n"]]], -2 ** 22, 0)
+        keep(x, x, [[0, x["n"] // 16], [1, 16]], A.is_equal, 0, 0, 1.0 / 32)
     R = 16 // N
     free_row = (R * (rank + 1)) % 16
-    oneb, onef = new("cb", 160), new("cf", 144)
-    iota(oneb, [[0, 160]], 1, 0)
-    e16, r16 = new("cb", 128, 16), new("cb", 352, 16)
-    keep(e16, ap("cb", 0, 128, 1, None, 16), [[0, 8], [1, 16]], A.is_equal, 0, -1)
-    iota(sub(r16, 0, 256), [[-1, 16], [0, 16]], 0, 0)
-    keep(sub(r16, 0, 256), sub(r16, 0, 256), [[0, 16], [1, 16]], A.is_equal, 0, -1, -2.0 ** 25)
-    iota(sub(r16, 256, 272), [[2, 16]], 0, 0)
-    iota(sub(r16, 272, 276), [[8, 4]], 0, 0)
-    iota(sub(r16, 276, 300), [[0, 3], [16, 8]], 0, 1)
-    keep(sub(r16, 300, 332), ap("cb", 0, 32, 1, None, 16), [[0, 2], [1, 16]], A.is_equal, 0, -1)
-    iota(sub(r16, 332, 337), [[0, 5]], 1, 0)
-    keep(sub(r16, 316, 333), sub(r16, 316, 333), [[0, 17]], A.is_ge, -R * rank, 1)
-    keep(sub(r16, 316, 333), sub(r16, 316, 333), [[0, 17]], A.is_ge, R * rank + R - 1, -1)
-    keep(sub(r16, 333, 337), sub(r16, 333, 337), [[-2, 2], [0, 2]], A.is_ge, 0, 1)
-    keep(sub(r16, 333, 337), sub(r16, 333, 337), [[2, 2], [0, 2]], A.is_ge, 1, -1)
-    mms(ap("py", 0, 337), [(e16, sub(r16, 0, 337))])
-    wt, cx, selb = new("cf", 276), new("cf", 57), new("cb", 4)
-    cp(cx, ap("py", 276, 333), "S")
-    aff(wt, ap("py", 0, 276), 1.0 / 32, 0.0, "S")
-    cp(selb, ap("py", 333, 337), "S")
-    row, eye, eyeo, own = sub(cx, 0, 1), sub(cx, 24, 40), sub(cx, 40, 56), sub(cx, 56, 57)
-    kk = {16: sub(wt, 256, 272), 4: sub(wt, 272, 276)}
+    ci = ap("t0i", 4, 8)
+    row, pair_, cm, ramp = new("cf", 1), new("cf", 1), new("cf", 8), new("cf", 40)
+    iota(sub(ci, 0, 1), [[0, 1]], 0, 1)
+    iota(sub(ramp, 0, 16), [[1, 16]], 0, 0)
+    iota(sub(ramp, 16, 40), [[0, 3], [16, 8]], 0, 0)
+    for i, (x, m) in enumerate(((row, 15), (pair_, 16 - R))):
+        ts(sub(ci, 1 + i, 2 + i), sub(ci, 0, 1), m, A.bitwise_and)
+        cp(x, sub(ci, 1 + i, 2 + i), "VS")
+    ts(cm, sub(ramp, 0, 16, R), pair_, A.is_equal)
+    eye, eyeo, own, selb = new("cf", 16), new("cf", 16), sub(cm, rank, rank + 1), new("cb", 4)
+    ts(eye, sub(ramp, 0, 16), row, A.is_equal)
+    aff(eyeo, eye, own, 0.0)
+    cp(selb, sub(cm, 0, 4), "VS")
     for b in range(4):
         w = (8, 24)[b // 2]
-        cp(ap("lo", b * NC + 132, b * NC + 132 + w), sub(cx, 0, w), "S")
-    bs, bd, b0, b0b = new("cb", 144), new("cb", 144), new("cf", 144), new("cb", 144)
-    band = [[-16, 9], [200, 16]]
-    for b_, c0 in ((bs, 0), (bd, 2)):
-        keep(b_, sub(oneb, 0, 144), band, A.is_ge, -3000 - c0, 1)
-        keep(b_, b_, [[16, 9], [0, 16]], A.is_ge, 1 + c0, -1)
-    iota(onef, [[0, 144]], 1, 0)
-    keep(b0, onef, band, A.is_equal, -3000 - free_row, 1)
-    keep(b0b, sub(oneb, 0, 144), band, A.is_equal, -3000 - free_row, 1)
-    nid = new("cf", 128)
-    iota(nid, [[0, 128]], -1, 0)
-    keep(nid, nid, [[-1, 128]], A.is_equal, 0, 1)
+        aff(ap("lo", b * NC + 132, b * NC + 132 + w), sub(ramp, 16, 16 + w), 1.0, row)
+    oneb = new("cb", 288)
+    iota(oneb, [[0, 288]], 1, 0)
+    b0, b0b = new("cf", 144), new("cb", 144)
+    bands = []
+    for i in range(2):
+        x = new("cb", 288)
+        keep(x, oneb, [[-2, 2], [-16, 9], [200, 16]], A.is_ge, -3000 - 4 * i, 1)
+        keep(x, x, [[2, 2], [16, 9], [0, 16]], A.is_ge, 1 + 4 * i, -1)
+        bands += [sub(x, 0, 144), sub(x, 144, 288)]
+    for x in (b0, b0b):
+        keep(x, sub(oneb, 0, 144), [[-16, 9], [200, 16]], A.is_equal, -3000 - free_row, 1)
+    e16, r16 = new("cb", 128, 16), new("cb", 352, 16)
+    keep(e16, dict(oneb, ap=T.cb[0:16, oneb["r"][0][1]:oneb["r"][0][1] + 128]), [[0, 8], [1, 16]], A.is_equal, 0, -1)
+    iota(sub(r16, 0, 256), [[-1, 16], [0, 16]], -1, 0)
+    iota(sub(r16, 256, 320), [[-1, 4], [0, 16]], 0, 0)
+    keep(sub(r16, 0, 320), sub(r16, 0, 320), [[0, 20], [1, 16]], A.is_equal, 0, -1, -2.0 ** 25)
+    iota(sub(r16, 320, 336), [[2, 16]], 0, 0)
+    iota(sub(r16, 336, 340), [[8, 4]], 0, 0)
+    mms(ap("ed", 0, 340), [(e16, sub(r16, 0, 340))])
+    wt = new("cf", 340)
+    aff(wt, ap("ed", 0, 340), 1.0 / 32, 0.0)
+    kk = {16: sub(wt, 320, 336), 4: sub(wt, 336, 340)}
+    ww_ = {16: sub(wt, 0, 256), 4: sub(wt, 256, 320)}
+    nidp, zero = new("cf", 192), new("cb", 192)
+    mset(zero, 0.0)
+    keep(nidp, zero, [[-1, 192]], A.not_equal, 64, 1, -1.0)
+    nid = sub(nidp, 64, 192)
+    id1, id2, dnc, dki, down = [new("cf", 128) for _ in range(5)]
+    for x, v in ((id1, 1.0), (id2, 2.0), (dnc, float(NC)), (dki, KI)):
+        keep(x, sub(zero, 0, 128), [[-1, 128]], A.not_equal, 0, 1, v)
+    aff(down, id1, own, 0.0)
     bm, bmb = new("cf", 128), new("cb", 128)
     keep(bmb, sub(oneb, 0, 128), [[-16, 8], [0, 16]], A.is_ge, 0, 1)
     keep(bmb, bmb, [[16, 8], [0, 16]], A.is_ge, 15, -1)
     keep(bm, bmb, [[0, 8], [1, 16]], A.is_equal, -free_row, 0)
     ib = [new("cb", 160), new("cb", 160)]
     for h in range(2):
-        keep(ib[h], oneb, [[32, 5], [1016, 2], [1, 16]], A.is_equal, -16 - 1000 * (1 - h), -1)
+        keep(ib[h], sub(oneb, 0, 160), [[32, 5], [1016, 2], [1, 16]], A.is_equal, -16 - 1000 * (1 - h), -1)
     cnc, kt, kf = new("cf", 8), new("cf", 8), new("cf", 32)
-    iota(cnc, [[0, 8]], NC, 0)
-    aff(kt, cnc, 0.0, KI, "S")
+    for x, v in ((cnc, float(NC)), (kt, KI)):
+        keep(x, sub(zero, 0, 8), [[0, 8]], A.not_equal, 0, 0, v)
+        keep(x, x, [[-16, 8]], A.is_ge, 0, 1, -10000.0)
+        keep(x, x, [[16, 8]], A.is_ge, 15, -1, -10000.0)
     iota(kf, [[16, 32]], 6016, 0)
     aff(kf, kf, 1.0, row, "S")
 
@@ -346,34 +359,30 @@ def build(T, topo, core, rank):
     cp(ul("p", 0, 256), ap("li", 0, 256), su)
     cp(ul("p", 256, 512), ap("li", 256, 512), su)
     mg0, mg3 = ul("mg", 0, 8), ul("mg", 24, 32)
-    b1, b1d = new("cf", 1), new("cf", 1)
-    aff(b1, ap("t0i", 0, 1), -1.0, 0.0)
-    aff(b1d, ap("t0i", 0, 1), -2.0, 0.0)
+    b1 = new("cf", 1)
+    cp(b1, ap("t0i", 0, 1), "VS")
     for b, src in enumerate((128, 384, 0, 256)):
         a_ = b * NC
         cp(ap("hi", a_ + 4, a_ + 132), ap("li", src, src + 128), "VS")
         tt(ap("lo", a_ + 4, a_ + 132), ap("li", src, src + 128), ap("hi", a_ + 4, a_ + 132), A.subtract)
         for j, nm in enumerate(("hi", "lo")):
-            o = F0 + MAP * (b // 2)
-            dst = ap("fw", o, o + MAP, p=2 * (b % 2) + j)
+            dst = ap("fw", F0, F0 + MAP, p=2 * b + j)
             dma("Y", dst["ap"], T[nm][:, a_:a_ + NC], [ap(nm, a_, a_ + NC)], [dst], 0.3, "fw")
-    fw, fwa, fw1 = ap("fw", 0, FWW), ap("fw", 0, HALF + 32), ap("fw", 16, HALF)
+    fw = ap("fw", 0, FWW)
 
-    def place(ym, u):
+    def place(ym, u, bk="pm"):
         n = ym["n"]
-        fl, t2 = new("cf", n), new("cf", n)
+        fl = new("cf", n)
         ts(fl, ym, C16, A.add, C16, A.subtract)
-        aff(t2, ym, float(NC), KC)
-        aff(fl, fl, KI, 0.0)
-        tt(t2, t2, fl, A.add)
-        cp(u, t2, su)
+        mms(ap(bk, 0, n), [(dnc, ym), (dki, fl)])
+        aff(u, ap(bk, 0, n), 1.0, KC)
 
-    def parents(win, us, ro, bank_, rs):
+    def parents(which, us, ro, bank_, rs):
         c = 0
         for u in us:
-            cp(ap("res", ro + 16 * c, ro + 16 * (c + u["n"])), ind(win, u), "VS")
+            cp(ap("res", ro + 16 * c, ro + 16 * (c + u["n"])), ind(fw, u), "VS")
             c += u["n"]
-        for ch, b_ in enumerate((bs, bd)):
+        for ch, b_ in enumerate(bands[2 * which:2 * which + 2]):
             mms(ap(bank_, ch * c, ch * c + c),
                 [(sub(b_, 15 - m, 143 - m), ap("res", ro + m, ro + 16 * c, 16)) for m in range(16)]
                 + ([(nid, rs)] if rs is not None else []))
@@ -400,19 +409,37 @@ def build(T, topo, core, rank):
     cp(ap("e0", 0, 128), ind(ap("tw", 0, 2048), mg0), si)
     ring([(ap("e0", 0, 128), ap("tw", 2048, 2176))], "r0")
     for a_, b_ in ((0, 512), (512, 1024), (1024, 1536), (1536, 2048), (2048, 2176)):
-        act(ap("h0", a_, b_), ap("tw", a_, b_), ACT.Abs, b1, 1.0)
+        act(ap("h0", a_, b_), ap("tw", a_, b_), ACT.Abs, b1, -1.0)
         aff(ap("w2", a_, b_), ap("h0", a_, b_), 2.0, 0.0)
-    parents(fw, [ul("l1", 0, 16)], 0, "pk", None)
-    cp(ul("g1"), ap("pk", 0, 32), su)
-    yg, rg = second(ap("pk", 8, 32))
-    for h in range(2):
-        cp(ap("e1", 128 * h, 128 * h + 128), ind(ap("tw", 0, 2176), ul("g1", 16 * h, 16 * h + 8)), si)
-    ring([(ap("e1", 0, 256), ap("tw", 2176, 2432))], "r1")
+    parents(1, [ul("l1", 0, 8)], 0, "pk", None)
+    if P["skip"]:
+        ring([(ap("e0", 0, 128), ap("z", 136, 264))], "r6", 2)
+        ts(ul("g1", 0, 16), ap("pk", 0, 16), 2047.0, A.min)
+        zl = new("cf", 8)
+        ts(zl, ap("pk", 8, 16), 2047.5, A.is_lt, -8192.0, A.mult)
+        tt(zl, zl, ap("pk", 8, 16), A.add)
+        ts(zl, zl, 6016.0 + 136.0 - 2048.0, A.add)
+        tt(zl, zl, sub(kf, 0, 8), A.max)
+        aff(ap("e1", 264, 272), zl, 1.0, -6016.0)
+        iota(ap("e1", 128, 136), [[0, 8]], 0, 0)
+        for h in range(2):
+            cp(ap("e1", 136 * h, 136 * h + 128), ind(ap("tw", 0, 2048), ul("g1", 8 * h, 8 * h + 8)), si)
+        ring([(ap("e1", 0, 136), ap("tw", 2176, 2312)), (ap("e1", 136, 272), ap("z", 0, 136))], "r1")
+        cp(ul("zl"), ap("z", 128, 136), su)
+        cp(ap("tw", 2304, 2432), ind(ap("z", 0, 264), ul("zl")), si)
+    else:
+        cp(ul("g1", 0, 16), ap("pk", 0, 16), su)
+        cp(ap("e1", 0, 256), ind(ap("tw", 0, 2176), ul("g1", 0, 16)), si)
+        ring([(ap("e1", 0, 256), ap("tw", 2176, 2432))], "r1")
+    parents(0, [ul("l1", 8, 16)], 128, "eb", None)
+    if P["e2v"]:
+        cp(ul("g1", 16, 32), ap("eb", 0, 16), su)
+    yg, rg = second(ap("eb", 0, 16))
     place(yg, ul("lg"))
-    parents(fw, [ul("lg")], 256, "pk", rg)
-    cp(ul("g2"), ap("pk", 0, 48), su)
-    for k, o in enumerate((0, 16, 24, 40)):
-        cp(ap("e2", 128 * k, 128 * k + 128), ind(ap("tw", 0, 2432), ul("g2", o, o + 8)), si)
+    parents(1, [ul("lg")], 256, "pk", rg)
+    cp(ul("g2"), ap("pk", 0, 32), su)
+    for k in range(2):
+        cp(ap("e2", 256 * k, 256 * k + 256), ind(ap("tw", 0, 2432), ul("g2", 16 * k, 16 * k + 16)), si)
     ring([(ap("e2", 0, 512), ap("tw", 2432, 2944))], "r2")
     for c in range(4):
         a_, b_ = 512 * c, 512 * c + 512
@@ -420,18 +447,26 @@ def build(T, topo, core, rank):
         tt(ap("w2", 2176 + a_, 2176 + b_), ind(ap("h0", 0, 2176), ul("p", 256 + 32 * c, 288 + 32 * c)), ap("sa", a_, b_), A.add)
 
     def pair(out, o, n, bk):
-        act(out, ap("tw", o, o + n), ACT.Abs, b1, 1.0)
-        act(ap(bk, 0, n), ap("tw", o + n, o + 2 * n), ACT.Abs, b1, 1.0)
+        act(out, ap("tw", o, o + n), ACT.Abs, b1, -1.0)
+        act(ap(bk, 0, n), ap("tw", o + n, o + 2 * n), ACT.Abs, b1, -1.0)
         tt(out, out, ap(bk, 0, n), A.add)
 
     pair(ap("w2", 4224, 4352), 2176, 128, "ea")
-    pair(ap("w2", 4352, 4608), 2432, 256, "eb")
-    parents(fwa, [ul("l1", 16, 48), ul("l1", 48, 80)], 640, "pc", r1)
-    cp(ul("xs", 0, 96), ap("pc", 0, 96), su)
-    y2, r2 = second(ap("pc", 0, 128))
-    place(y2, ul("l2"))
-    parents(fw, [ul("l2", 32 * c, 32 * c + 32) for c in range(4)], 1664, "py", r2)
-    cp(ul("x"), ap("py", 0, 256), su)
+    if P["e2v"]:
+        iota(ap("w2", 4480, 4608), [[0, 128]], 0, 0)
+        cp(ap("le", 768, 896), ind(ap("w2", 0, 4224), ul("g1", 16, 24)), "VS")
+        tt(ap("le", 896, 1024), ind(ap("w2", 0, 4352), ul("g1", 24, 32)), ap("le", 768, 896), A.add)
+        ring([(ap("le", 896, 1024), ap("w2", 4352, 4480))], "r5")
+    else:
+        pair(ap("w2", 4352, 4608), 2432, 256, "eb")
+    for i, (ba, bb) in enumerate((("pc", "py"), ("ec", "ed"))):
+        parents(0, [ul("l1", 16 + 32 * i, 48 + 32 * i)], 640 + 512 * i, ba, sub(r1, 32 * i, 32 * i + 32))
+        if i == 0:
+            cp(ul("xs", 0, 64), ap(ba, 0, 64), su)
+        y2, r2 = second(ap(ba, 0, 64))
+        place(y2, ul("l2", 64 * i, 64 * i + 64), ("pm", ba)[i])
+        parents(1, [ul("l2", 64 * i + c, 64 * i + c + 32) for c in (0, 32)], 1664 + 1024 * i, bb, r2)
+        cp(ul("x", 128 * i, 128 * i + 128), ap(bb, 0, 128), su)
 
     def runs(out, src, big, lo, hi):
         op = A.max if big else A.min
@@ -454,41 +489,40 @@ def build(T, topo, core, rank):
         op = A.add if big else A.subtract
         act(junk, ap(run, w // 2 - 1, n // 2, w // 2), ACT.Sign, best, -1.0, cnt)
         ts(u, kk[w], cnt, op, float(w), A.mult)
-        tt(t_, ind(src, u), sub(wt, 0, 16 * w), op)
+        tt(t_, ind(src, u), ww_[w], op)
         red(r_, t_, A.max if big else A.min)
         return cnt, k, r_, t_, best
 
     def look_up(win, u, o, lo, hi):
         st = new("cb", 128)
-        tt(st, ind(win, u), bmb, A.mult)
+        cp(st, ind(win, u), "VS")
         mms(ap("pk", o, o + hi - lo), [(st, sub(selb, lo, hi))])
 
     def step(run, big, ua, u, o, lo, hi):
         cnt, k, r_, _t, best = where(run, gg, big, ua)
         ts(k, r_, best, A.subtract, -32.0 if big else 32.0, A.mult)
         ts(u, cnc, k, A.mult, cnt, A.add if big else A.subtract)
-        look_up(fw1, u, o, lo, hi)
+        look_up(fw, u, o, lo, hi)
         return cnt, k
 
     def aims(land, sem, k):
         spread(land, sem)
-        b_, b2_ = new("cf", 1), new("cf", 1)
-        act(new("cf", 8), ap(land, 3, 11), ACT.Identity, 0.0, -1.0, b_)
-        aff(b2_, b_, 2.0, 0.0)
-        aff(ap("yts", k, k + 1), b_, -1.0, 0.0)
-        return b_, b2_
+        bs_ = [ap("yts", k, k + 1), new("cf", 1), new("cf", 1)]
+        for i in range(3 if "lc" in P["pairs"] else 2):
+            act(new("cf", 8), ap(land, 3, 11), ACT.Identity, 0.0, 2.0 ** i, bs_[i])
+        return bs_
 
     step("k1", True, ul("a1"), ul("ca"), 0, 0, 1)
-    cnt, kb = step("k2", False, ul("a2"), ul("cc"), 1, 1, 3)
+    cnt, kb = step("k2", False, ul("a2"), ul("cc"), 1, 0, 2)
     jb = new("cf", 1)
     aff(jb, cnt, -16.0, kb)
     y3, r3 = second(ap("pk", 0, 3))
     fl3, c3 = new("cf", 3), new("cf", 3)
     ts(fl3, y3, C16, A.add, C16, A.subtract)
     aff(c3, y3, float(NC), KC)
-    for i, (o, lo_, hi_) in enumerate(((8, 0, 1), (9, 1, 3), (11, 1, 3))):
+    for i, (o, lo_, hi_) in enumerate(((8, 2, 3), (9, 2, 4), (11, 2, 4))):
         u = ul("c2", 8 * i, 8 * i + 8)
-        aff(u, kt, sub(fl3, i, i + 1), sub(c3, i, i + 1), su)
+        aff(u, kt, sub(fl3, i, i + 1), sub(c3, i, i + 1), "V")
         look_up(fw, u, o, lo_, hi_)
     ts(ul("tw", 0, 1), ap("pk", 8, 9), sub(r3, 0, 1), A.subtract)
     for i in range(2):
@@ -496,25 +530,62 @@ def build(T, topo, core, rank):
     tp = new("cf", 16)
     tt(tp, ind(ap("tw", 0, 2432), ul("tw", 0, 1)), eyeo, A.mult)
     red(ap("an1", 3, 4), tp, A.add)
-    b2, b2d = aims("an1", "ra1", 0)
+    b2 = aims("an1", "ra1", 0)
     cp(ap("bl", 0, 64), ind(ap("tw", 0, 2432), ul("tb")), "VS")
 
     tw = ap("tw", 0, 2944)
     for i, lv in enumerate(("la", "lc")):
-        for k in range(4):
-            o = 32 * i + 64 * k
-            cp(ap(lv, 512 * k, 512 * k + 512), ind(tw, ul("x", o, o + 32)), "VS")
+        if lv not in P["pairs"]:
+            for k in range(4):
+                o = 128 * i + 32 * k
+                cp(ap(lv, 512 * k, 512 * k + 512), ind(tw, ul("x", o, o + 32)), "VS")
+            continue
+        for h in range(2):
+            o = 128 * i + 32 * h
+            a_, s_ = ap("sa", 1024 * i + 512 * h, 1024 * i + 512 * h + 512), ap(lv, 512 * h, 512 * h + 512)
+            bk = ap((("ea", "eb"), ("ec", "ed"))[i][h], 0, 512)
+            cp(a_, ind(tw, ul("x", o, o + 32)), "VS")
+            tt(s_, ind(tw, ul("x", o + 64, o + 96)), a_, A.add)
+            mms(bk, [(id2, a_)], True, False)
+            mms(bk, [(nid, s_)], False, True)
+            act(ap(lv, 1024 + 512 * h, 1536 + 512 * h), bk, ACT.Abs, 0.0, i + 1.0)
 
-    def big_sum(out, lv, b_, sc, n=512, banks=None):
+    def big_sum(out, lv, bs_, sc, k_=0, n=512, banks=None):
         bk = [ap(x, 0, n) for x in (banks or (("ea", "eb") if lv == "la" else ("ec", "ed")))]
-        act(out, ap(lv, 0, n), ACT.Abs, b_, sc)
+        if banks is None and lv == "lc" and "cd"[k_] in P["sum"]:
+            for h in range(2):
+                x = ap("pq", 1024 * k_ + 512 * h, 1024 * k_ + 512 * h + 512)
+                act(bk[h], ap(lv, n * h, n * h + n), ACT.Abs, bs_[sc], -float(sc))
+                tt(x, ap(lv, n * (h + 2), n * (h + 3)), bk[h], A.max)
+            for h in range(2):
+                mms(bk[0], [(id1, ap("pq", 1024 * k_ + 512 * h, 1024 * k_ + 512 * h + 512))], h == 0, h == 1)
+            cp(out, bk[0], "VS")
+            return
+        if ("la" if lv == "le" else lv) in P["pairs"]:
+            for h, x in enumerate((out, bk[1])):
+                act(bk[h], ap(lv, n * h, n * h + n), ACT.Abs, bs_[sc], -float(sc))
+                tt(x, ap(lv, n * (h + 2), n * (h + 3)), bk[h], A.max)
+            tt(out, out, bk[1], A.add)
+            return
+        pe = P["far"][2 + k_] if lv == "lc" else 0
+        act(out, ap(lv, 0, n), ACT.Abs, bs_[sc - 1], -float(sc))
+        if pe:
+            for k in range(pe):
+                x = ap("pq", 1536 * k_ + 512 * k, 1536 * k_ + 512 * k + 512)
+                act(x, ap(lv, n * (3 - k), n * (4 - k)), ACT.Abs, bs_[sc - 1], -float(sc))
+                mms(bk[0], [(id1, x)], k == 0, k == pe - 1)
+            if pe == 2:
+                act(bk[1], ap(lv, n, 2 * n), ACT.Abs, bs_[sc - 1], -float(sc))
+                tt(out, out, bk[1], A.add)
+            tt(out, out, bk[0], A.add)
+            return
         for k in range(1, 4):
-            act(bk[k % 2], ap(lv, n * k, n * k + n), ACT.Abs, b_, sc)
+            act(bk[k % 2], ap(lv, n * k, n * k + n), ACT.Abs, bs_[sc - 1], -float(sc))
             tt(out, out, bk[k % 2], A.add)
 
     def best_sum(b_):
         t_, bv = new("cf", 64), new("cf", 16)
-        act(t_, ap("bl", 0, 64), ACT.Abs, b_, 1.0)
+        act(t_, ap("bl", 0, 64), ACT.Abs, b_, -1.0)
         tt(sub(t_, 0, 32), sub(t_, 0, 32), sub(t_, 32, 64), A.add)
         tt(bv, sub(t_, 0, 16), sub(t_, 16, 32), A.add)
         return bv
@@ -535,31 +606,54 @@ def build(T, topo, core, rank):
     def sires(col, u, k, base):
         r_, tb = new("cf", 16), new("cf", 16)
         aff(r_, eye, col, 0.0)
-        mms(ap("py", 0, 16), [(bm, r_)])
-        if k == 0:
-            aff(tb, ap("bl", 0, 16), own, 0.0)
-            tt(tb, tb, ap("py", 0, 16), A.add)
-        else:
-            aff(tb, ap("py", 0, 16), 1.0, -256.0)
+        mms(ap("py", 0, 16), [(bm, r_)] + [(down, ap("bl", 0, 16))] * (1 - k))
+        aff(tb, ap("py", 0, 16), 1.0, -256.0 * k)
         flat, pick = (("yfl", b0), ("yb", b0b))[k]
         cp(ap(flat, 0, 512), ind(tb, u), "VS")
-        mms(ap("py", 32, 64), [(sub(pick, 15 - m, 143 - m), ap(flat, m, 512, 16)) for m in range(16)])
+        w = (4, 16)[k]
+        for o in range(0, 16, w):
+            mms(ap("py", 32, 64), [(sub(pick, 15 - m, 143 - m), ap(flat, m, 512, 16)) for m in range(o, o + w)],
+                o == 0, o + w == 16)
         aff(ap("yss", 32 * k, 32 * k + 32), ap("py", 32, 64), 1.0, base)
 
     w2 = ap("w2", 0, 4608)
     cp(ap("xa", 640, 1152), ind(w2, ul("xs", 0, 32)), "VS")
-    tt(ap("xa", 0, 512), ind(w2, ul("xs", 64, 96)), ap("xa", 640, 1152), A.add)
+    if P["xape"]:
+        cp(ap("xa", 0, 512), ind(w2, ul("xs", 32, 64)), "VS")
+        mms(ap("eb", 0, 512), [(id1, ap("xa", 640, 1152))], True, False)
+        mms(ap("eb", 0, 512), [(id1, ap("xa", 0, 512))], False, True)
+        worst_row(ap("eb", 0, 512), ul("m3", 0, 32))
+    else:
+        tt(ap("xa", 0, 512), ind(w2, ul("xs", 32, 64)), ap("xa", 640, 1152), A.add)
+        if npp > 512:
+            cp(ap("xa", 512, 640), ind(ap("xa", 0, 512), mg3), "VS")
+        worst_row(ap("xa", 0, npp), ul("m3", 0, npp // 16))
     if P["early"]:
-        cp(ap("xa", 512, 640), ind(ap("xa", 0, 512), mg3), "VS")
         for k in range(4):
             cp(ap("le", 128 * k, 128 * k + 128), ind(ap("la", 512 * k, 512 * k + 512), mg3), "VS")
-    worst_row(ap("xa", 0, npp), ul("m3", 0, npp // 16))
     m3 = ul("m3", 0, 32)
-    sires(jb, m3, 0, 4352.0)
+    sires(jb, m3, 0, 4351.0)
 
     def made(out, b_, o):
-        bv = best_sum(b_)
-        big_sum(ap("d3", o, o + 512), "la", b_, 1.0)
+        bv = best_sum(b_[0])
+        k_ = o // 512 - 1
+        if "ab"[k_] in P["sum"] or "AB"[k_] in P["sum"]:
+            t_ = ap("d3", o, o + 512)
+            cp(t_, ind(bv, m3), "VS")
+            pe = P["far"][k_] if "ab"[k_] in P["sum"] else 0
+            far = ap(("pc", "pk")[k_], 0, 512)
+            for k in range(pe):
+                x = ap(("sa", "sb")[k_], 512 * k, 512 * k + 512)
+                act(x, ap("la", 512 * k, 512 * k + 512), ACT.Abs, b_[0], -1.0)
+                mms(far, [(id1, x)], k == 0, k == pe - 1)
+            for k in range(pe, 4):
+                bk = ap(("ea", "eb")[k % 2], 0, 512)
+                act(bk, ap("la", 512 * k, 512 * k + 512), ACT.Abs, b_[0], -1.0)
+                tt(out, t_ if k == pe else out, bk, A.add)
+            if pe:
+                tt(out, out if pe < 4 else t_, far, A.add)
+            return t_
+        big_sum(ap("d3", o, o + 512), "la", b_, 1)
         tt(out, ind(bv, m3), ap("d3", o, o + 512), A.add)
         return bv
 
@@ -572,47 +666,58 @@ def build(T, topo, core, rank):
         red(ap("an2", 3, 4), y_, A.add)
         return aims("an2", "ra2", 1)
 
-    def third(w_, b_, bd_, k, bv):
+    def third(w_, b_, k, bv):
         e3 = ap("e3", 128 * k, 128 * k + 128)
-        if k and P["early"]:
-            big_sum(ap("le", 512, 640), "le", b_, 1.0, 128, ("pk", "pc"))
-            tt(e3, ind(bv, ul("m3", 32, 40)), ap("le", 512, 640), A.add)
+        if P["early"] > 1 - k:
+            x = ap("le", 512 + 128 * k, 640 + 128 * k)
+            t_ = ap("lt", 512 * k, 512 * k + 512)
+            if "la" in P["pairs"]:
+                act(sub(t_, 0, 256), ap("le", 0, 256), ACT.Abs, b_[1], -1.0)
+                tt(sub(t_, 0, 256), sub(t_, 0, 256), ap("le", 256, 512), A.max)
+            else:
+                act(t_, ap("le", 0, 512), ACT.Abs, b_[0], -1.0)
+                tt(sub(t_, 0, 256), sub(t_, 0, 256), sub(t_, 256, 512), A.add)
+            tt(x, sub(t_, 0, 128), sub(t_, 128, 256), A.add)
+            tt(e3, ind(bv, ul("m3", 32, 40) if bv["n"] == 16 else mg3), x, A.add)
         else:
             cp(e3, ind(ap(w_, 512, 1024), mg3), "VS")
         ring([(e3, ap(w_, 1024, 1152))], ("r3", "r4")[k])
-        big_sum(ap(w_, 0, 512), "lc", bd_, 2.0)
+        big_sum(ap(w_, 0, 512), "lc", b_, 2, k)
 
     xo = ap("d3", 1536, 2048)
-    bo = new("cf", 1)
-    aff(bo, ap("an1", 3, 4), -1.0, 0.0)
-    if P["own"] == 1:
-        made(xo, bo, 0)
-    else:
+    bo = ap("an1", 3, 4)
+    if True:
+        sd = "la" in P["pairs"]
         for k in range(4):
             for r in range(R):
                 p0 = 32 * k + 16 * r
-                dma("Y", T.cs[p0:p0 + 16, :], T.la[R * rank + r::16, 512 * k:512 * k + 512],
-                    [ap("la", 512 * k, 512 * k + 512)], [ap("cs", 0, 256)], 0.2, "fw")
+                nm, o = (("sa", "la")[k // 2], 512 * (k % 2)) if sd else ("la", 512 * k)
+                dma("Y", T.cs[p0:p0 + 16, :], T[nm][R * rank + r::16, o:o + 512], [ap(nm, o, o + 512)], [ap("cs", 0, 256)],
+                    0.2, "fw")
+        cs = ap("cs", 0, 256)
+        if sd:
+            mms(ap("pc", 0, 256), [(id1, cs), (sub(nidp, 0, 128), cs)])
+            cs = ap("pc", 0, 256)
         back, out_, bc, pc_ = ap("bk", 0, 256), new("cf", 128), new("cf", 1), new("cf", 256)
         b32 = ap("bk", 0, 256, 1, None, 32)
         iota(b32, [[0, 256]], 1, 0)
         keep(b32, b32, [[-1, 2], [-2, 8], [-16, 16]], A.is_equal, 16 * R * rank, 1)
         for k in range(1, 4):
             dma("Y", T.bk[32 * k:32 * k + 32, :], T.bk[0:32, :], [back], [back])
-        iota(out_, [[0, 128]], -1, 0)
+        iota(out_, [[0, 128]], 1, 0)
         for k in range(4):
             x = sub(out_, 32 * k, 32 * k + 32)
             keep(x, x, [[-1, 2], [-16, 8], [0, 2]], A.is_equal, -R * rank, 1)
-        mms(ap("pk", 0, 1), [(out_, ap("an1", 3, 4))])
-        cp(bc, ap("pk", 0, 1), "VS")
-        act(pc_, ap("cs", 0, 256), ACT.Abs, bc, 1.0)
+        mms(ap("pk", 0, 16), [(out_, tp)])
+        act(new("cf", 16), ap("pk", 0, 16), ACT.Identity, 0.0, 1.0, bc)
+        act(pc_, cs, ACT.Abs, bc, -1.0)
         for c in range(2):
-            mms(ap("ea", 256 * c, 256 * c + 256), [(sub(back, 128 * c, 128 * c + 128), pc_)])
+            mms(ap("pc", 256 * c, 256 * c + 256), [(sub(back, 128 * c, 128 * c + 128), pc_)])
         cp(ap("d3", 0, 512), ind(best_sum(bo), m3), "VS")
-        tt(xo, ap("d3", 0, 512), ap("ea", 0, 512), A.add)
-    b3, b3d = next_aim(xo)
+        tt(xo, ap("d3", 0, 512), ap("pc", 0, 512), A.add)
+    b3 = next_aim(xo)
     x2, x3 = ap("wd2", 512, 1024), ap("wd3", 512, 1024)
-    third("wd2", b2, b2d, 0, made(x2, b2, 512))
+    third("wd2", b2, 0, made(x2, b2, 512))
     runs("k4", x2, False, 0, 512)
     cnt, kc, r_, _t, best = where("k4", x2, False, ul("a4"))
     ts(kc, r_, best, A.subtract, 32.0, A.mult)
@@ -623,7 +728,7 @@ def build(T, topo, core, rank):
     worst_row(ap("xb", 0, 512), ul("m4"))
     sires(jc, ul("m4"), 1, 6528.0 + 256.0)
 
-    third("wd3", b3, b3d, 1, made(x3, b3, 1024))
+    third("wd3", b3, 1, made(x3, b3, 1024))
     aff(ap("yfs", 0, 512), x3, -0.125, 65535.0)
     bt = new("cf", 16)
     aff(bt, ind(x3, ul("b2", 0, 1)), -0.0625, 0.0)
@@ -679,9 +784,11 @@ def schedule(nodes):
     has = set(j for x in nodes for j in x["deps"])
     pre.append([(k, nodes[k]["lat"]) for k in range(n) if k not in has])
     post = [[] for _ in range(n + 1)]
+    up = [set() for _ in range(n + 1)]
     for k in range(n + 1):
         for j, d in pre[k]:
             post[j].append((k, d))
+            up[k] |= up[j] | {j}
     eng = [x["eng"] for x in nodes] + ["X"]
     rng = np.random.default_rng(P["seed"])
 
@@ -701,7 +808,22 @@ def schedule(nodes):
         st, on = lay_out(rank_by(key, pre, post), dur, eng, pre, bias)
         sb, _o = lay_out(rank_by([-st[k] - dur[k] for k in range(n + 1)], post, pre), dur, on, post, 0.0)
         s2, o2 = lay_out(rank_by([-sb[k] - dur[k] for k in range(n + 1)], pre, post), dur, eng, pre, bias)
-        return (st, on) if st[n] < s2[n] else (s2, o2)
+        if st[n] < s2[n]:
+            s2, o2 = st, on
+        order = sorted(range(n + 1), key=lambda k: s2[k])
+        total = s2[n]
+        for du, more in others:
+            end, free = [0.0] * (n + 1), {}
+            for k in order:
+                t = free.get(o2[k], 0.0) if o2[k] != "X" else 0.0
+                for j, d in pre[k]:
+                    if end[j] + d * more > t:
+                        t = end[j] + d * more
+                end[k] = free[o2[k]] = t + du[k]
+            total += P["wo"] * end[n]
+        return s2, o2, total
+
+    others = [([d * (P["slow"] if eng[k] == "P" else 1.0) for k, d in enumerate(dur)], 1.0), (dur, P["late"])]
 
     pr = [0.0] * (n + 1)
     for k in range(n, -1, -1):
@@ -710,18 +832,29 @@ def schedule(nodes):
     big = [k for k in range(n) if eng[k] == "VS"]
     for it in range(P["iters"]):
         key = list(cur[0])
-        for _i in range(int(rng.integers(1, 5))):
-            key[int(rng.integers(n))] += float(rng.normal(0, P["sd"]))
         e2 = list(cur[1])
+        if rng.random() < 0.5:
+            k = int(rng.integers(n))
+            d, w = abs(float(rng.normal(0, 3.0))), 10.0 * rng.random()
+            for j in list(up[k]) + [k]:
+                if key[j] > cur[0][k] - w:
+                    key[j] -= d
+            if rng.random() < 0.3:
+                for j in big:
+                    if cur[0][k] - w < cur[0][j] < cur[0][k] + 2:
+                        e2[j] = "VS"
+        else:
+            for _i in range(int(rng.integers(1, 5))):
+                key[int(rng.integers(n))] += float(rng.normal(0, P["sd"]))
         for _i in range(int(rng.integers(0, 6))):
             e2[big[int(rng.integers(len(big)))]] = "VS"
         if rng.random() < 0.3:
             k = big[int(rng.integers(len(big)))]
             e2[k] = "S" if cur[1][k] == "V" else "V"
         c = both(key, P["bias"] * 2 * rng.random(), e2)
-        if c[0][n] <= cur[0][n] - P["T"] * (1 - it / P["iters"]) * np.log(rng.random()):
+        if c[2] <= cur[2] - P["T"] * (1 - it / P["iters"]) * np.log(rng.random()):
             cur = c
-            if c[0][n] < best[0][n]:
+            if c[2] < best[2]:
                 best = c
     PLAN[n] = (sorted(range(n), key=lambda k: (best[0][k], k)), best[0], best[1])
     return PLAN[n]

import numpy as np
from concourse.bass import DstId, RemoteDMATransfer
from concourse.mybir import AluOpType, AxisListType, ActivationFunctionType

F32, BF, I32, U16 = "float32", "bfloat16", "int32", "uint16"
NC = 156
MAP = 16 * NC
F0 = NC - 4
FWW = F0 + MAP + 40
C16 = 1.5 * 2 ** 27
C1 = 1.5 * 2 ** 23
KI = -(16 * NC - 1) / 16.0
KC = 7.5 * NC - 268.0 + F0
TO2 = 2176.0 - 7.5

ULAY = [("p", 512), ("mg", 32), ("l1", 80), ("xs", 128), ("l2", 128), ("x", 256), ("g1", 32), ("lg", 16), ("g2", 32),
        ("i4", 32), ("m3", 40), ("m4", 32), ("a1", 16), ("a2", 16), ("a3", 4), ("a4", 4), ("ca", 8), ("cc", 8), ("c2", 24),
        ("tw", 2), ("tb", 4), ("b2", 2), ("zl", 8)]
UOFF = {}
_o = 0
for _n, _w in ULAY:
    UOFF[_n] = (_o, _o + _w)
    _o += _w
UW = _o


def _sb(n, d=F32):
    return ("sbuf", [128, n], d)


SCRATCH = {
    "tw": _sb(2944, I32), "t0i": _sb(8, I32), "li": _sb(608, I32), "u": _sb(UW, U16), "hi": _sb(4 * NC, BF),
    "lo": _sb(4 * NC, BF), "fw": _sb(FWW, BF), "h0": _sb(2176), "w2": _sb(4608), "sa": _sb(2048),
    "sb": _sb(2048), "gg": _sb(2048), "k1": _sb(1024), "k2": _sb(1024), "k3": _sb(256), "k4": _sb(256),
    "res": _sb(3712, BF), "la": _sb(2048), "lc": _sb(2048), "bl": _sb(64), "e0": _sb(128, I32), "e1": _sb(272, I32), "z": _sb(264, I32),
    "e2": _sb(512, I32), "e3": _sb(256), "xa": _sb(1152), "xb": _sb(512), "xt": _sb(640), "xs": _sb(640), "wd2": _sb(1152),
    "wd3": _sb(1152), "d3": _sb(2048), "bk": _sb(256), "yb": _sb(512, BF), "cs": _sb(256), "yfl": _sb(512),
    "yfs": _sb(1024), "yss": _sb(64), "yts": _sb(2), "f4t": _sb(512), "an1": _sb(12), "an2": _sb(12), "cf": _sb(6144),
    "cb": _sb(3584, BF), "pp": _sb(640, BF), "le": _sb(1024), "lt": _sb(1024), "pq": _sb(4096),
}
for _n in ("ea", "eb", "ec", "ed", "pc", "pk", "pm", "py"):
    SCRATCH[_n] = ("psum", [128, 512], F32)
NDMA = 36
SEMAPHORES = (["cV", "cS", "cP", "cG", "sent", "r0", "r1", "r2", "r3", "r4", "r5", "r6", "ra1", "ra2"]
              + ["dm%d" % i for i in range(NDMA)])

A = AluOpType
ACT = ActivationFunctionType
CY = 0.00104
P = {"fix": 0.03, "sync": 0.12, "pe": 0.0006, "dma": 2.0, "hop": 3.0, "hopa": 5.0, "giss": 0.3, "first": 1.0,
     "iters": 14000, "seed": 1, "T": 0.2, "bias": 0.5, "sd": 2.0, "si": "VS", "su": "VS", "early": 1, "e2v": 1,
     "pairs": "", "xape": 1, "sum": "B", "far": (0, 0, 3, 0), "skip": 1, "wo": 0.5, "slow": 1.35, "late": 1.35}
PLAN = {}


def build(T, topo, core, rank):
    N = len(T.cores)
    nodes = []
    acc = {}
    alloc = {"cf": 0, "cb": 0, "dma": 0, "rem": 0}

    def ap(name, lo, hi, step=1, p=None, top=None):
        t = T[name]
        if p is not None:
            x = t[p::16, lo:hi]
        elif top is not None:
            x = t[0:top, lo:hi] if step == 1 else t[0:top, lo:hi:step]
        else:
            x = t[:, lo:hi] if step == 1 else t[:, lo:hi:step]
        return {"ap": x, "r": [(name, lo, hi)], "n": len(range(lo, hi, step)), "dt": SCRATCH[name][2],
                "ps": SCRATCH[name][0] == "psum", "ind": False, "top": top}

    def sub(a, lo, hi, step=1):
        name, b, _e = a["r"][0]
        return ap(name, b + lo, b + hi, step, None, a["top"])

    def new(name, n, top=None):
        o = alloc[name]
        alloc[name] = o + (n + 15) // 16 * 16
        assert alloc[name] <= SCRATCH[name][1][1], name
        return ap(name, o, o + n, 1, None, top)

    def ul(name, lo=0, hi=None):
        b, e = UOFF[name]
        return ap("u", b + lo, e if hi is None else b + hi)

    def ind(win, off):
        return {"ap": win["ap"].indirect(off["ap"]), "r": win["r"] + off["r"], "n": 16 * off["n"], "dt": win["dt"],
                "ps": False, "ind": True}

    def node(eng, fn, reads, writes, dur, lat=0.0, kind="c", sem=None, val=0, deps=()):
        k = len(nodes)
        d = {}
        for x in deps:
            d[x] = "raw"
        rr = []
        ww = []
        for a in reads:
            for (nm, lo, hi) in a["r"]:
                if SCRATCH[nm][0] == "psum":
                    ww.append((nm, 0, 512, True))
                else:
                    rr.append((nm, lo, hi))
        for a in writes:
            nm, lo, hi = a["r"][0]
            if SCRATCH[nm][0] == "psum":
                ww.append((nm, 0, 512, False))
            else:
                ww.append((nm, lo, hi, False))
        for (nm, lo, hi) in rr:
            for (j, l2, h2, w) in acc.get(nm, []):
                if w and l2 < hi and lo < h2:
                    d[j] = "raw"
        for (nm, lo, hi, rd) in ww:
            for (j, l2, h2, w) in acc.get(nm, []):
                if l2 < hi and lo < h2 and j != k:
                    if kind == "fw" and nodes[j]["kind"] == "fw":
                        continue
                    if rd and nodes[j]["eng"] != eng:
                        d[j] = "raw"
                    elif j not in d:
                        d[j] = "ord" if (rd and eng != "VS" and nodes[j]["rd"].get(nm)) else "war"
        for (nm, lo, hi) in rr:
            acc.setdefault(nm, []).append((k, lo, hi, False))
        only = {}
        for (nm, lo, hi, rd) in ww:
            only[nm] = only.get(nm, True) and rd
            if kind != "fw" and not rd:
                acc[nm] = [e for e in acc.get(nm, []) if not (lo <= e[1] and e[2] <= hi and e[0] != k)]
            acc.setdefault(nm, []).append((k, lo, hi, True))
        nodes.append({"eng": eng, "fn": fn, "deps": d, "dur": dur, "lat": lat, "kind": kind, "sem": sem, "val": val,
                      "rd": only, "nm": "%s%d" % (writes or reads or [{"r": [("out", 0)]}])[0]["r"][0][:2]})
        return k

    def cost(n, c):
        return P["fix"] + max(64, n * c) * CY

    def cc(*xs):
        if any(x["ind"] for x in xs):
            return 1.56
        return 0.5 if all(x["dt"] in (BF, U16) for x in xs) else 1.0

    def isap(x):
        return isinstance(x, dict)

    def val(x):
        return x["ap"] if isap(x) else x

    def aps(*xs):
        return [x for x in xs if isap(x)]

    def cp(out, in_, eng="V"):
        def fn(g, e):
            if e == "V":
                return g.vector.tensor_copy(out["ap"], in_["ap"])
            return g.scalar.activation(out["ap"], in_["ap"], ACT.Copy)
        return node(eng, fn, [in_], [out], cost(out["n"], cc(out, in_) if (eng == "V" or in_["ind"]) else 1.0))

    def aff(out, in_, scale, bias, eng="VS"):
        def fn(g, e):
            if e == "V":
                return g.vector.tensor_scalar(out["ap"], in_["ap"], val(scale), val(bias), A.mult, A.add)
            return g.scalar.activation(out["ap"], in_["ap"], ACT.Identity, bias=val(bias), scale=val(scale))
        return node(eng, fn, aps(in_, scale, bias), [out], cost(out["n"], 1.56 if in_["ind"] else 1.0))

    def ts(out, in0, s1, op0, s2=None, op1=None):
        def fn(g, e):
            if op1 is None:
                return g.vector.tensor_scalar(out["ap"], in0["ap"], val(s1), None, op0)
            return g.vector.tensor_scalar(out["ap"], in0["ap"], val(s1), val(s2), op0, op1)
        return node("V", fn, aps(in0, s1, s2), [out], cost(out["n"], cc(out, in0)))

    def tt(out, in0, in1, op):
        c = 1.56 if in0["ind"] else (1.0 if (in0["ps"] or in1["ps"]) else 2.0)
        return node("V", lambda g, e: g.vector.tensor_tensor(out["ap"], in0["ap"], in1["ap"], op), [in0, in1], [out],
                    cost(out["n"], c))

    def red(out, in_, op):
        def fn(g, e):
            if e == "V":
                return g.vector.tensor_reduce(out["ap"], in_["ap"], AxisListType.X, op)
            return g.scalar.activation(junk[0]["ap"], in_["ap"], ACT.Identity, accum_out=out["ap"])
        junk = [new("cf", in_["n"])] if op is A.add else []
        return node("VS" if junk else "V", fn, [in_], [out] + junk, cost(in_["n"], 1.0))

    def scan(out, d0, d1, op0, op1, init):
        return node("V", lambda g, e: g.vector.tensor_tensor_scan(out["ap"], d0["ap"], d1["ap"], val(init), op0, op1),
                    aps(d0, d1, init), [out], cost(out["n"], 1.0))

    def mset(out, v):
        return node("V", lambda g, e: g.vector.memset(out["ap"], v), [], [out], cost(out["n"], cc(out)))

    def act(out, in_, func, bias, scale, total=None):
        def fn(g, e):
            return g.scalar.activation(out["ap"], in_["ap"], func, bias=val(bias), scale=val(scale), accum_out=val(total))
        return node("S", fn, aps(in_, bias, scale), aps(out, total), cost(out["n"], 1.56 if in_["ind"] else 1.0))

    def mms(out, pairs, start=True, stop=True):
        def fn(g, e):
            r = None
            for i, (l, x) in enumerate(pairs):
                r = g.tensor.matmul(out["ap"], l["ap"], x["ap"], start and i == 0, stop and i == len(pairs) - 1)
            return r
        rd = []
        w = 0
        for l, x in pairs:
            rd += [l, x]
            w += 4 if l["dt"] == F32 else 1
        return node("P", fn, rd, [out], 0.05 + w * max(64, out["n"]) * P["pe"])

    def iota(out, pat, base, cm):
        def fn(g, e):
            if out["dt"] == I32:
                return g.iota(out["ap"], pat, base, cm)
            return g.iota(out["ap"], pat, base, cm, allow_small_or_imprecise_dtypes=True)
        return node("G", fn, [], [out], 0.13 + 2 * out["n"] * CY)

    def keep(out, in_, pat, op, base, cm, fill=0.0):
        return node("G", lambda g, e: g.affine_select(out["ap"], in_["ap"], pat, op, fill, base, cm), [in_], [out],
                    0.17 + 2 * out["n"] * CY)

    def dma(q, out, in_, reads, writes, extra=0.0, kind="d"):
        s = "dm%d" % alloc["dma"]
        alloc["dma"] += 1

        def fn(g, e):
            qq = g.sync if q == "Y" else g.scalar
            return qq.dma_start(out, in_)
        return node(q, fn, reads, writes, 0.06, P["dma"] + extra, kind, s, 16)

    def issue():
        alloc["rem"] += 1
        return P["giss"] + (P["first"] if alloc["rem"] == 1 else 0.0)

    def ring(parts, sem, far=1):
        nxt = T.cores[(rank + far) % N]
        en = topo.engines(core, nxt)
        w = len(en) // len(parts)
        rid, pid = topo.addr(nxt, core)

        def fn(g, e):
            return g.remote_dma_fused(
                [RemoteDMATransfer(dst_ids=[DstId(rid=rid, pnc=pid)], dma_engine_mask=sum(1 << x for x in en[i * w:i * w + w]),
                                   remote_sem=T.sem[sem], srcs=[b[0]["ap"]], dsts=[b[1]["ap"]]) for i, b in enumerate(parts)],
                local_sem=T.sem["sent"])
        k = node("G", fn, [b[0] for b in parts], [], issue(), 0.0, "s", "sent", len(en))
        prv = T.cores[(rank - far) % N]
        node("X", None, [], [b[1] for b in parts], 0.0, P["hop"] + sum(b[1]["n"] for b in parts) * 0.002, "x", sem,
             len(topo.engines(prv, core)), [k])

    def common(src):
        m = -1
        for c in T.cores:
            if c != src:
                m &= topo.mask(src, c)
        return m

    def spread(land, sem):
        m = common(core)
        ids, dsts = [], []
        for c in range(1, N):
            d = T.cores[(rank - c) % N]
            rid, pid = topo.addr(d, core)
            ids.append(DstId(rid=rid, pnc=pid))
            dsts.append(T[land][:, 3 + c:4 + c])
        src = ap(land, 3, 4)

        def fn(g, e):
            tr = RemoteDMATransfer(dst_ids=ids, dma_engine_mask=m, remote_sem=T.sem[sem], srcs=[src["ap"]], dsts=dsts)
            return g.remote_dma_fused([tr], local_sem=T.sem["sent"])
        k = node("G", fn, [src], [], issue(), 0.0, "s", "sent", bin(m).count("1"))
        tot = sum(bin(common(c)).count("1") for c in T.cores if c != core)
        return node("X", None, [], [ap(land, 4, 11)], 0.0, P["hopa"], "x", sem, tot, [k])

    si, su = P["si"], P["su"]
    for (dst, src) in ((ap("li", 576, 608), T.mg[:]), (ap("li", 0, 256), T.sire[:]), (ap("li", 256, 576), T.dam[:]),
                       (ap("t0i", 0, 1), T.aim0[:])):
        dma("Y", dst["ap"], src, [], [dst])
    for c in range(4):
        dst = ap("tw", 512 * c, 512 * c + 512)
        dma("S", dst["ap"], T.trait[:, 512 * c:512 * c + 512], [], [dst], 0.7 * (c + 1))

    mset(ap("fw", 0, FWW), 0.0)
    mset(ap("hi", 0, 2 * NC), 4352.0)
    mset(ap("hi", 2 * NC, 4 * NC), 2176.0)
    mset(ap("lo", 0, 4 * NC), 0.0)
    for b, lo_, hi_, base in ((1, 132, 140, 4480), (2, 140, 156, 2432), (3, 132, 140, 2304), (3, 140, 156, 2688)):
        iota(ap("hi", b * NC + lo_, b * NC + hi_), [[128, (hi_ - lo_) // 8], [0, 8]], base, 0)
    npp = 640 if P["early"] and "b" not in P["sum"].lower() else 512
    for o in range(0, npp, 320):
        x = ap("pp", o, min(npp, o + 320))
        iota(x, [[0, x["n"]]], -2 ** 22, 0)
        keep(x, x, [[0, x["n"] // 16], [1, 16]], A.is_equal, 0, 0, 1.0 / 32)
    R = 16 // N
    free_row = (R * (rank + 1)) % 16
    ci = ap("t0i", 4, 8)
    row, pair_, cm, ramp = new("cf", 1), new("cf", 1), new("cf", 8), new("cf", 40)
    iota(sub(ci, 0, 1), [[0, 1]], 0, 1)
    iota(sub(ramp, 0, 16), [[1, 16]], 0, 0)
    iota(sub(ramp, 16, 40), [[0, 3], [16, 8]], 0, 0)
    for i, (x, m) in enumerate(((row, 15), (pair_, 16 - R))):
        ts(sub(ci, 1 + i, 2 + i), sub(ci, 0, 1), m, A.bitwise_and)
        cp(x, sub(ci, 1 + i, 2 + i), "VS")
    ts(cm, sub(ramp, 0, 16, R), pair_, A.is_equal)
    eye, eyeo, own, selb = new("cf", 16), new("cf", 16), sub(cm, rank, rank + 1), new("cb", 4)
    ts(eye, sub(ramp, 0, 16), row, A.is_equal)
    aff(eyeo, eye, own, 0.0)
    cp(selb, sub(cm, 0, 4), "VS")
    for b in range(4):
        w = (8, 24)[b // 2]
        aff(ap("lo", b * NC + 132, b * NC + 132 + w), sub(ramp, 16, 16 + w), 1.0, row)
    oneb = new("cb", 288)
    iota(oneb, [[0, 288]], 1, 0)
    b0, b0b = new("cf", 144), new("cb", 144)
    bands = []
    for i in range(2):
        x = new("cb", 288)
        keep(x, oneb, [[-2, 2], [-16, 9], [200, 16]], A.is_ge, -3000 - 4 * i, 1)
        keep(x, x, [[2, 2], [16, 9], [0, 16]], A.is_ge, 1 + 4 * i, -1)
        bands += [sub(x, 0, 144), sub(x, 144, 288)]
    for x in (b0, b0b):
        keep(x, sub(oneb, 0, 144), [[-16, 9], [200, 16]], A.is_equal, -3000 - free_row, 1)
    e16, r16 = new("cb", 128, 16), new("cb", 352, 16)
    keep(e16, dict(oneb, ap=T.cb[0:16, oneb["r"][0][1]:oneb["r"][0][1] + 128]), [[0, 8], [1, 16]], A.is_equal, 0, -1)
    iota(sub(r16, 0, 256), [[-1, 16], [0, 16]], -1, 0)
    iota(sub(r16, 256, 320), [[-1, 4], [0, 16]], 0, 0)
    keep(sub(r16, 0, 320), sub(r16, 0, 320), [[0, 20], [1, 16]], A.is_equal, 0, -1, -2.0 ** 25)
    iota(sub(r16, 320, 336), [[2, 16]], 0, 0)
    iota(sub(r16, 336, 340), [[8, 4]], 0, 0)
    mms(ap("ed", 0, 340), [(e16, sub(r16, 0, 340))])
    wt = new("cf", 340)
    aff(wt, ap("ed", 0, 340), 1.0 / 32, 0.0)
    kk = {16: sub(wt, 320, 336), 4: sub(wt, 336, 340)}
    ww_ = {16: sub(wt, 0, 256), 4: sub(wt, 256, 320)}
    nidp, zero = new("cf", 192), new("cb", 192)
    mset(zero, 0.0)
    keep(nidp, zero, [[-1, 192]], A.not_equal, 64, 1, -1.0)
    nid = sub(nidp, 64, 192)
    id1, id2, dnc, dki, down = [new("cf", 128) for _ in range(5)]
    for x, v in ((id1, 1.0), (id2, 2.0), (dnc, float(NC)), (dki, KI)):
        keep(x, sub(zero, 0, 128), [[-1, 128]], A.not_equal, 0, 1, v)
    aff(down, id1, own, 0.0)
    bm, bmb = new("cf", 128), new("cb", 128)
    keep(bmb, sub(oneb, 0, 128), [[-16, 8], [0, 16]], A.is_ge, 0, 1)
    keep(bmb, bmb, [[16, 8], [0, 16]], A.is_ge, 15, -1)
    keep(bm, bmb, [[0, 8], [1, 16]], A.is_equal, -free_row, 0)
    ib = [new("cb", 160), new("cb", 160)]
    for h in range(2):
        keep(ib[h], sub(oneb, 0, 160), [[32, 5], [1016, 2], [1, 16]], A.is_equal, -16 - 1000 * (1 - h), -1)
    cnc, kt, kf = new("cf", 8), new("cf", 8), new("cf", 32)
    for x, v in ((cnc, float(NC)), (kt, KI)):
        keep(x, sub(zero, 0, 8), [[0, 8]], A.not_equal, 0, 0, v)
        keep(x, x, [[-16, 8]], A.is_ge, 0, 1, -10000.0)
        keep(x, x, [[16, 8]], A.is_ge, 15, -1, -10000.0)
    iota(kf, [[16, 32]], 6016, 0)
    aff(kf, kf, 1.0, row, "S")

    cp(ul("mg"), ap("li", 576, 608), su)
    cp(ul("p", 0, 256), ap("li", 0, 256), su)
    cp(ul("p", 256, 512), ap("li", 256, 512), su)
    mg0, mg3 = ul("mg", 0, 8), ul("mg", 24, 32)
    b1 = new("cf", 1)
    cp(b1, ap("t0i", 0, 1), "VS")
    for b, src in enumerate((128, 384, 0, 256)):
        a_ = b * NC
        cp(ap("hi", a_ + 4, a_ + 132), ap("li", src, src + 128), "VS")
        tt(ap("lo", a_ + 4, a_ + 132), ap("li", src, src + 128), ap("hi", a_ + 4, a_ + 132), A.subtract)
        for j, nm in enumerate(("hi", "lo")):
            dst = ap("fw", F0, F0 + MAP, p=2 * b + j)
            dma("Y", dst["ap"], T[nm][:, a_:a_ + NC], [ap(nm, a_, a_ + NC)], [dst], 0.3, "fw")
    fw = ap("fw", 0, FWW)

    def place(ym, u, bk="pm"):
        n = ym["n"]
        fl = new("cf", n)
        ts(fl, ym, C16, A.add, C16, A.subtract)
        mms(ap(bk, 0, n), [(dnc, ym), (dki, fl)])
        aff(u, ap(bk, 0, n), 1.0, KC)

    def parents(which, us, ro, bank_, rs):
        c = 0
        for u in us:
            cp(ap("res", ro + 16 * c, ro + 16 * (c + u["n"])), ind(fw, u), "VS")
            c += u["n"]
        for ch, b_ in enumerate(bands[2 * which:2 * which + 2]):
            mms(ap(bank_, ch * c, ch * c + c),
                [(sub(b_, 15 - m, 143 - m), ap("res", ro + m, ro + 16 * c, 16)) for m in range(16)]
                + ([(nid, rs)] if rs is not None else []))

    def second(y):
        ym, r_ = new("cf", y["n"]), new("cf", y["n"])
        ts(ym, y, 2175.0, A.max, TO2, A.add)
        act(r_, y, ACT.Relu, 2176.0, -1.0)
        return ym, r_

    ym, r1 = new("cf", 80), new("cf", 64)
    aff(sub(ym, 0, 8), ap("li", 584, 592), 1.0, 2176.0 + TO2)
    aff(sub(ym, 8, 16), ap("li", 592, 600), 1.0, 4352.0 - 7.5)
    ts(sub(ym, 16, 80), ap("li", 512, 576), 4351.0, A.max, -7.5, A.add)
    act(r1, ap("li", 512, 576), ACT.Relu, 4352.0, -1.0)
    place(ym, ul("l1"))
    d4 = ap("li", 544, 576)
    q1 = new("cf", 32)
    ts(q1, d4, 6527.5, A.is_lt, -8192.0, A.mult)
    tt(q1, q1, d4, A.add)
    tt(q1, q1, kf, A.max)
    ts(ul("i4"), q1, -6016.0, A.add)

    cp(ap("e0", 0, 128), ind(ap("tw", 0, 2048), mg0), si)
    ring([(ap("e0", 0, 128), ap("tw", 2048, 2176))], "r0")
    for a_, b_ in ((0, 512), (512, 1024), (1024, 1536), (1536, 2048), (2048, 2176)):
        act(ap("h0", a_, b_), ap("tw", a_, b_), ACT.Abs, b1, -1.0)
        aff(ap("w2", a_, b_), ap("h0", a_, b_), 2.0, 0.0)
    parents(1, [ul("l1", 0, 8)], 0, "pk", None)
    if P["skip"]:
        ring([(ap("e0", 0, 128), ap("z", 136, 264))], "r6", 2)
        ts(ul("g1", 0, 16), ap("pk", 0, 16), 2047.0, A.min)
        zl = new("cf", 8)
        ts(zl, ap("pk", 8, 16), 2047.5, A.is_lt, -8192.0, A.mult)
        tt(zl, zl, ap("pk", 8, 16), A.add)
        ts(zl, zl, 6016.0 + 136.0 - 2048.0, A.add)
        tt(zl, zl, sub(kf, 0, 8), A.max)
        aff(ap("e1", 264, 272), zl, 1.0, -6016.0)
        iota(ap("e1", 128, 136), [[0, 8]], 0, 0)
        for h in range(2):
            cp(ap("e1", 136 * h, 136 * h + 128), ind(ap("tw", 0, 2048), ul("g1", 8 * h, 8 * h + 8)), si)
        ring([(ap("e1", 0, 136), ap("tw", 2176, 2312)), (ap("e1", 136, 272), ap("z", 0, 136))], "r1")
        cp(ul("zl"), ap("z", 128, 136), su)
        cp(ap("tw", 2304, 2432), ind(ap("z", 0, 264), ul("zl")), si)
    else:
        cp(ul("g1", 0, 16), ap("pk", 0, 16), su)
        cp(ap("e1", 0, 256), ind(ap("tw", 0, 2176), ul("g1", 0, 16)), si)
        ring([(ap("e1", 0, 256), ap("tw", 2176, 2432))], "r1")
    parents(0, [ul("l1", 8, 16)], 128, "eb", None)
    if P["e2v"]:
        cp(ul("g1", 16, 32), ap("eb", 0, 16), su)
    yg, rg = second(ap("eb", 0, 16))
    place(yg, ul("lg"))
    parents(1, [ul("lg")], 256, "pk", rg)
    cp(ul("g2"), ap("pk", 0, 32), su)
    for k in range(2):
        cp(ap("e2", 256 * k, 256 * k + 256), ind(ap("tw", 0, 2432), ul("g2", 16 * k, 16 * k + 16)), si)
    ring([(ap("e2", 0, 512), ap("tw", 2432, 2944))], "r2")
    for c in range(4):
        a_, b_ = 512 * c, 512 * c + 512
        cp(ap("sa", a_, b_), ind(ap("h0", 0, 2048), ul("p", 32 * c, 32 * c + 32)), "VS")
        tt(ap("w2", 2176 + a_, 2176 + b_), ind(ap("h0", 0, 2176), ul("p", 256 + 32 * c, 288 + 32 * c)), ap("sa", a_, b_), A.add)

    def pair(out, o, n, bk):
        act(out, ap("tw", o, o + n), ACT.Abs, b1, -1.0)
        act(ap(bk, 0, n), ap("tw", o + n, o + 2 * n), ACT.Abs, b1, -1.0)
        tt(out, out, ap(bk, 0, n), A.add)

    pair(ap("w2", 4224, 4352), 2176, 128, "ea")
    if P["e2v"]:
        iota(ap("w2", 4480, 4608), [[0, 128]], 0, 0)
        cp(ap("le", 768, 896), ind(ap("w2", 0, 4224), ul("g1", 16, 24)), "VS")
        tt(ap("le", 896, 1024), ind(ap("w2", 0, 4352), ul("g1", 24, 32)), ap("le", 768, 896), A.add)
        ring([(ap("le", 896, 1024), ap("w2", 4352, 4480))], "r5")
    else:
        pair(ap("w2", 4352, 4608), 2432, 256, "eb")
    for i, (ba, bb) in enumerate((("pc", "py"), ("ec", "ed"))):
        parents(0, [ul("l1", 16 + 32 * i, 48 + 32 * i)], 640 + 512 * i, ba, sub(r1, 32 * i, 32 * i + 32))
        if i == 0:
            cp(ul("xs", 0, 64), ap(ba, 0, 64), su)
        y2, r2 = second(ap(ba, 0, 64))
        place(y2, ul("l2", 64 * i, 64 * i + 64), ("pm", ba)[i])
        parents(1, [ul("l2", 64 * i + c, 64 * i + c + 32) for c in (0, 32)], 1664 + 1024 * i, bb, r2)
        cp(ul("x", 128 * i, 128 * i + 128), ap(bb, 0, 128), su)

    def runs(out, src, big, lo, hi):
        op = A.max if big else A.min
        scan(ap(out, lo // 2, hi // 2), sub(src, lo, hi, 2), sub(src, lo + 1, hi, 2), op, op,
             ap(out, lo // 2 - 1, lo // 2) if lo else (-1.0 if big else 2.0 ** 21))

    gg = ap("gg", 0, 2048)
    for c in range(4):
        a_, b_ = 512 * c, 512 * c + 512
        cp(ap("sb", a_, b_), ind(ap("w2", 0, 4224), ul("p", 128 + 32 * c, 160 + 32 * c)), "VS")
        tt(ap("gg", a_, b_), ind(ap("w2", 0, 4352), ul("p", 384 + 32 * c, 416 + 32 * c)), ap("sb", a_, b_), A.add)
        runs("k1", gg, True, a_, b_)
        runs("k2", gg, False, a_, b_)

    def where(run, src, big, u):
        n, w = src["n"], u["n"]
        best = ap(run, n // 2 - 1, n // 2)
        cnt, k, r_ = new("cf", 1), new("cf", 1), new("cf", 1)
        junk, t_ = new("cf", n // w), new("cf", 16 * w)
        op = A.add if big else A.subtract
        act(junk, ap(run, w // 2 - 1, n // 2, w // 2), ACT.Sign, best, -1.0, cnt)
        ts(u, kk[w], cnt, op, float(w), A.mult)
        tt(t_, ind(src, u), ww_[w], op)
        red(r_, t_, A.max if big else A.min)
        return cnt, k, r_, t_, best

    def look_up(win, u, o, lo, hi):
        st = new("cb", 128)
        cp(st, ind(win, u), "VS")
        mms(ap("pk", o, o + hi - lo), [(st, sub(selb, lo, hi))])

    def step(run, big, ua, u, o, lo, hi):
        cnt, k, r_, _t, best = where(run, gg, big, ua)
        ts(k, r_, best, A.subtract, -32.0 if big else 32.0, A.mult)
        ts(u, cnc, k, A.mult, cnt, A.add if big else A.subtract)
        look_up(fw, u, o, lo, hi)
        return cnt, k

    def aims(land, sem, k):
        spread(land, sem)
        bs_ = [ap("yts", k, k + 1), new("cf", 1), new("cf", 1)]
        for i in range(3 if "lc" in P["pairs"] else 2):
            act(new("cf", 8), ap(land, 3, 11), ACT.Identity, 0.0, 2.0 ** i, bs_[i])
        return bs_

    step("k1", True, ul("a1"), ul("ca"), 0, 0, 1)
    cnt, kb = step("k2", False, ul("a2"), ul("cc"), 1, 0, 2)
    jb = new("cf", 1)
    aff(jb, cnt, -16.0, kb)
    y3, r3 = second(ap("pk", 0, 3))
    fl3, c3 = new("cf", 3), new("cf", 3)
    ts(fl3, y3, C16, A.add, C16, A.subtract)
    aff(c3, y3, float(NC), KC)
    for i, (o, lo_, hi_) in enumerate(((8, 2, 3), (9, 2, 4), (11, 2, 4))):
        u = ul("c2", 8 * i, 8 * i + 8)
        aff(u, kt, sub(fl3, i, i + 1), sub(c3, i, i + 1), "V")
        look_up(fw, u, o, lo_, hi_)
    ts(ul("tw", 0, 1), ap("pk", 8, 9), sub(r3, 0, 1), A.subtract)
    for i in range(2):
        ts(ul("tb", 2 * i, 2 * i + 2), ap("pk", 9 + 2 * i, 11 + 2 * i), sub(r3, 1 + i, 2 + i), A.subtract)
    tp = new("cf", 16)
    tt(tp, ind(ap("tw", 0, 2432), ul("tw", 0, 1)), eyeo, A.mult)
    red(ap("an1", 3, 4), tp, A.add)
    b2 = aims("an1", "ra1", 0)
    cp(ap("bl", 0, 64), ind(ap("tw", 0, 2432), ul("tb")), "VS")

    tw = ap("tw", 0, 2944)
    for i, lv in enumerate(("la", "lc")):
        if lv not in P["pairs"]:
            for k in range(4):
                o = 128 * i + 32 * k
                cp(ap(lv, 512 * k, 512 * k + 512), ind(tw, ul("x", o, o + 32)), "VS")
            continue
        for h in range(2):
            o = 128 * i + 32 * h
            a_, s_ = ap("sa", 1024 * i + 512 * h, 1024 * i + 512 * h + 512), ap(lv, 512 * h, 512 * h + 512)
            bk = ap((("ea", "eb"), ("ec", "ed"))[i][h], 0, 512)
            cp(a_, ind(tw, ul("x", o, o + 32)), "VS")
            tt(s_, ind(tw, ul("x", o + 64, o + 96)), a_, A.add)
            mms(bk, [(id2, a_)], True, False)
            mms(bk, [(nid, s_)], False, True)
            act(ap(lv, 1024 + 512 * h, 1536 + 512 * h), bk, ACT.Abs, 0.0, i + 1.0)

    def big_sum(out, lv, bs_, sc, k_=0, n=512, banks=None):
        bk = [ap(x, 0, n) for x in (banks or (("ea", "eb") if lv == "la" else ("ec", "ed")))]
        if banks is None and lv == "lc" and "cd"[k_] in P["sum"]:
            for h in range(2):
                x = ap("pq", 1024 * k_ + 512 * h, 1024 * k_ + 512 * h + 512)
                act(bk[h], ap(lv, n * h, n * h + n), ACT.Abs, bs_[sc], -float(sc))
                tt(x, ap(lv, n * (h + 2), n * (h + 3)), bk[h], A.max)
            for h in range(2):
                mms(bk[0], [(id1, ap("pq", 1024 * k_ + 512 * h, 1024 * k_ + 512 * h + 512))], h == 0, h == 1)
            cp(out, bk[0], "VS")
            return
        if ("la" if lv == "le" else lv) in P["pairs"]:
            for h, x in enumerate((out, bk[1])):
                act(bk[h], ap(lv, n * h, n * h + n), ACT.Abs, bs_[sc], -float(sc))
                tt(x, ap(lv, n * (h + 2), n * (h + 3)), bk[h], A.max)
            tt(out, out, bk[1], A.add)
            return
        pe = P["far"][2 + k_] if lv == "lc" else 0
        act(out, ap(lv, 0, n), ACT.Abs, bs_[sc - 1], -float(sc))
        if pe:
            for k in range(pe):
                x = ap("pq", 1536 * k_ + 512 * k, 1536 * k_ + 512 * k + 512)
                act(x, ap(lv, n * (3 - k), n * (4 - k)), ACT.Abs, bs_[sc - 1], -float(sc))
                mms(bk[0], [(id1, x)], k == 0, k == pe - 1)
            if pe == 2:
                act(bk[1], ap(lv, n, 2 * n), ACT.Abs, bs_[sc - 1], -float(sc))
                tt(out, out, bk[1], A.add)
            tt(out, out, bk[0], A.add)
            return
        for k in range(1, 4):
            act(bk[k % 2], ap(lv, n * k, n * k + n), ACT.Abs, bs_[sc - 1], -float(sc))
            tt(out, out, bk[k % 2], A.add)

    def best_sum(b_):
        t_, bv = new("cf", 64), new("cf", 16)
        act(t_, ap("bl", 0, 64), ACT.Abs, b_, -1.0)
        tt(sub(t_, 0, 32), sub(t_, 0, 32), sub(t_, 32, 64), A.add)
        tt(bv, sub(t_, 0, 16), sub(t_, 16, 32), A.add)
        return bv

    def worst_row(x, u):
        n = x["n"]
        node("V", lambda g, e: g.vector.transpose(T.xt[:, 0:n], x["ap"]), [x], [ap("xt", 0, n)], cost(n, 1))
        scan(ap("xs", 0, n), ap("pp", 0, n), ap("xt", 0, n), A.add, A.max, 0.0)
        w = n // 16
        a_, r_ = new("cf", w), new("cb", w)
        ts(a_, ap("xs", 15, n, 16), C1, A.add, C1, A.subtract)
        tt(r_, a_, ap("xs", 15, n, 16), A.subtract)
        for h in range(2):
            mms(ap("pm", h, w, 2),
                [(sub(ib[h], 16 - 16 * (par - h), 144 - 16 * (par - h)), sub(r_, par, w, 2)) for par in range(2)])
        aff(u, ap("pm", 0, w), 32.0, 15.0, su)

    def sires(col, u, k, base):
        r_, tb = new("cf", 16), new("cf", 16)
        aff(r_, eye, col, 0.0)
        mms(ap("py", 0, 16), [(bm, r_)] + [(down, ap("bl", 0, 16))] * (1 - k))
        aff(tb, ap("py", 0, 16), 1.0, -256.0 * k)
        flat, pick = (("yfl", b0), ("yb", b0b))[k]
        cp(ap(flat, 0, 512), ind(tb, u), "VS")
        w = (4, 16)[k]
        for o in range(0, 16, w):
            mms(ap("py", 32, 64), [(sub(pick, 15 - m, 143 - m), ap(flat, m, 512, 16)) for m in range(o, o + w)],
                o == 0, o + w == 16)
        aff(ap("yss", 32 * k, 32 * k + 32), ap("py", 32, 64), 1.0, base)

    w2 = ap("w2", 0, 4608)
    cp(ap("xa", 640, 1152), ind(w2, ul("xs", 0, 32)), "VS")
    if P["xape"]:
        cp(ap("xa", 0, 512), ind(w2, ul("xs", 32, 64)), "VS")
        mms(ap("eb", 0, 512), [(id1, ap("xa", 640, 1152))], True, False)
        mms(ap("eb", 0, 512), [(id1, ap("xa", 0, 512))], False, True)
        worst_row(ap("eb", 0, 512), ul("m3", 0, 32))
    else:
        tt(ap("xa", 0, 512), ind(w2, ul("xs", 32, 64)), ap("xa", 640, 1152), A.add)
        if npp > 512:
            cp(ap("xa", 512, 640), ind(ap("xa", 0, 512), mg3), "VS")
        worst_row(ap("xa", 0, npp), ul("m3", 0, npp // 16))
    if P["early"]:
        for k in range(4):
            cp(ap("le", 128 * k, 128 * k + 128), ind(ap("la", 512 * k, 512 * k + 512), mg3), "VS")
    m3 = ul("m3", 0, 32)
    sires(jb, m3, 0, 4351.0)

    def made(out, b_, o):
        bv = best_sum(b_[0])
        k_ = o // 512 - 1
        if "ab"[k_] in P["sum"] or "AB"[k_] in P["sum"]:
            t_ = ap("d3", o, o + 512)
            cp(t_, ind(bv, m3), "VS")
            pe = P["far"][k_] if "ab"[k_] in P["sum"] else 0
            far = ap(("pc", "pk")[k_], 0, 512)
            for k in range(pe):
                x = ap(("sa", "sb")[k_], 512 * k, 512 * k + 512)
                act(x, ap("la", 512 * k, 512 * k + 512), ACT.Abs, b_[0], -1.0)
                mms(far, [(id1, x)], k == 0, k == pe - 1)
            for k in range(pe, 4):
                bk = ap(("ea", "eb")[k % 2], 0, 512)
                act(bk, ap("la", 512 * k, 512 * k + 512), ACT.Abs, b_[0], -1.0)
                tt(out, t_ if k == pe else out, bk, A.add)
            if pe:
                tt(out, out if pe < 4 else t_, far, A.add)
            return t_
        big_sum(ap("d3", o, o + 512), "la", b_, 1)
        tt(out, ind(bv, m3), ap("d3", o, o + 512), A.add)
        return bv

    def next_aim(x):
        runs("k3", x, True, 0, 512)
        _c, _k, r_, t_, _b = where("k3", x, True, ul("a3"))
        ts(t_, t_, r_, A.is_equal, own, A.mult)
        y_ = new("cf", 64)
        tt(y_, ind(ap("yfl", 0, 512), ul("a3")), t_, A.mult)
        red(ap("an2", 3, 4), y_, A.add)
        return aims("an2", "ra2", 1)

    def third(w_, b_, k, bv):
        e3 = ap("e3", 128 * k, 128 * k + 128)
        if P["early"] > 1 - k:
            x = ap("le", 512 + 128 * k, 640 + 128 * k)
            t_ = ap("lt", 512 * k, 512 * k + 512)
            if "la" in P["pairs"]:
                act(sub(t_, 0, 256), ap("le", 0, 256), ACT.Abs, b_[1], -1.0)
                tt(sub(t_, 0, 256), sub(t_, 0, 256), ap("le", 256, 512), A.max)
            else:
                act(t_, ap("le", 0, 512), ACT.Abs, b_[0], -1.0)
                tt(sub(t_, 0, 256), sub(t_, 0, 256), sub(t_, 256, 512), A.add)
            tt(x, sub(t_, 0, 128), sub(t_, 128, 256), A.add)
            tt(e3, ind(bv, ul("m3", 32, 40) if bv["n"] == 16 else mg3), x, A.add)
        else:
            cp(e3, ind(ap(w_, 512, 1024), mg3), "VS")
        ring([(e3, ap(w_, 1024, 1152))], ("r3", "r4")[k])
        big_sum(ap(w_, 0, 512), "lc", b_, 2, k)

    xo = ap("d3", 1536, 2048)
    bo = ap("an1", 3, 4)
    if True:
        sd = "la" in P["pairs"]
        for k in range(4):
            for r in range(R):
                p0 = 32 * k + 16 * r
                nm, o = (("sa", "la")[k // 2], 512 * (k % 2)) if sd else ("la", 512 * k)
                dma("Y", T.cs[p0:p0 + 16, :], T[nm][R * rank + r::16, o:o + 512], [ap(nm, o, o + 512)], [ap("cs", 0, 256)],
                    0.2, "fw")
        cs = ap("cs", 0, 256)
        if sd:
            mms(ap("pc", 0, 256), [(id1, cs), (sub(nidp, 0, 128), cs)])
            cs = ap("pc", 0, 256)
        back, out_, bc, pc_ = ap("bk", 0, 256), new("cf", 128), new("cf", 1), new("cf", 256)
        b32 = ap("bk", 0, 256, 1, None, 32)
        iota(b32, [[0, 256]], 1, 0)
        keep(b32, b32, [[-1, 2], [-2, 8], [-16, 16]], A.is_equal, 16 * R * rank, 1)
        for k in range(1, 4):
            dma("Y", T.bk[32 * k:32 * k + 32, :], T.bk[0:32, :], [back], [back])
        iota(out_, [[0, 128]], 1, 0)
        for k in range(4):
            x = sub(out_, 32 * k, 32 * k + 32)
            keep(x, x, [[-1, 2], [-16, 8], [0, 2]], A.is_equal, -R * rank, 1)
        mms(ap("pk", 0, 16), [(out_, tp)])
        act(new("cf", 16), ap("pk", 0, 16), ACT.Identity, 0.0, 1.0, bc)
        act(pc_, cs, ACT.Abs, bc, -1.0)
        for c in range(2):
            mms(ap("pc", 256 * c, 256 * c + 256), [(sub(back, 128 * c, 128 * c + 128), pc_)])
        cp(ap("d3", 0, 512), ind(best_sum(bo), m3), "VS")
        tt(xo, ap("d3", 0, 512), ap("pc", 0, 512), A.add)
    b3 = next_aim(xo)
    x2, x3 = ap("wd2", 512, 1024), ap("wd3", 512, 1024)
    third("wd2", b2, 0, made(x2, b2, 512))
    runs("k4", x2, False, 0, 512)
    cnt, kc, r_, _t, best = where("k4", x2, False, ul("a4"))
    ts(kc, r_, best, A.subtract, 32.0, A.mult)
    jc = new("cf", 1)
    aff(ul("b2", 0, 1), cnt, -4.0, kc, su)
    aff(jc, cnt, -4.0, kc)
    cp(ap("xb", 0, 512), ind(ap("wd2", 0, 1152), ul("i4")), "VS")
    worst_row(ap("xb", 0, 512), ul("m4"))
    sires(jc, ul("m4"), 1, 6528.0 + 256.0)

    third("wd3", b3, 1, made(x3, b3, 1024))
    aff(ap("yfs", 0, 512), x3, -0.125, 65535.0)
    bt = new("cf", 16)
    aff(bt, ind(x3, ul("b2", 0, 1)), -0.0625, 0.0)
    for c in range(2):
        a_, b_ = 256 * c, 256 * c + 256
        aff(ap("f4t", a_, b_), ind(ap("wd3", 0, 1152), ul("i4", 16 * c, 16 * c + 16)), -0.0625, 65535.0)
        tt(ap("yfs", 512 + a_, 512 + b_), ind(bt, ul("m4", 16 * c, 16 * c + 16)), ap("f4t", a_, b_), A.add)
    dma("Y", T.yt[:], T.yts[:], [ap("yts", 0, 2)], [])
    dma("Y", T.ys[:], T.yss[:], [ap("yss", 0, 64)], [])
    dma("Y", T.yf[:, 0:512], T.yfs[:, 0:512], [ap("yfs", 0, 512)], [], 0.5)
    for c in (512, 768):
        dma("Y", T.yf[:, c:c + 256], T.yfs[:, c:c + 256], [ap("yfs", c, c + 256)], [], 0.25)
    assert alloc["dma"] <= NDMA
    return nodes


def lay_out(order, dur, eng, pre, bias):
    n = len(dur)
    st, on = [0.0] * n, [None] * n
    line = {e: [] for e in "VSPGY"}
    for k in order:
        t0 = 0.0
        for j, d in pre[k]:
            t = st[j] + dur[j] + d
            if t > t0:
                t0 = t
        if eng[k] == "X":
            st[k], on[k] = t0, "X"
            continue
        best = None
        for e in eng[k]:
            t, ln = t0, line[e]
            i = len(ln)
            while i > 0 and ln[i - 1][1] > t0:
                i -= 1
            while i < len(ln) and ln[i][0] < t + dur[k]:
                t = max(t, ln[i][1])
                i += 1
            c = t + (bias if e == "V" else 0.0)
            if best is None or c < best[0]:
                best = (c, t, e, i)
        _c, st[k], on[k], i = best
        line[on[k]].insert(i, (st[k], st[k] + dur[k]))
    return st, on


def schedule(nodes):
    n = len(nodes)
    if n in PLAN:
        return PLAN[n]
    dur = [x["dur"] for x in nodes] + [0.0]
    pre = [[(j, nodes[j]["lat"] + P["sync"]) for j in x["deps"]] for x in nodes]
    has = set(j for x in nodes for j in x["deps"])
    pre.append([(k, nodes[k]["lat"]) for k in range(n) if k not in has])
    post = [[] for _ in range(n + 1)]
    up = [set() for _ in range(n + 1)]
    for k in range(n + 1):
        for j, d in pre[k]:
            post[j].append((k, d))
            up[k] |= up[j] | {j}
    eng = [x["eng"] for x in nodes] + ["X"]
    rng = np.random.default_rng(P["seed"])

    def rank_by(key, pre, post):
        left = [len(x) for x in pre]
        key = list(key)
        todo = [k for k in range(n + 1) if not left[k]]
        for k in todo:
            for j, _d in post[k]:
                key[j] = max(key[j], key[k] + 1e-6)
                left[j] -= 1
                if not left[j]:
                    todo.append(j)
        return sorted(range(n + 1), key=lambda k: key[k])

    def both(key, bias, eng):
        st, on = lay_out(rank_by(key, pre, post), dur, eng, pre, bias)
        sb, _o = lay_out(rank_by([-st[k] - dur[k] for k in range(n + 1)], post, pre), dur, on, post, 0.0)
        s2, o2 = lay_out(rank_by([-sb[k] - dur[k] for k in range(n + 1)], pre, post), dur, eng, pre, bias)
        if st[n] < s2[n]:
            s2, o2 = st, on
        order = sorted(range(n + 1), key=lambda k: s2[k])
        total = s2[n]
        for du, more in others:
            end, free = [0.0] * (n + 1), {}
            for k in order:
                t = free.get(o2[k], 0.0) if o2[k] != "X" else 0.0
                for j, d in pre[k]:
                    if end[j] + d * more > t:
                        t = end[j] + d * more
                end[k] = free[o2[k]] = t + du[k]
            total += P["wo"] * end[n]
        return s2, o2, total

    others = [([d * (P["slow"] if eng[k] == "P" else 1.0) for k, d in enumerate(dur)], 1.0), (dur, P["late"])]

    pr = [0.0] * (n + 1)
    for k in range(n, -1, -1):
        pr[k] = dur[k] + max([pr[j] + d for j, d in post[k]] + [0.0])
    cur = best = both([-x for x in pr], P["bias"], eng)
    big = [k for k in range(n) if eng[k] == "VS"]
    for it in range(P["iters"]):
        key = list(cur[0])
        e2 = list(cur[1])
        if rng.random() < 0.5:
            k = int(rng.integers(n))
            d, w = abs(float(rng.normal(0, 3.0))), 10.0 * rng.random()
            for j in list(up[k]) + [k]:
                if key[j] > cur[0][k] - w:
                    key[j] -= d
            if rng.random() < 0.3:
                for j in big:
                    if cur[0][k] - w < cur[0][j] < cur[0][k] + 2:
                        e2[j] = "VS"
        else:
            for _i in range(int(rng.integers(1, 5))):
                key[int(rng.integers(n))] += float(rng.normal(0, P["sd"]))
        for _i in range(int(rng.integers(0, 6))):
            e2[big[int(rng.integers(len(big)))]] = "VS"
        if rng.random() < 0.3:
            k = big[int(rng.integers(len(big)))]
            e2[k] = "S" if cur[1][k] == "V" else "V"
        c = both(key, P["bias"] * 2 * rng.random(), e2)
        if c[2] <= cur[2] - P["T"] * (1 - it / P["iters"]) * np.log(rng.random()):
            cur = c
            if c[2] < best[2]:
                best = c
    PLAN[n] = (sorted(range(n), key=lambda k: (best[0][k], k)), best[0], best[1])
    return PLAN[n]


def rank_program(g, core, T, topo):
    rank = T.rank_of(core)
    if rank is None:
        return
    nodes = build(T, topo, core, rank)
    order, _st, eng = schedule(nodes)
    for k, x in enumerate(nodes):
        x["on"] = eng[k]
    q = {"V": g.vector, "S": g.scalar, "P": g.tensor, "G": g, "Y": g.sync}
    need = set()
    for k, x in enumerate(nodes):
        if x["on"] == "X":
            continue
        for j, how in x["deps"].items():
            y = nodes[j]
            if y["kind"] == "c" and (y["on"] != x["on"] or x["kind"] != "c" or (how != "ord" and y["on"] != "P")):
                need.add(j)
    cnt = {"V": 0, "S": 0, "P": 0, "G": 0}
    seen = {}
    sent = 0
    for k in order:
        x = nodes[k]
        e = x["on"]
        if e == "X":
            continue
        want = {}
        for j, how in x["deps"].items():
            y = nodes[j]
            if y["kind"] == "c":
                if y["on"] == e and x["kind"] == "c" and (how == "ord" or e == "P"):
                    continue
                s, v = "c" + y["on"], y["sig"]
            else:
                s, v = y["sem"], y["val"]
            want[s] = max(want.get(s, 0), v)
        for s, v in want.items():
            if seen.get((e, s), 0) < v:
                q[e].wait_ge(T.sem[s], v)
                seen[(e, s)] = v
        ins = x["fn"](g, e)
        if x["kind"] == "c":
            if k in need:
                cnt[e] += 1
                x["sig"] = cnt[e]
                ins.then_inc(T.sem["c" + e], 1)
        elif x["kind"] == "s":
            sent += x["val"]
        else:
            ins.then_inc(T.sem[x["sem"]], 16)
    g.wait_ge(T.sem["sent"], sent)
    for x in nodes:
        if x["kind"] in ("d", "fw") and not any(seen.get((e, x["sem"]), 0) for e in q):
            g.sync.wait_ge(T.sem[x["sem"]], 16)
